import numpy as np
import ml_dtypes


def mxq(x, axis, fmt="e4m3"):
    dtype, down = {"e4m3": (ml_dtypes.float8_e4m3fn, 7), "e5m2": (ml_dtypes.float8_e5m2, 14)}[fmt]
    v = np.moveaxis(np.asarray(x, np.float32).astype(ml_dtypes.bfloat16).astype(np.float64), axis, -1)
    blocks = v.reshape(v.shape[:-1] + (-1, 32))
    amax = np.abs(blocks).max(-1, keepdims=True)
    byte = np.maximum(np.where(amax > 0, np.frexp(amax)[1] - 1 + 127, 0) - down, 1)
    scale = np.exp2(byte - 127.0)
    codes = (blocks / scale).astype(np.float32).astype(dtype).astype(np.float64)
    return np.moveaxis((codes * scale).reshape(v.shape), -1, axis)


WIDE = False


def mx_kscale(k):
    if not WIDE:
        return np.ones(k)
    levels = np.array([10, -10, 5, -5, 0])
    if k % 512:
        return np.exp2(np.random.permutation(np.resize(levels, k // 32))).repeat(32)
    a = np.empty((k // 512, 16))
    for p in range(k // 512):
        a[p, :8] = np.random.permutation(np.resize(levels, 8))
        for g in range(8):
            far = levels[np.abs(levels - a[p, g]) >= 10]
            a[p, g + 8] = far[np.random.randint(len(far))]
    return np.exp2(a.ravel()).repeat(32)


def f64(x):
    return np.asarray(x).astype(np.float64)


def striped(idx):
    return np.tile(idx.reshape(-1, 16).T, (8, 1)).astype(np.uint16)


def unstriped(offs):
    return offs[:16].T.reshape(-1).astype(np.int64)


E2M1 = np.array([0.0, 0.5, 1.0, 1.5, 2.0, 3.0, 4.0, 6.0, -0.0, -0.5, -1.0, -1.5, -2.0, -3.0, -4.0, -6.0])


def pack_weight(w, fmt):
    k, n = w.shape
    w = f64(np.asarray(w, np.float32).astype(ml_dtypes.bfloat16)).reshape(k // 32, 32, n)
    amax = np.abs(w).max(1)
    if fmt == "e4m3":
        byte = np.frexp(amax)[1] - 1 + 127 - 7
    else:
        mant, ex = np.frexp(amax / 6.0)
        byte = np.where(mant > 0.5, ex, ex - 1) + 127
    byte = np.clip(np.where(amax > 0, byte, 1), 1, 254)
    scaled = (w * np.exp2(127.0 - byte)[:, None, :]).reshape(k, n).astype(np.float32)
    by_word = np.ascontiguousarray(scaled.reshape(k // 512, 128, 4, n).transpose(0, 1, 3, 2))
    if fmt == "e4m3":
        words = by_word.astype(ml_dtypes.float8_e4m3fn).view(np.uint8)
    else:
        c = by_word.astype(ml_dtypes.float4_e2m1fn).view(np.uint8) & 0xF
        words = (c[..., 0::2] | (c[..., 1::2] << 4)).reshape(k // 512, 128, 2 * n)
    return np.ascontiguousarray(words), np.ascontiguousarray(byte.astype(np.uint8).reshape(k // 512, 16, n))


def unpack_weight(words, scales, fmt):
    g, _, n = scales.shape
    words = np.ascontiguousarray(words).reshape(g, 128, n, -1)
    if fmt == "e4m3":
        vals = words.view(ml_dtypes.float8_e4m3fn).astype(np.float64)
    else:
        nib = np.empty((g, 128, n, 4), np.uint8)
        nib[..., 0::2] = words & 0xF
        nib[..., 1::2] = words >> 4
        vals = E2M1[nib]
    vals = vals * np.repeat(np.exp2(scales.astype(np.float64) - 127.0), 8, axis=1)[..., None]
    return vals.transpose(0, 1, 3, 2).reshape(g * 512, n)


def gelu(v):
    return 0.5 * v * (1.0 + np.tanh(np.sqrt(2.0 / np.pi) * (v + 0.044715 * v**3)))


K, C, H, N, T, T2, S = 1024, 512, 1024, 512, 2048, 2048, 1024

def setup_inputs():
    n = np.random.standard_normal
    s = mx_kscale(K)[:, None]
    s2 = mx_kscale(C)[:, None]
    u = mx_kscale(H)[:, None]
    tab_words, tab_scales = pack_weight(n((K, T)) * s, "e4m3")
    tab2_words, tab2_scales = pack_weight(n((C, T2)) * s2, "e4m3")
    wb_words, wb_scales = pack_weight(n((C, H)) / s2 / np.sqrt(C), "e2m1")
    wa = (n((K, H)) / s * u.T / np.sqrt(K)).astype(np.float32)
    wt = (1.6 * n((H, N)) / u / np.sqrt(H)).astype(np.float32)
    bc = (0.4 * n(H)).astype(np.float32)
    gT = n((N, T)).astype(np.float32)
    offs = striped(np.random.permutation(T)[:S])
    offs2 = striped(np.random.permutation(T2)[:S])
    return dict(tab_words=tab_words, tab_scales=tab_scales, offs=offs,
                tab2_words=tab2_words, tab2_scales=tab2_scales, offs2=offs2,
                wa=wa, wb_words=wb_words, wb_scales=wb_scales, bc=bc, wt=wt, gT=gT)

def reference(tab_words, tab_scales, offs, tab2_words, tab2_scales, offs2,
              wa, wb_words, wb_scales, bc, wt, gT):
    v = unpack_weight(tab_words, tab_scales, "e4m3")[:, unstriped(offs)]
    v2 = unpack_weight(tab2_words, tab2_scales, "e4m3")[:, unstriped(offs2)]
    wb = unpack_weight(wb_words, wb_scales, "e2m1")
    a = mxq(f64(wa), 0, "e4m3").T @ v
    b = np.tanh((wb.T @ v2) + f64(bc)[:, None])
    h = a * b
    y = mxq(f64(wt), 0, "e4m3").T @ mxq(h, 0, "e4m3")
    g = f64(gT)[:, unstriped(offs)]
    return np.abs(y - g)

@@ -1,0 +1,249 @@
+from contextlib import ExitStack
+
+import concourse.mybir as mybir
+
+K, C, H, N, T, S = 1024, 512, 1024, 512, 2048, 1024
+FLOPS = 2 * S * (K * H + C * H + H * N)
+
+F32 = mybir.dt.float32
+BF16 = mybir.dt.bfloat16
+I32 = mybir.dt.int32
+U32 = mybir.dt.uint32
+U16 = mybir.dt.uint16
+U8 = mybir.dt.uint8
+FP8X4 = mybir.dt.float8_e4m3fn_x4
+FP4X4 = mybir.dt.float4_e2m1fn_x4
+ACT = mybir.ActivationFunctionType
+ALU = mybir.AluOpType
+
+P = 128
+PACK = 4
+KP = P * PACK
+HALF = 512
+TOK = 128
+
+
+def tile_list_locus_cell_tracks_kernel(
+    tc, tab_words, tab_scales, offs, tab2_words, tab2_scales, offs2, wa, wb_words, wb_scales, bc, wt, gT, out
+):
+    nc = tc.nc
+    with ExitStack() as ctx:
+        keep = ctx.enter_context(tc.tile_pool(name="keep", bufs=1))
+        ring = ctx.enter_context(tc.tile_pool(name="ring", bufs=3))
+        pa_pool = ctx.enter_context(tc.psum_pool(name="pa", bufs=4))
+        pb_pool = ctx.enter_context(tc.psum_pool(name="pb", bufs=2))
+        py_pool = ctx.enter_context(tc.psum_pool(name="py", bufs=2))
+
+        def held(shape, dtype, name):
+            return keep.tile(shape, dtype, name=name, align_bytes=64)
+
+        idx = keep.tile([P, S // 16], U16, name="idx")
+        idx2 = keep.tile([P, S // 16], U16, name="idx2")
+        ts_all = held([P, T], U8, "ts_all")
+        t2s_all = held([P, T], U8, "t2s_all")
+        wbs_raw = held([P, H], U8, "wbs_raw")
+        wbw_raw = held([P, 2 * H], U8, "wbw_raw")
+        bias = held([P, H // KP, PACK], F32, "bias")
+        tw_all = [held([P, T], U32, "tw_all%d" % a) for a in range(2)]
+        t2w_all = held([P, T], U32, "t2w_all")
+        wa_raw = [[held([P, PACK, KP], F32, "wa_raw%d%d" % (b, a)) for a in range(2)] for b in range(2)]
+        wt_raw = [held([P, PACK, N], F32, "wt_raw%d" % b) for b in range(2)]
+        g_all = [held([P, T], F32, "g_all%d" % nb) for nb in range(4)]
+
+        nc.vector.memset(ts_all[:].bitcast(I32), 0)
+        nc.vector.memset(t2s_all[:].bitcast(I32), 0)
+        nc.vector.memset(wbs_raw[:].bitcast(I32), 0)
+
+        def load_words(dst, src):
+            nc.sync.dma_start(out=dst[:].bitcast(I32), in_=src.rearrange("p t i -> p (t i)").bitcast(I32))
+
+        def load_scales(queue, dst, src):
+            passes = src.shape[0]
+            for q in range(4):
+                queue.dma_start(
+                    out=dst[32 * q : 32 * q + 4 * passes, :].bitcast(I32),
+                    in_=src[:, 4 * q : 4 * q + 4, :].bitcast(I32),
+                )
+
+        def load_wa(b, a):
+            nc.sync.dma_start(
+                out=wa_raw[b][a][:],
+                in_=wa[a * KP : (a + 1) * KP, b * KP : (b + 1) * KP].rearrange("(p j) c -> p j c", j=PACK),
+            )
+
+        nc.sync.dma_start(idx[:], offs)
+        nc.sync.dma_start(idx2[:], offs2)
+        load_scales(nc.scalar, ts_all, tab_scales)
+        load_scales(nc.gpsimd, t2s_all, tab2_scales)
+        load_wa(0, 0)
+        load_wa(0, 1)
+        nc.sync.dma_start(out=wbw_raw[:].bitcast(I32), in_=wb_words[0].bitcast(I32))
+        nc.sync.dma_start(out=bias[:], in_=bc.rearrange("(b p t) -> p b t", p=P, t=PACK))
+        load_wa(1, 0)
+        load_scales(nc.sync, wbs_raw, wb_scales)
+        load_words(t2w_all, tab2_words[0])
+        load_words(tw_all[0], tab_words[0])
+        load_words(tw_all[1], tab_words[1])
+        load_wa(1, 1)
+        for b in range(2):
+            nc.sync.dma_start(out=wt_raw[b][:], in_=wt[b * KP : (b + 1) * KP, :].rearrange("(p j) n -> p j n", j=PACK))
+        for nb in range(4):
+            nc.sync.dma_start(out=g_all[nb][:], in_=gT[nb * P : (nb + 1) * P, :])
+
+        def half_list(lst, hf):
+            return lst[:, hf * HALF // 16 : (hf + 1) * HALF // 16]
+
+        ts = held([P, S], U8, "ts")
+        t2s = held([P, S], U8, "t2s")
+        tw = [[held([P, HALF], U32, "tw%d%d" % (hf, a)) for a in range(2)] for hf in range(2)]
+        t2w = [held([P, HALF], U32, "t2w%d" % hf) for hf in range(2)]
+        wbw = held([P, 2 * H], U8, "wbw")
+        wbs = held([P, H], U8, "wbs")
+        wa_q = [[held([P, KP], U32, "wa_q%d%d" % (b, a)) for a in range(2)] for b in range(2)]
+        wa_s = [[held([P, KP], U8, "wa_s%d%d" % (b, a)) for a in range(2)] for b in range(2)]
+        wt_q = [held([P, N], U32, "wt_q%d" % b) for b in range(2)]
+        wt_s = [held([P, N], U8, "wt_s%d" % b) for b in range(2)]
+        h_q = [[held([P, HALF], U32, "h_q%d%d" % (hf, b)) for b in range(2)] for hf in range(2)]
+        h_s = [[held([P, HALF], U8, "h_s%d%d" % (hf, b)) for b in range(2)] for hf in range(2)]
+        mod = [[held([P, PACK, HALF], F32, "mod%d%d" % (hf, b)) for b in range(2)] for hf in range(2)]
+        staged = {}
+
+        def cast_wa(b, a):
+            w16 = ring.tile([P, PACK, P, PACK], BF16, name="w16", align_bytes=64)
+            nc.scalar.activation(
+                out=w16[:].rearrange("p t m j -> p m j t"),
+                in_=wa_raw[b][a][:].rearrange("p j (m t) -> p m j t", t=PACK),
+                func=ACT.Copy,
+            )
+            staged["wa", b, a] = w16[:].rearrange("p t m j -> p (t m j)")
+
+        def cast_wt(b):
+            w16 = ring.tile([P, N, PACK], BF16, name="w16", align_bytes=64)
+            nc.scalar.activation(
+                out=w16[:].rearrange("p (c i) j -> p c j i", i=4),
+                in_=wt_raw[b][:].rearrange("p j (c i) -> p c j i", i=4),
+                func=ACT.Copy,
+            )
+            staged["wt", b] = w16[:].rearrange("p n j -> p (n j)")
+
+        def quantize(codes, scales, src):
+            nc.vector.quantize_mx(out=codes[:].bitcast(FP8X4), scales=scales[:], in_=src)
+
+        def gather(dst, table, lst):
+            nc.vector.tensor_copy(dst[:], table[:].indirect(lst))
+
+        def permute_wb():
+            nc.vector.tensor_copy(
+                out=wbw[:].bitcast(U16).rearrange("p (b t m) -> p b t m", b=2, t=PACK),
+                in_=wbw_raw[:].bitcast(U16).rearrange("p (b m t) -> p b t m", b=2, t=PACK),
+            )
+            nc.vector.tensor_copy(
+                out=wbs[:].rearrange("p (b t m) -> p b t m", b=2, t=PACK),
+                in_=wbs_raw[:].rearrange("p (b m t) -> p b t m", b=2, t=PACK),
+            )
+
+        def modulation(hf, b):
+            for t in range(PACK):
+                c0 = b * KP + t * P
+                pb = pb_pool.tile([P, HALF], F32, name="pb")
+                nc.tensor.matmul_mx(
+                    out=pb[:],
+                    lhsT=wbw[:, 2 * c0 : 2 * (c0 + P)].bitcast(FP4X4),
+                    lhsT_scale=wbs[:, c0 : c0 + P],
+                    rhs=t2w[hf][:].bitcast(FP8X4),
+                    rhs_scale=t2s[:, hf * HALF : (hf + 1) * HALF],
+                    start=True,
+                    stop=True,
+                )
+                nc.scalar.activation(out=mod[hf][b][:, t, :], in_=pb[:], func=ACT.Tanh, bias=bias[:, b, t : t + 1])
+
+        def hidden(hf, b):
+            h16 = ring.tile([P, HALF, PACK], BF16, name="h16", align_bytes=64)
+            for u in range(HALF // TOK):
+                cols = slice(u * TOK, (u + 1) * TOK)
+                pa = pa_pool.tile([P, PACK, TOK], F32, name="pa")
+                for t in range(PACK):
+                    for a in range(2):
+                        nc.tensor.matmul_mx(
+                            out=pa[:, t, :],
+                            lhsT=wa_q[b][a][:, t * P : (t + 1) * P].bitcast(FP8X4),
+                            lhsT_scale=wa_s[b][a][:, t * P : (t + 1) * P],
+                            rhs=tw[hf][a][:, cols].bitcast(FP8X4),
+                            rhs_scale=ts[4 * a : P, hf * HALF + u * TOK : hf * HALF + (u + 1) * TOK],
+                            start=(a == 0),
+                            stop=(a == 1),
+                        )
+                nc.vector.tensor_tensor(
+                    out=h16[:, cols, :].rearrange("p (c i) t -> p c t i", i=4),
+                    in0=pa[:].rearrange("p t (c i) -> p c t i", i=4),
+                    in1=mod[hf][b][:, :, cols].rearrange("p t (c i) -> p c t i", i=4),
+                    op=ALU.mult,
+                )
+            staged["h", hf, b] = h16[:].rearrange("p n t -> p (n t)")
+
+        def predict(hf, nb):
+            py = py_pool.tile([P, HALF], F32, name="py")
+            for b in range(2):
+                nc.tensor.matmul_mx(
+                    out=py[:],
+                    lhsT=wt_q[b][:, nb * P : (nb + 1) * P].bitcast(FP8X4),
+                    lhsT_scale=wt_s[b][:, nb * P : (nb + 1) * P],
+                    rhs=h_q[hf][b][:].bitcast(FP8X4),
+                    rhs_scale=h_s[hf][b][:],
+                    start=(b == 0),
+                    stop=(b == 1),
+                )
+            y = ring.tile([P, HALF], F32, name="y", bufs=4)
+            nc.scalar.copy(out=y[:], in_=py[:])
+            staged["y", hf, nb] = y
+
+        def finish(hf, nb):
+            d = ring.tile([P, HALF], F32, name="d", bufs=4)
+            nc.vector.tensor_tensor(
+                out=d[:], in0=g_all[nb][:].indirect(half_list(idx, hf)), in1=staged["y", hf, nb][:], op=ALU.subtract
+            )
+            nc.scalar.activation(out=d[:], in_=d[:], func=ACT.Abs)
+            nc.sync.dma_start(out=out[nb * P : (nb + 1) * P, hf * HALF : (hf + 1) * HALF], in_=d[:])
+
+        gather(ts, ts_all, idx[:])
+        cast_wa(0, 0)
+        gather(t2s, t2s_all, idx2[:])
+        quantize(wa_q[0][0], wa_s[0][0], staged["wa", 0, 0])
+        cast_wa(0, 1)
+        permute_wb()
+        quantize(wa_q[0][1], wa_s[0][1], staged["wa", 0, 1])
+        cast_wa(1, 0)
+        gather(t2w[0], t2w_all, half_list(idx2, 0))
+        modulation(0, 0)
+        gather(t2w[1], t2w_all, half_list(idx2, 1))
+        gather(tw[0][0], tw_all[0], half_list(idx, 0))
+        quantize(wa_q[1][0], wa_s[1][0], staged["wa", 1, 0])
+        modulation(0, 1)
+        gather(tw[1][0], tw_all[0], half_list(idx, 1))
+        gather(tw[0][1], tw_all[1], half_list(idx, 0))
+        hidden(0, 0)
+        cast_wa(1, 1)
+        gather(tw[1][1], tw_all[1], half_list(idx, 1))
+        quantize(h_q[0][0], h_s[0][0], staged["h", 0, 0])
+        quantize(wa_q[1][1], wa_s[1][1], staged["wa", 1, 1])
+        cast_wt(0)
+        hidden(0, 1)
+        modulation(1, 0)
+        quantize(wt_q[0], wt_s[0], staged["wt", 0])
+        quantize(h_q[0][1], h_s[0][1], staged["h", 0, 1])
+        cast_wt(1)
+        hidden(1, 0)
+        modulation(1, 1)
+        quantize(wt_q[1], wt_s[1], staged["wt", 1])
+        quantize(h_q[1][0], h_s[1][0], staged["h", 1, 0])
+        for nb in range(4):
+            predict(0, nb)
+        hidden(1, 1)
+        finish(0, 0)
+        quantize(h_q[1][1], h_s[1][1], staged["h", 1, 1])
+        for nb in range(1, 4):
+            finish(0, nb)
+        for nb in range(4):
+            predict(1, nb)
+        for nb in range(4):
+            finish(1, nb)

@@ -21,6 +21,9 @@ PACK = 4
 KP = P * PACK
 HALF = 512
 TOK = 128
+FUSED = (0, 1, 2, 3)
+DBUFS = 4
+MODTAG = [["mod", "wa_raw11"], ["wa_raw01", "wt_raw0"]]
 
 
 def tile_list_locus_cell_tracks_kernel(
@@ -31,8 +34,7 @@ def tile_list_locus_cell_tracks_kernel(
         keep = ctx.enter_context(tc.tile_pool(name="keep", bufs=1))
         ring = ctx.enter_context(tc.tile_pool(name="ring", bufs=3))
         pa_pool = ctx.enter_context(tc.psum_pool(name="pa", bufs=4))
-        pb_pool = ctx.enter_context(tc.psum_pool(name="pb", bufs=2))
-        py_pool = ctx.enter_context(tc.psum_pool(name="py", bufs=2))
+        wide_pool = ctx.enter_context(tc.psum_pool(name="wide", bufs=4))
 
         def held(shape, dtype, name):
             return keep.tile(shape, dtype, name=name, align_bytes=64)
@@ -50,9 +52,9 @@ def tile_list_locus_cell_tracks_kernel(
         wt_raw = [held([P, PACK, N], F32, "wt_raw%d" % b) for b in range(2)]
         g_all = [held([P, T], F32, "g_all%d" % nb) for nb in range(4)]
 
-        nc.vector.memset(ts_all[:].bitcast(I32), 0)
         nc.vector.memset(t2s_all[:].bitcast(I32), 0)
         nc.vector.memset(wbs_raw[:].bitcast(I32), 0)
+        nc.vector.memset(ts_all[:].bitcast(I32), 0)
 
         def load_words(dst, src):
             nc.sync.dma_start(out=dst[:].bitcast(I32), in_=src.rearrange("p t i -> p (t i)").bitcast(I32))
@@ -71,24 +73,32 @@ def tile_list_locus_cell_tracks_kernel(
                 in_=wa[a * KP : (a + 1) * KP, b * KP : (b + 1) * KP].rearrange("(p j) c -> p j c", j=PACK),
             )
 
-        nc.sync.dma_start(idx[:], offs)
-        nc.sync.dma_start(idx2[:], offs2)
-        load_scales(nc.scalar, ts_all, tab_scales)
-        load_scales(nc.gpsimd, t2s_all, tab2_scales)
-        load_wa(0, 0)
-        load_wa(0, 1)
-        nc.sync.dma_start(out=wbw_raw[:].bitcast(I32), in_=wb_words[0].bitcast(I32))
-        nc.sync.dma_start(out=bias[:], in_=bc.rearrange("(b p t) -> p b t", p=P, t=PACK))
-        load_wa(1, 0)
-        load_scales(nc.sync, wbs_raw, wb_scales)
-        load_words(t2w_all, tab2_words[0])
-        load_words(tw_all[0], tab_words[0])
-        load_words(tw_all[1], tab_words[1])
-        load_wa(1, 1)
-        for b in range(2):
+        def load_wt(b):
             nc.sync.dma_start(out=wt_raw[b][:], in_=wt[b * KP : (b + 1) * KP, :].rearrange("(p j) n -> p j n", j=PACK))
-        for nb in range(4):
+
+        def load_g(nb):
             nc.sync.dma_start(out=g_all[nb][:], in_=gT[nb * P : (nb + 1) * P, :])
+
+        nc.sync.dma_start(idx2[:], offs2)
+        nc.sync.dma_start(out=wbw_raw[:].bitcast(I32), in_=wb_words[0].bitcast(I32))
+        load_scales(nc.sync, t2s_all, tab2_scales)
+        load_words(t2w_all, tab2_words[0])
+        load_scales(nc.sync, wbs_raw, wb_scales)
+        load_wa(0, 0)
+        nc.sync.dma_start(idx[:], offs)
+        nc.sync.dma_start(out=bias[:], in_=bc.rearrange("(b p t) -> p b t", p=P, t=PACK))
+        load_words(tw_all[0], tab_words[0])
+        load_scales(nc.sync, ts_all, tab_scales)
+        load_wa(0, 1)
+        load_words(tw_all[1], tab_words[1])
+        load_wa(1, 0)
+        load_wa(1, 1)
+        load_wt(0)
+        load_wt(1)
+        load_g(0)
+        load_g(1)
+        load_g(2)
+        load_g(3)
 
         def half_list(lst, hf):
             return lst[:, hf * HALF // 16 : (hf + 1) * HALF // 16]
@@ -99,32 +109,30 @@ def tile_list_locus_cell_tracks_kernel(
         t2w = [held([P, HALF], U32, "t2w%d" % hf) for hf in range(2)]
         wbw = held([P, 2 * H], U8, "wbw")
         wbs = held([P, H], U8, "wbs")
-        wa_q = [[held([P, KP], U32, "wa_q%d%d" % (b, a)) for a in range(2)] for b in range(2)]
-        wa_s = [[held([P, KP], U8, "wa_s%d%d" % (b, a)) for a in range(2)] for b in range(2)]
-        wt_q = [held([P, N], U32, "wt_q%d" % b) for b in range(2)]
-        wt_s = [held([P, N], U8, "wt_s%d" % b) for b in range(2)]
+        wa_q = [held([P, 2 * KP], U32, "wa_q%d" % b) for b in range(2)]
+        wa_s = [held([P, 2 * KP], U8, "wa_s%d" % b) for b in range(2)]
+        wt_q = held([P, 2 * N], U32, "wt_q")
+        wt_s = held([P, 2 * N], U8, "wt_s")
+        wa16 = [held([P, 2 * KP * PACK], BF16, "wa16%d" % b) for b in range(2)]
+        wt16 = held([P, 2 * N * PACK], BF16, "wt16")
         h_q = [[held([P, HALF], U32, "h_q%d%d" % (hf, b)) for b in range(2)] for hf in range(2)]
         h_s = [[held([P, HALF], U8, "h_s%d%d" % (hf, b)) for b in range(2)] for hf in range(2)]
-        mod = [[held([P, PACK, HALF], F32, "mod%d%d" % (hf, b)) for b in range(2)] for hf in range(2)]
+        mod = [[None, None], [None, None]]
         staged = {}
 
         def cast_wa(b, a):
-            w16 = ring.tile([P, PACK, P, PACK], BF16, name="w16", align_bytes=64)
             nc.scalar.activation(
-                out=w16[:].rearrange("p t m j -> p m j t"),
+                out=wa16[b][:, a * KP * PACK : (a + 1) * KP * PACK].rearrange("p (t m j) -> p m j t", t=PACK, j=PACK),
                 in_=wa_raw[b][a][:].rearrange("p j (m t) -> p m j t", t=PACK),
                 func=ACT.Copy,
             )
-            staged["wa", b, a] = w16[:].rearrange("p t m j -> p (t m j)")
 
         def cast_wt(b):
-            w16 = ring.tile([P, N, PACK], BF16, name="w16", align_bytes=64)
             nc.scalar.activation(
-                out=w16[:].rearrange("p (c i) j -> p c j i", i=4),
+                out=wt16[:, b * N * PACK : (b + 1) * N * PACK].rearrange("p (c i j) -> p c j i", i=4, j=PACK),
                 in_=wt_raw[b][:].rearrange("p j (c i) -> p c j i", i=4),
                 func=ACT.Copy,
             )
-            staged["wt", b] = w16[:].rearrange("p n j -> p (n j)")
 
         def quantize(codes, scales, src):
             nc.vector.quantize_mx(out=codes[:].bitcast(FP8X4), scales=scales[:], in_=src)
@@ -132,20 +140,23 @@ def tile_list_locus_cell_tracks_kernel(
         def gather(dst, table, lst):
             nc.vector.tensor_copy(dst[:], table[:].indirect(lst))
 
-        def permute_wb():
+        def permute_wbw():
             nc.vector.tensor_copy(
                 out=wbw[:].bitcast(U16).rearrange("p (b t m) -> p b t m", b=2, t=PACK),
                 in_=wbw_raw[:].bitcast(U16).rearrange("p (b m t) -> p b t m", b=2, t=PACK),
             )
+
+        def permute_wbs():
             nc.vector.tensor_copy(
                 out=wbs[:].rearrange("p (b t m) -> p b t m", b=2, t=PACK),
                 in_=wbs_raw[:].rearrange("p (b m t) -> p b t m", b=2, t=PACK),
             )
 
         def modulation(hf, b):
+            mod[hf][b] = held([P, PACK, HALF], F32, MODTAG[hf][b])
             for t in range(PACK):
                 c0 = b * KP + t * P
-                pb = pb_pool.tile([P, HALF], F32, name="pb")
+                pb = wide_pool.tile([P, HALF], F32, name="wide")
                 nc.tensor.matmul_mx(
                     out=pb[:],
                     lhsT=wbw[:, 2 * c0 : 2 * (c0 + P)].bitcast(FP4X4),
@@ -166,8 +177,8 @@ def tile_list_locus_cell_tracks_kernel(
                     for a in range(2):
                         nc.tensor.matmul_mx(
                             out=pa[:, t, :],
-                            lhsT=wa_q[b][a][:, t * P : (t + 1) * P].bitcast(FP8X4),
-                            lhsT_scale=wa_s[b][a][:, t * P : (t + 1) * P],
+                            lhsT=wa_q[b][:, a * KP + t * P : a * KP + (t + 1) * P].bitcast(FP8X4),
+                            lhsT_scale=wa_s[b][:, a * KP + t * P : a * KP + (t + 1) * P],
                             rhs=tw[hf][a][:, cols].bitcast(FP8X4),
                             rhs_scale=ts[4 * a : P, hf * HALF + u * TOK : hf * HALF + (u + 1) * TOK],
                             start=(a == 0),
@@ -182,68 +193,90 @@ def tile_list_locus_cell_tracks_kernel(
             staged["h", hf, b] = h16[:].rearrange("p n t -> p (n t)")
 
         def predict(hf, nb):
-            py = py_pool.tile([P, HALF], F32, name="py")
+            py = wide_pool.tile([P, HALF], F32, name="wide")
             for b in range(2):
                 nc.tensor.matmul_mx(
                     out=py[:],
-                    lhsT=wt_q[b][:, nb * P : (nb + 1) * P].bitcast(FP8X4),
-                    lhsT_scale=wt_s[b][:, nb * P : (nb + 1) * P],
+                    lhsT=wt_q[:, b * N + nb * P : b * N + (nb + 1) * P].bitcast(FP8X4),
+                    lhsT_scale=wt_s[:, b * N + nb * P : b * N + (nb + 1) * P],
                     rhs=h_q[hf][b][:].bitcast(FP8X4),
                     rhs_scale=h_s[hf][b][:],
                     start=(b == 0),
                     stop=(b == 1),
                 )
-            y = ring.tile([P, HALF], F32, name="y", bufs=4)
-            nc.scalar.copy(out=y[:], in_=py[:])
-            staged["y", hf, nb] = y
+            if nb in FUSED:
+                y = ring.tile([P, HALF], F32, name="y", bufs=4)
+                nc.scalar.copy(out=y[:], in_=py[:])
+                staged["y", hf, nb] = y
+            else:
+                staged["y", hf, nb] = py
 
-        def finish(hf, nb):
-            d = ring.tile([P, HALF], F32, name="d", bufs=4)
-            nc.vector.tensor_tensor(
-                out=d[:], in0=g_all[nb][:].indirect(half_list(idx, hf)), in1=staged["y", hf, nb][:], op=ALU.subtract
-            )
-            nc.scalar.activation(out=d[:], in_=d[:], func=ACT.Abs)
-            nc.sync.dma_start(out=out[nb * P : (nb + 1) * P, hf * HALF : (hf + 1) * HALF], in_=d[:])
+        def gather_g(nb):
+            if nb not in FUSED:
+                g = held([P, S], F32, "g%d" % nb)
+                gather(g, g_all[nb], idx[:])
+                staged["g", nb] = g
 
-        gather(ts, ts_all, idx[:])
-        cast_wa(0, 0)
+        def finish(hf, nb, pieces=1):
+            d = ring.tile([P, HALF], F32, name="d", bufs=DBUFS)
+            w = HALF // pieces
+            for u in range(pieces):
+                cols = slice(u * w, (u + 1) * w)
+                s0 = hf * HALF + u * w
+                if nb in FUSED:
+                    measured = g_all[nb][:].indirect(idx[:, s0 // 16 : (s0 + w) // 16])
+                    nc.vector.tensor_tensor(out=d[:, cols], in0=measured, in1=staged["y", hf, nb][:, cols], op=ALU.subtract)
+                else:
+                    nc.vector.tensor_tensor(
+                        out=d[:, cols], in0=staged["y", hf, nb][:, cols], in1=staged["g", nb][:, s0 : s0 + w], op=ALU.subtract
+                    )
+                nc.scalar.activation(out=d[:, cols], in_=d[:, cols], func=ACT.Abs)
+                nc.sync.dma_start(out=out[nb * P : (nb + 1) * P, s0 : s0 + w], in_=d[:, cols])
+
+        permute_wbw()
         gather(t2s, t2s_all, idx2[:])
-        quantize(wa_q[0][0], wa_s[0][0], staged["wa", 0, 0])
-        cast_wa(0, 1)
-        permute_wb()
-        quantize(wa_q[0][1], wa_s[0][1], staged["wa", 0, 1])
-        cast_wa(1, 0)
         gather(t2w[0], t2w_all, half_list(idx2, 0))
-        modulation(0, 0)
         gather(t2w[1], t2w_all, half_list(idx2, 1))
+        permute_wbs()
+        cast_wa(0, 0)
+        modulation(0, 0)
         gather(tw[0][0], tw_all[0], half_list(idx, 0))
-        quantize(wa_q[1][0], wa_s[1][0], staged["wa", 1, 0])
-        modulation(0, 1)
         gather(tw[1][0], tw_all[0], half_list(idx, 1))
+        gather(ts, ts_all, idx[:])
+        cast_wa(0, 1)
         gather(tw[0][1], tw_all[1], half_list(idx, 0))
+        quantize(wa_q[0], wa_s[0], wa16[0][:])
+        modulation(1, 0)
         hidden(0, 0)
-        cast_wa(1, 1)
         gather(tw[1][1], tw_all[1], half_list(idx, 1))
+        cast_wa(1, 0)
+        cast_wa(1, 1)
         quantize(h_q[0][0], h_s[0][0], staged["h", 0, 0])
-        quantize(wa_q[1][1], wa_s[1][1], staged["wa", 1, 1])
+        hidden(1, 0)
+        quantize(wa_q[1], wa_s[1], wa16[1][:])
+        quantize(h_q[1][0], h_s[1][0], staged["h", 1, 0])
+        modulation(0, 1)
         cast_wt(0)
         hidden(0, 1)
-        modulation(1, 0)
-        quantize(wt_q[0], wt_s[0], staged["wt", 0])
-        quantize(h_q[0][1], h_s[0][1], staged["h", 0, 1])
-        cast_wt(1)
-        hidden(1, 0)
         modulation(1, 1)
-        quantize(wt_q[1], wt_s[1], staged["wt", 1])
-        quantize(h_q[1][0], h_s[1][0], staged["h", 1, 0])
-        for nb in range(4):
-            predict(0, nb)
+        cast_wt(1)
+        quantize(h_q[0][1], h_s[0][1], staged["h", 0, 1])
         hidden(1, 1)
-        finish(0, 0)
+        quantize(wt_q, wt_s, wt16[:])
         quantize(h_q[1][1], h_s[1][1], staged["h", 1, 1])
-        for nb in range(1, 4):
-            finish(0, nb)
-        for nb in range(4):
-            predict(1, nb)
-        for nb in range(4):
-            finish(1, nb)
+        predict(0, 0)
+        predict(0, 1)
+        predict(0, 2)
+        predict(0, 3)
+        finish(0, 0)
+        finish(0, 1)
+        finish(0, 2)
+        finish(0, 3)
+        predict(1, 0)
+        predict(1, 1)
+        predict(1, 2)
+        predict(1, 3)
+        finish(1, 0)
+        finish(1, 1)
+        finish(1, 2)
+        finish(1, 3, 2)

@@ -21,9 +21,12 @@ PACK = 4
 KP = P * PACK
 HALF = 512
 TOK = 128
+RUN = 2
 FUSED = (0, 1, 2, 3)
-DBUFS = 4
-MODTAG = [["mod", "wa_raw11"], ["wa_raw01", "wt_raw0"]]
+GCAST = ()
+VCAST = ((0, 1),)
+DBUFS = 8
+YBUFS = 6
 
 
 def tile_list_locus_cell_tracks_kernel(
@@ -117,22 +120,36 @@ def tile_list_locus_cell_tracks_kernel(
         wt16 = held([P, 2 * N * PACK], BF16, "wt16")
         h_q = [[held([P, HALF], U32, "h_q%d%d" % (hf, b)) for b in range(2)] for hf in range(2)]
         h_s = [[held([P, HALF], U8, "h_s%d%d" % (hf, b)) for b in range(2)] for hf in range(2)]
-        mod = [[None, None], [None, None]]
+        mod = [[held([P, PACK, HALF], F32, "mod00"), held([P, PACK, HALF], F32, "mod01")], [wa_raw[0][0], wt_raw[1]]]
         staged = {}
+        REUSE = {(1, 0): wa16[1]}
 
         def cast_wa(b, a):
-            nc.scalar.activation(
-                out=wa16[b][:, a * KP * PACK : (a + 1) * KP * PACK].rearrange("p (t m j) -> p m j t", t=PACK, j=PACK),
-                in_=wa_raw[b][a][:].rearrange("p j (m t) -> p m j t", t=PACK),
-                func=ACT.Copy,
-            )
+            dst = wa16[b][:, a * KP * PACK : (a + 1) * KP * PACK].rearrange("p (t m j) -> p m j t", t=PACK, j=PACK)
+            src = wa_raw[b][a][:].rearrange("p j (m t) -> p m j t", t=PACK)
+            for pair in (slice(0, 2), slice(2, 4)):
+                if (b, a) in VCAST:
+                    nc.vector.tensor_copy(out=dst[:, :, :, pair], in_=src[:, :, :, pair])
+                else:
+                    nc.scalar.activation(out=dst[:, :, :, pair], in_=src[:, :, :, pair], func=ACT.Copy)
 
         def cast_wt(b):
-            nc.scalar.activation(
-                out=wt16[:, b * N * PACK : (b + 1) * N * PACK].rearrange("p (c i j) -> p c j i", i=4, j=PACK),
-                in_=wt_raw[b][:].rearrange("p j (c i) -> p c j i", i=4),
-                func=ACT.Copy,
-            )
+            if b in GCAST:
+                for u in range(4):
+                    nc.gpsimd.tensor_scalar(
+                        out=wt16[:, (b * N + u * P) * PACK : (b * N + (u + 1) * P) * PACK].rearrange("p (n j) -> p n j", j=PACK),
+                        in0=wt_raw[b][:, :, u * P : (u + 1) * P].rearrange("p j n -> p n j"),
+                        scalar1=1.0,
+                        scalar2=0.0,
+                        op0=ALU.mult,
+                        op1=ALU.add,
+                    )
+            else:
+                nc.scalar.activation(
+                    out=wt16[:, b * N * PACK : (b + 1) * N * PACK].rearrange("p (c i j) -> p c j i", i=RUN, j=PACK),
+                    in_=wt_raw[b][:].rearrange("p j (c i) -> p c j i", i=RUN),
+                    func=ACT.Copy,
+                )
 
         def quantize(codes, scales, src):
             nc.vector.quantize_mx(out=codes[:].bitcast(FP8X4), scales=scales[:], in_=src)
@@ -153,7 +170,6 @@ def tile_list_locus_cell_tracks_kernel(
             )
 
         def modulation(hf, b):
-            mod[hf][b] = held([P, PACK, HALF], F32, MODTAG[hf][b])
             for t in range(PACK):
                 c0 = b * KP + t * P
                 pb = wide_pool.tile([P, HALF], F32, name="wide")
@@ -169,7 +185,10 @@ def tile_list_locus_cell_tracks_kernel(
                 nc.scalar.activation(out=mod[hf][b][:, t, :], in_=pb[:], func=ACT.Tanh, bias=bias[:, b, t : t + 1])
 
         def hidden(hf, b):
-            h16 = ring.tile([P, HALF, PACK], BF16, name="h16", align_bytes=64)
+            if (hf, b) in REUSE:
+                h16 = REUSE[hf, b][:, : HALF * PACK].rearrange("p (n t) -> p n t", t=PACK)
+            else:
+                h16 = ring.tile([P, HALF, PACK], BF16, name="h16", align_bytes=64)
             for u in range(HALF // TOK):
                 cols = slice(u * TOK, (u + 1) * TOK)
                 pa = pa_pool.tile([P, PACK, TOK], F32, name="pa")
@@ -185,9 +204,9 @@ def tile_list_locus_cell_tracks_kernel(
                             stop=(a == 1),
                         )
                 nc.vector.tensor_tensor(
-                    out=h16[:, cols, :].rearrange("p (c i) t -> p c t i", i=4),
-                    in0=pa[:].rearrange("p t (c i) -> p c t i", i=4),
-                    in1=mod[hf][b][:, :, cols].rearrange("p t (c i) -> p c t i", i=4),
+                    out=h16[:, cols, :].rearrange("p (c i) t -> p c t i", i=RUN),
+                    in0=pa[:].rearrange("p t (c i) -> p c t i", i=RUN),
+                    in1=mod[hf][b][:, :, cols].rearrange("p t (c i) -> p c t i", i=RUN),
                     op=ALU.mult,
                 )
             staged["h", hf, b] = h16[:].rearrange("p n t -> p (n t)")
@@ -205,7 +224,7 @@ def tile_list_locus_cell_tracks_kernel(
                     stop=(b == 1),
                 )
             if nb in FUSED:
-                y = ring.tile([P, HALF], F32, name="y", bufs=4)
+                y = ring.tile([P, HALF], F32, name="y", bufs=YBUFS)
                 nc.scalar.copy(out=y[:], in_=py[:])
                 staged["y", hf, nb] = y
             else:
@@ -240,42 +259,42 @@ def tile_list_locus_cell_tracks_kernel(
         permute_wbs()
         cast_wa(0, 0)
         modulation(0, 0)
+        modulation(1, 0)
+        modulation(0, 1)
         gather(tw[0][0], tw_all[0], half_list(idx, 0))
         gather(tw[1][0], tw_all[0], half_list(idx, 1))
         gather(ts, ts_all, idx[:])
         cast_wa(0, 1)
         gather(tw[0][1], tw_all[1], half_list(idx, 0))
         quantize(wa_q[0], wa_s[0], wa16[0][:])
-        modulation(1, 0)
         hidden(0, 0)
         gather(tw[1][1], tw_all[1], half_list(idx, 1))
         cast_wa(1, 0)
         cast_wa(1, 1)
         quantize(h_q[0][0], h_s[0][0], staged["h", 0, 0])
-        hidden(1, 0)
         quantize(wa_q[1], wa_s[1], wa16[1][:])
+        hidden(1, 0)
         quantize(h_q[1][0], h_s[1][0], staged["h", 1, 0])
-        modulation(0, 1)
         cast_wt(0)
+        cast_wt(1)
         hidden(0, 1)
         modulation(1, 1)
-        cast_wt(1)
         quantize(h_q[0][1], h_s[0][1], staged["h", 0, 1])
-        hidden(1, 1)
         quantize(wt_q, wt_s, wt16[:])
-        quantize(h_q[1][1], h_s[1][1], staged["h", 1, 1])
         predict(0, 0)
         predict(0, 1)
         predict(0, 2)
         predict(0, 3)
+        hidden(1, 1)
         finish(0, 0)
-        finish(0, 1)
-        finish(0, 2)
-        finish(0, 3)
+        quantize(h_q[1][1], h_s[1][1], staged["h", 1, 1])
         predict(1, 0)
         predict(1, 1)
         predict(1, 2)
         predict(1, 3)
+        finish(0, 1)
+        finish(0, 2)
+        finish(0, 3)
         finish(1, 0)
         finish(1, 1)
         finish(1, 2)

@@ -19,14 +19,13 @@ ALU = mybir.AluOpType
 P = 128
 PACK = 4
 KP = P * PACK
-HALF = 512
+HALF = S // 2
 TOK = 128
 RUN = 2
-FUSED = (0, 1, 2, 3)
-GCAST = ()
-VCAST = ((0, 1),)
-DBUFS = 8
-YBUFS = 6
+PER_COL = 16
+OUT_TILES = 2 * N // P
+FREE = 2
+LAST_PIECES = (256, 128, 128)
 
 
 def tile_list_locus_cell_tracks_kernel(
@@ -35,15 +34,15 @@ def tile_list_locus_cell_tracks_kernel(
     nc = tc.nc
     with ExitStack() as ctx:
         keep = ctx.enter_context(tc.tile_pool(name="keep", bufs=1))
-        ring = ctx.enter_context(tc.tile_pool(name="ring", bufs=3))
-        pa_pool = ctx.enter_context(tc.psum_pool(name="pa", bufs=4))
-        wide_pool = ctx.enter_context(tc.psum_pool(name="wide", bufs=4))
+        ring = ctx.enter_context(tc.tile_pool(name="ring", bufs=2))
+        a_banks = ctx.enter_context(tc.psum_pool(name="a_banks", bufs=4))
+        wide_banks = ctx.enter_context(tc.psum_pool(name="wide_banks", bufs=4))
 
         def held(shape, dtype, name):
             return keep.tile(shape, dtype, name=name, align_bytes=64)
 
-        idx = keep.tile([P, S // 16], U16, name="idx")
-        idx2 = keep.tile([P, S // 16], U16, name="idx2")
+        idx = keep.tile([P, S // PER_COL], U16, name="idx")
+        idx2 = keep.tile([P, S // PER_COL], U16, name="idx2")
         ts_all = held([P, T], U8, "ts_all")
         t2s_all = held([P, T], U8, "t2s_all")
         wbs_raw = held([P, H], U8, "wbs_raw")
@@ -53,249 +52,214 @@ def tile_list_locus_cell_tracks_kernel(
         t2w_all = held([P, T], U32, "t2w_all")
         wa_raw = [[held([P, PACK, KP], F32, "wa_raw%d%d" % (b, a)) for a in range(2)] for b in range(2)]
         wt_raw = [held([P, PACK, N], F32, "wt_raw%d" % b) for b in range(2)]
-        g_all = [held([P, T], F32, "g_all%d" % nb) for nb in range(4)]
+        g_all = [held([P, T], F32, "g_all%d" % nb) for nb in range(N // P)]
 
-        nc.vector.memset(t2s_all[:].bitcast(I32), 0)
-        nc.vector.memset(wbs_raw[:].bitcast(I32), 0)
-        nc.vector.memset(ts_all[:].bitcast(I32), 0)
+        for scale_tile in (t2s_all, wbs_raw, ts_all):
+            nc.vector.memset(scale_tile[:].bitcast(I32), 0)
 
         def load_words(dst, src):
             nc.sync.dma_start(out=dst[:].bitcast(I32), in_=src.rearrange("p t i -> p (t i)").bitcast(I32))
 
-        def load_scales(queue, dst, src):
+        def load_scales(dst, src):
             passes = src.shape[0]
             for q in range(4):
-                queue.dma_start(
+                nc.sync.dma_start(
                     out=dst[32 * q : 32 * q + 4 * passes, :].bitcast(I32),
                     in_=src[:, 4 * q : 4 * q + 4, :].bitcast(I32),
                 )
 
+        def load_rows(dst, rows):
+            nc.sync.dma_start(out=dst[:], in_=rows.rearrange("(p j) c -> p j c", j=PACK))
+
         def load_wa(b, a):
-            nc.sync.dma_start(
-                out=wa_raw[b][a][:],
-                in_=wa[a * KP : (a + 1) * KP, b * KP : (b + 1) * KP].rearrange("(p j) c -> p j c", j=PACK),
-            )
-
-        def load_wt(b):
-            nc.sync.dma_start(out=wt_raw[b][:], in_=wt[b * KP : (b + 1) * KP, :].rearrange("(p j) n -> p j n", j=PACK))
-
-        def load_g(nb):
-            nc.sync.dma_start(out=g_all[nb][:], in_=gT[nb * P : (nb + 1) * P, :])
+            load_rows(wa_raw[b][a], wa[a * KP : (a + 1) * KP, b * KP : (b + 1) * KP])
 
         nc.sync.dma_start(idx2[:], offs2)
         nc.sync.dma_start(out=wbw_raw[:].bitcast(I32), in_=wb_words[0].bitcast(I32))
-        load_scales(nc.sync, t2s_all, tab2_scales)
+        load_scales(t2s_all, tab2_scales)
         load_words(t2w_all, tab2_words[0])
-        load_scales(nc.sync, wbs_raw, wb_scales)
-        load_wa(0, 0)
+        load_scales(wbs_raw, wb_scales)
+        load_words(tw_all[0], tab_words[0])
         nc.sync.dma_start(idx[:], offs)
         nc.sync.dma_start(out=bias[:], in_=bc.rearrange("(b p t) -> p b t", p=P, t=PACK))
-        load_words(tw_all[0], tab_words[0])
-        load_scales(nc.sync, ts_all, tab_scales)
+        load_wa(0, 0)
+        load_scales(ts_all, tab_scales)
         load_wa(0, 1)
         load_words(tw_all[1], tab_words[1])
         load_wa(1, 0)
         load_wa(1, 1)
-        load_wt(0)
-        load_wt(1)
-        load_g(0)
-        load_g(1)
-        load_g(2)
-        load_g(3)
-
-        def half_list(lst, hf):
-            return lst[:, hf * HALF // 16 : (hf + 1) * HALF // 16]
+        for b in range(2):
+            load_rows(wt_raw[b], wt[b * KP : (b + 1) * KP, :])
+        for nb in range(N // P):
+            nc.sync.dma_start(out=g_all[nb][:], in_=gT[nb * P : (nb + 1) * P, :])
 
         ts = held([P, S], U8, "ts")
         t2s = held([P, S], U8, "t2s")
-        tw = [[held([P, HALF], U32, "tw%d%d" % (hf, a)) for a in range(2)] for hf in range(2)]
-        t2w = [held([P, HALF], U32, "t2w%d" % hf) for hf in range(2)]
+        t2w = held([P, S], U32, "t2w")
+        tw = [held([P, S], U32, "tw%d" % a) for a in range(2)]
         wbw = held([P, 2 * H], U8, "wbw")
         wbs = held([P, H], U8, "wbs")
         wa_q = [held([P, 2 * KP], U32, "wa_q%d" % b) for b in range(2)]
         wa_s = [held([P, 2 * KP], U8, "wa_s%d" % b) for b in range(2)]
         wt_q = held([P, 2 * N], U32, "wt_q")
         wt_s = held([P, 2 * N], U8, "wt_s")
-        wa16 = [held([P, 2 * KP * PACK], BF16, "wa16%d" % b) for b in range(2)]
-        wt16 = held([P, 2 * N * PACK], BF16, "wt16")
         h_q = [[held([P, HALF], U32, "h_q%d%d" % (hf, b)) for b in range(2)] for hf in range(2)]
         h_s = [[held([P, HALF], U8, "h_s%d%d" % (hf, b)) for b in range(2)] for hf in range(2)]
-        mod = [[held([P, PACK, HALF], F32, "mod00"), held([P, PACK, HALF], F32, "mod01")], [wa_raw[0][0], wt_raw[1]]]
-        staged = {}
-        REUSE = {(1, 0): wa16[1]}
 
-        def cast_wa(b, a):
-            dst = wa16[b][:, a * KP * PACK : (a + 1) * KP * PACK].rearrange("p (t m j) -> p m j t", t=PACK, j=PACK)
-            src = wa_raw[b][a][:].rearrange("p j (m t) -> p m j t", t=PACK)
-            for pair in (slice(0, 2), slice(2, 4)):
-                if (b, a) in VCAST:
-                    nc.vector.tensor_copy(out=dst[:, :, :, pair], in_=src[:, :, :, pair])
-                else:
-                    nc.scalar.activation(out=dst[:, :, :, pair], in_=src[:, :, :, pair], func=ACT.Copy)
+        shared16 = held([P, FREE * TOK * PACK + 2 * KP * PACK], BF16, "shared16")
+        wa16 = [held([P, 2 * KP * PACK], BF16, "wa16"), shared16[:, FREE * TOK * PACK :]]
+        wt16 = held([P, 2 * N * PACK], BF16, "wt16")
+        h16 = {(1, 0): shared16[:, : HALF * PACK]}
+        mod = [[held([P, PACK, HALF], F32, "mod%d" % b) for b in range(2)], [wa_raw[0][0], wt_raw[1]]]
+        y_sb = {}
 
-        def cast_wt(b):
-            if b in GCAST:
-                for u in range(4):
-                    nc.gpsimd.tensor_scalar(
-                        out=wt16[:, (b * N + u * P) * PACK : (b * N + (u + 1) * P) * PACK].rearrange("p (n j) -> p n j", j=PACK),
-                        in0=wt_raw[b][:, :, u * P : (u + 1) * P].rearrange("p j n -> p n j"),
-                        scalar1=1.0,
-                        scalar2=0.0,
-                        op0=ALU.mult,
-                        op1=ALU.add,
-                    )
-            else:
-                nc.scalar.activation(
-                    out=wt16[:, b * N * PACK : (b + 1) * N * PACK].rearrange("p (c i j) -> p c j i", i=RUN, j=PACK),
-                    in_=wt_raw[b][:].rearrange("p j (c i) -> p c j i", i=RUN),
-                    func=ACT.Copy,
-                )
+        def entries(lst, start, count):
+            return lst[:, start // PER_COL : (start + count) // PER_COL]
+
+        def gather(dst, table, lst):
+            nc.vector.tensor_copy(dst, table[:].indirect(lst))
 
         def quantize(codes, scales, src):
             nc.vector.quantize_mx(out=codes[:].bitcast(FP8X4), scales=scales[:], in_=src)
 
-        def gather(dst, table, lst):
-            nc.vector.tensor_copy(dst[:], table[:].indirect(lst))
+        def scalar_cast(dst, src):
+            nc.scalar.activation(out=dst, in_=src, func=ACT.Copy)
 
-        def permute_wbw():
-            nc.vector.tensor_copy(
-                out=wbw[:].bitcast(U16).rearrange("p (b t m) -> p b t m", b=2, t=PACK),
-                in_=wbw_raw[:].bitcast(U16).rearrange("p (b m t) -> p b t m", b=2, t=PACK),
+        def cast_wa(b, a, cast):
+            dst = wa16[b][:, a * KP * PACK : (a + 1) * KP * PACK].rearrange("p (t m j) -> p m j t", t=PACK, j=PACK)
+            src = wa_raw[b][a][:].rearrange("p j (m t) -> p m j t", t=PACK)
+            for pair in (slice(0, 2), slice(2, 4)):
+                cast(dst[:, :, :, pair], src[:, :, :, pair])
+
+        def cast_wt(b):
+            scalar_cast(
+                wt16[:, b * N * PACK : (b + 1) * N * PACK].rearrange("p (c i j) -> p c j i", i=RUN, j=PACK),
+                wt_raw[b][:].rearrange("p j (c i) -> p c j i", i=RUN),
             )
 
-        def permute_wbs():
+        def reorder_wb(dst, src):
             nc.vector.tensor_copy(
-                out=wbs[:].rearrange("p (b t m) -> p b t m", b=2, t=PACK),
-                in_=wbs_raw[:].rearrange("p (b m t) -> p b t m", b=2, t=PACK),
+                out=dst.rearrange("p (b t m) -> p b t m", b=2, t=PACK),
+                in_=src.rearrange("p (b m t) -> p b t m", b=2, t=PACK),
             )
 
         def modulation(hf, b):
+            cols = slice(hf * HALF, (hf + 1) * HALF)
             for t in range(PACK):
                 c0 = b * KP + t * P
-                pb = wide_pool.tile([P, HALF], F32, name="wide")
+                bank = wide_banks.tile([P, HALF], F32, name="wide")
                 nc.tensor.matmul_mx(
-                    out=pb[:],
+                    out=bank[:],
                     lhsT=wbw[:, 2 * c0 : 2 * (c0 + P)].bitcast(FP4X4),
                     lhsT_scale=wbs[:, c0 : c0 + P],
-                    rhs=t2w[hf][:].bitcast(FP8X4),
-                    rhs_scale=t2s[:, hf * HALF : (hf + 1) * HALF],
+                    rhs=t2w[:, cols].bitcast(FP8X4),
+                    rhs_scale=t2s[:, cols],
                     start=True,
                     stop=True,
                 )
-                nc.scalar.activation(out=mod[hf][b][:, t, :], in_=pb[:], func=ACT.Tanh, bias=bias[:, b, t : t + 1])
+                nc.scalar.activation(out=mod[hf][b][:, t, :], in_=bank[:], func=ACT.Tanh, bias=bias[:, b, t : t + 1])
 
         def hidden(hf, b):
-            if (hf, b) in REUSE:
-                h16 = REUSE[hf, b][:, : HALF * PACK].rearrange("p (n t) -> p n t", t=PACK)
-            else:
-                h16 = ring.tile([P, HALF, PACK], BF16, name="h16", align_bytes=64)
+            if (hf, b) not in h16:
+                h16[hf, b] = ring.tile([P, HALF * PACK], BF16, name="h16", align_bytes=64)
             for u in range(HALF // TOK):
-                cols = slice(u * TOK, (u + 1) * TOK)
-                pa = pa_pool.tile([P, PACK, TOK], F32, name="pa")
+                cols = slice(hf * HALF + u * TOK, hf * HALF + (u + 1) * TOK)
+                bank = a_banks.tile([P, PACK, TOK], F32, name="a")
                 for t in range(PACK):
                     for a in range(2):
+                        w_cols = slice(a * KP + t * P, a * KP + (t + 1) * P)
                         nc.tensor.matmul_mx(
-                            out=pa[:, t, :],
-                            lhsT=wa_q[b][:, a * KP + t * P : a * KP + (t + 1) * P].bitcast(FP8X4),
-                            lhsT_scale=wa_s[b][:, a * KP + t * P : a * KP + (t + 1) * P],
-                            rhs=tw[hf][a][:, cols].bitcast(FP8X4),
-                            rhs_scale=ts[4 * a : P, hf * HALF + u * TOK : hf * HALF + (u + 1) * TOK],
+                            out=bank[:, t, :],
+                            lhsT=wa_q[b][:, w_cols].bitcast(FP8X4),
+                            lhsT_scale=wa_s[b][:, w_cols],
+                            rhs=tw[a][:, cols].bitcast(FP8X4),
+                            rhs_scale=ts[4 * a : P, cols],
                             start=(a == 0),
                             stop=(a == 1),
                         )
+                dst = h16[hf, b][:, u * TOK * PACK : (u + 1) * TOK * PACK]
                 nc.vector.tensor_tensor(
-                    out=h16[:, cols, :].rearrange("p (c i) t -> p c t i", i=RUN),
-                    in0=pa[:].rearrange("p t (c i) -> p c t i", i=RUN),
-                    in1=mod[hf][b][:, :, cols].rearrange("p t (c i) -> p c t i", i=RUN),
+                    out=dst.rearrange("p (c i t) -> p c t i", i=RUN, t=PACK),
+                    in0=bank[:].rearrange("p t (c i) -> p c t i", i=RUN),
+                    in1=mod[hf][b][:, :, u * TOK : (u + 1) * TOK].rearrange("p t (c i) -> p c t i", i=RUN),
                     op=ALU.mult,
                 )
-            staged["h", hf, b] = h16[:].rearrange("p n t -> p (n t)")
 
-        def predict(hf, nb):
-            py = wide_pool.tile([P, HALF], F32, name="wide")
-            for b in range(2):
-                nc.tensor.matmul_mx(
-                    out=py[:],
-                    lhsT=wt_q[:, b * N + nb * P : b * N + (nb + 1) * P].bitcast(FP8X4),
-                    lhsT_scale=wt_s[:, b * N + nb * P : b * N + (nb + 1) * P],
-                    rhs=h_q[hf][b][:].bitcast(FP8X4),
-                    rhs_scale=h_s[hf][b][:],
-                    start=(b == 0),
-                    stop=(b == 1),
-                )
-            if nb in FUSED:
-                y = ring.tile([P, HALF], F32, name="y", bufs=YBUFS)
-                nc.scalar.copy(out=y[:], in_=py[:])
-                staged["y", hf, nb] = y
-            else:
-                staged["y", hf, nb] = py
+        def quantize_h(hf, b):
+            quantize(h_q[hf][b], h_s[hf][b], h16[hf, b][:])
 
-        def gather_g(nb):
-            if nb not in FUSED:
-                g = held([P, S], F32, "g%d" % nb)
-                gather(g, g_all[nb], idx[:])
-                staged["g", nb] = g
-
-        def finish(hf, nb, pieces=1):
-            d = ring.tile([P, HALF], F32, name="d", bufs=DBUFS)
-            w = HALF // pieces
-            for u in range(pieces):
-                cols = slice(u * w, (u + 1) * w)
-                s0 = hf * HALF + u * w
-                if nb in FUSED:
-                    measured = g_all[nb][:].indirect(idx[:, s0 // 16 : (s0 + w) // 16])
-                    nc.vector.tensor_tensor(out=d[:, cols], in0=measured, in1=staged["y", hf, nb][:, cols], op=ALU.subtract)
-                else:
-                    nc.vector.tensor_tensor(
-                        out=d[:, cols], in0=staged["y", hf, nb][:, cols], in1=staged["g", nb][:, s0 : s0 + w], op=ALU.subtract
+        def predict(hf):
+            for nb in range(N // P):
+                bank = wide_banks.tile([P, HALF], F32, name="wide")
+                for b in range(2):
+                    w_cols = slice(b * N + nb * P, b * N + (nb + 1) * P)
+                    nc.tensor.matmul_mx(
+                        out=bank[:],
+                        lhsT=wt_q[:, w_cols].bitcast(FP8X4),
+                        lhsT_scale=wt_s[:, w_cols],
+                        rhs=h_q[hf][b][:].bitcast(FP8X4),
+                        rhs_scale=h_s[hf][b][:],
+                        start=(b == 0),
+                        stop=(b == 1),
                     )
-                nc.scalar.activation(out=d[:, cols], in_=d[:, cols], func=ACT.Abs)
-                nc.sync.dma_start(out=out[nb * P : (nb + 1) * P, s0 : s0 + w], in_=d[:, cols])
+                y_sb[hf, nb] = ring.tile([P, HALF], F32, name="y", bufs=OUT_TILES)
+                nc.scalar.copy(out=y_sb[hf, nb][:], in_=bank[:])
 
-        permute_wbw()
-        gather(t2s, t2s_all, idx2[:])
-        gather(t2w[0], t2w_all, half_list(idx2, 0))
-        gather(t2w[1], t2w_all, half_list(idx2, 1))
-        permute_wbs()
-        cast_wa(0, 0)
+        def finish(hf, nb, pieces=(HALF,)):
+            diff = ring.tile([P, HALF], F32, name="diff", bufs=OUT_TILES)
+            c0 = 0
+            for width in pieces:
+                cols = slice(c0, c0 + width)
+                s0 = hf * HALF + c0
+                nc.vector.tensor_tensor(
+                    out=diff[:, cols],
+                    in0=g_all[nb][:].indirect(entries(idx, s0, width)),
+                    in1=y_sb[hf, nb][:, cols],
+                    op=ALU.subtract,
+                )
+                nc.scalar.activation(out=diff[:, cols], in_=diff[:, cols], func=ACT.Abs)
+                nc.sync.dma_start(out=out[nb * P : (nb + 1) * P, s0 : s0 + width], in_=diff[:, cols])
+                c0 = c0 + width
+
+        reorder_wb(wbw[:].bitcast(U16), wbw_raw[:].bitcast(U16))
+        gather(t2s[:], t2s_all, idx2[:])
+        gather(t2w[:], t2w_all, idx2[:])
+        reorder_wb(wbs[:], wbs_raw[:])
         modulation(0, 0)
+
+        gather(tw[0][:], tw_all[0], idx[:])
+        cast_wa(0, 0, nc.vector.tensor_copy)
         modulation(1, 0)
+        gather(ts[:], ts_all, idx[:])
+        cast_wa(0, 1, nc.vector.tensor_copy)
         modulation(0, 1)
-        gather(tw[0][0], tw_all[0], half_list(idx, 0))
-        gather(tw[1][0], tw_all[0], half_list(idx, 1))
-        gather(ts, ts_all, idx[:])
-        cast_wa(0, 1)
-        gather(tw[0][1], tw_all[1], half_list(idx, 0))
         quantize(wa_q[0], wa_s[0], wa16[0][:])
+        for hf in range(2):
+            gather(tw[1][:, hf * HALF : (hf + 1) * HALF], tw_all[1], entries(idx, hf * HALF, HALF))
+
         hidden(0, 0)
-        gather(tw[1][1], tw_all[1], half_list(idx, 1))
-        cast_wa(1, 0)
-        cast_wa(1, 1)
-        quantize(h_q[0][0], h_s[0][0], staged["h", 0, 0])
+        cast_wa(1, 0, scalar_cast)
+        cast_wa(1, 1, scalar_cast)
+        quantize_h(0, 0)
         quantize(wa_q[1], wa_s[1], wa16[1][:])
         hidden(1, 0)
-        quantize(h_q[1][0], h_s[1][0], staged["h", 1, 0])
+        quantize_h(1, 0)
         cast_wt(0)
         cast_wt(1)
+
         hidden(0, 1)
         modulation(1, 1)
-        quantize(h_q[0][1], h_s[0][1], staged["h", 0, 1])
+        quantize_h(0, 1)
         quantize(wt_q, wt_s, wt16[:])
-        predict(0, 0)
-        predict(0, 1)
-        predict(0, 2)
-        predict(0, 3)
+        predict(0)
         hidden(1, 1)
         finish(0, 0)
-        quantize(h_q[1][1], h_s[1][1], staged["h", 1, 1])
-        predict(1, 0)
-        predict(1, 1)
-        predict(1, 2)
-        predict(1, 3)
-        finish(0, 1)
-        finish(0, 2)
-        finish(0, 3)
-        finish(1, 0)
-        finish(1, 1)
-        finish(1, 2)
-        finish(1, 3, 2)
+        quantize_h(1, 1)
+        predict(1)
+
+        last = N // P - 1
+        for hf in range(2):
+            for nb in range(1 - hf, last):
+                finish(hf, nb)
+        finish(0, last)
+        finish(1, last, LAST_PIECES)

@@ -25,6 +25,8 @@ RUN = 2
 PER_COL = 16
 OUT_TILES = 2 * N // P
 FREE = 2
+EARLY = 2
+NH = N // 2
 LAST_PIECES = (256, 128, 128)
 
 
@@ -38,8 +40,8 @@ def tile_list_locus_cell_tracks_kernel(
         a_banks = ctx.enter_context(tc.psum_pool(name="a_banks", bufs=4))
         wide_banks = ctx.enter_context(tc.psum_pool(name="wide_banks", bufs=4))
 
-        def held(shape, dtype, name):
-            return keep.tile(shape, dtype, name=name, align_bytes=64)
+        def held(shape, dtype, name, tag=None):
+            return keep.tile(shape, dtype, name=name, tag=tag or name, align_bytes=64)
 
         idx = keep.tile([P, S // PER_COL], U16, name="idx")
         idx2 = keep.tile([P, S // PER_COL], U16, name="idx2")
@@ -50,8 +52,12 @@ def tile_list_locus_cell_tracks_kernel(
         bias = held([P, H // KP, PACK], F32, "bias")
         tw_all = [held([P, T], U32, "tw_all%d" % a) for a in range(2)]
         t2w_all = held([P, T], U32, "t2w_all")
-        wa_raw = [[held([P, PACK, KP], F32, "wa_raw%d%d" % (b, a)) for a in range(2)] for b in range(2)]
-        wt_raw = [held([P, PACK, N], F32, "wt_raw%d" % b) for b in range(2)]
+        shared32 = held([P, EARLY + PACK, KP], F32, "shared32")
+        wa_raw = [
+            [held([P, PACK, KP], F32, "wa_raw0%d" % a)[:] for a in range(2)],
+            [held([P, PACK, KP], F32, "wa_raw10")[:], shared32[:, EARLY:, :]],
+        ]
+        wt_raw = held([P, 2, PACK, N], F32, "wt_raw")
         g_all = [held([P, T], F32, "g_all%d" % nb) for nb in range(N // P)]
 
         for scale_tile in (t2s_all, wbs_raw, ts_all):
@@ -60,16 +66,15 @@ def tile_list_locus_cell_tracks_kernel(
         def load_words(dst, src):
             nc.sync.dma_start(out=dst[:].bitcast(I32), in_=src.rearrange("p t i -> p (t i)").bitcast(I32))
 
-        def load_scales(dst, src):
-            passes = src.shape[0]
+        def load_scales(dst, src, a=0):
             for q in range(4):
                 nc.sync.dma_start(
-                    out=dst[32 * q : 32 * q + 4 * passes, :].bitcast(I32),
-                    in_=src[:, 4 * q : 4 * q + 4, :].bitcast(I32),
+                    out=dst[32 * q + 4 * a : 32 * q + 4 * a + 4, :].bitcast(I32),
+                    in_=src[a, 4 * q : 4 * q + 4, :].bitcast(I32),
                 )
 
         def load_rows(dst, rows):
-            nc.sync.dma_start(out=dst[:], in_=rows.rearrange("(p j) c -> p j c", j=PACK))
+            nc.sync.dma_start(out=dst, in_=rows.rearrange("(p j) c -> p j c", j=PACK))
 
         def load_wa(b, a):
             load_rows(wa_raw[b][a], wa[a * KP : (a + 1) * KP, b * KP : (b + 1) * KP])
@@ -78,24 +83,24 @@ def tile_list_locus_cell_tracks_kernel(
         nc.sync.dma_start(out=wbw_raw[:].bitcast(I32), in_=wb_words[0].bitcast(I32))
         load_scales(t2s_all, tab2_scales)
         load_words(t2w_all, tab2_words[0])
+        nc.sync.dma_start(out=bias[:], in_=bc.rearrange("(b p t) -> p b t", p=P, t=PACK))
         load_scales(wbs_raw, wb_scales)
         load_words(tw_all[0], tab_words[0])
         nc.sync.dma_start(idx[:], offs)
-        nc.sync.dma_start(out=bias[:], in_=bc.rearrange("(b p t) -> p b t", p=P, t=PACK))
+        load_scales(ts_all, tab_scales, 0)
         load_wa(0, 0)
-        load_scales(ts_all, tab_scales)
+        load_scales(ts_all, tab_scales, 1)
         load_wa(0, 1)
         load_words(tw_all[1], tab_words[1])
         load_wa(1, 0)
         load_wa(1, 1)
         for b in range(2):
-            load_rows(wt_raw[b], wt[b * KP : (b + 1) * KP, :])
+            load_rows(wt_raw[:, b], wt[b * KP : (b + 1) * KP, :])
         for nb in range(N // P):
             nc.sync.dma_start(out=g_all[nb][:], in_=gT[nb * P : (nb + 1) * P, :])
 
         ts = held([P, S], U8, "ts")
         t2s = held([P, S], U8, "t2s")
-        t2w = held([P, S], U32, "t2w")
         tw = [held([P, S], U32, "tw%d" % a) for a in range(2)]
         wbw = held([P, 2 * H], U8, "wbw")
         wbs = held([P, H], U8, "wbs")
@@ -110,7 +115,18 @@ def tile_list_locus_cell_tracks_kernel(
         wa16 = [held([P, 2 * KP * PACK], BF16, "wa16"), shared16[:, FREE * TOK * PACK :]]
         wt16 = held([P, 2 * N * PACK], BF16, "wt16")
         h16 = {(1, 0): shared16[:, : HALF * PACK]}
-        mod = [[held([P, PACK, HALF], F32, "mod%d" % b) for b in range(2)], [wa_raw[0][0], wt_raw[1]]]
+        mod = [
+            [held([P, PACK, HALF], F32, "mod")[:], shared32[:, :PACK, :]],
+            [wa_raw[0][0], wt_raw[:, :, :, :NH].rearrange("p u t c -> p t u c")],
+        ]
+
+        def mod_cols(hf, b, c0, count):
+            if (hf, b) == (1, 1):
+                if count == HALF:
+                    return mod[1][1]
+                return mod[1][1][:, :, c0 // NH, c0 % NH : c0 % NH + count]
+            return mod[hf][b][:, :, c0 : c0 + count]
+
         y_sb = {}
 
         def entries(lst, start, count):
@@ -120,22 +136,28 @@ def tile_list_locus_cell_tracks_kernel(
             nc.vector.tensor_copy(dst, table[:].indirect(lst))
 
         def quantize(codes, scales, src):
-            nc.vector.quantize_mx(out=codes[:].bitcast(FP8X4), scales=scales[:], in_=src)
+            nc.vector.quantize_mx(out=codes.bitcast(FP8X4), scales=scales, in_=src)
 
         def scalar_cast(dst, src):
             nc.scalar.activation(out=dst, in_=src, func=ACT.Copy)
 
         def cast_wa(b, a, cast):
             dst = wa16[b][:, a * KP * PACK : (a + 1) * KP * PACK].rearrange("p (t m j) -> p m j t", t=PACK, j=PACK)
-            src = wa_raw[b][a][:].rearrange("p j (m t) -> p m j t", t=PACK)
+            src = wa_raw[b][a].rearrange("p j (m t) -> p m j t", t=PACK)
             for pair in (slice(0, 2), slice(2, 4)):
                 cast(dst[:, :, :, pair], src[:, :, :, pair])
 
-        def cast_wt(b):
-            scalar_cast(
-                wt16[:, b * N * PACK : (b + 1) * N * PACK].rearrange("p (c i j) -> p c j i", i=RUN, j=PACK),
-                wt_raw[b][:].rearrange("p j (c i) -> p c j i", i=RUN),
-            )
+        def cast_wt(nh):
+            for b in range(2):
+                c0 = (2 * nh + b) * NH * PACK
+                scalar_cast(
+                    wt16[:, c0 : c0 + NH * PACK].rearrange("p (c i j) -> p c j i", i=RUN, j=PACK),
+                    wt_raw[:, b, :, nh * NH : (nh + 1) * NH].rearrange("p j (c i) -> p c j i", i=RUN),
+                )
+
+        def quantize_wt(nh):
+            cols = slice(nh * N, (nh + 1) * N)
+            quantize(wt_q[:, cols], wt_s[:, cols], wt16[:, nh * N * PACK : (nh + 1) * N * PACK])
 
         def reorder_wb(dst, src):
             nc.vector.tensor_copy(
@@ -152,12 +174,14 @@ def tile_list_locus_cell_tracks_kernel(
                     out=bank[:],
                     lhsT=wbw[:, 2 * c0 : 2 * (c0 + P)].bitcast(FP4X4),
                     lhsT_scale=wbs[:, c0 : c0 + P],
-                    rhs=t2w[:, cols].bitcast(FP8X4),
+                    rhs=t2w[hf][:].bitcast(FP8X4),
                     rhs_scale=t2s[:, cols],
                     start=True,
                     stop=True,
                 )
-                nc.scalar.activation(out=mod[hf][b][:, t, :], in_=bank[:], func=ACT.Tanh, bias=bias[:, b, t : t + 1])
+                dst = mod_cols(hf, b, 0, HALF)[:, t]
+                src = bank[:].rearrange("p (u c) -> p u c", u=2) if (hf, b) == (1, 1) else bank[:]
+                nc.scalar.activation(out=dst, in_=src, func=ACT.Tanh, bias=bias[:, b, t : t + 1])
 
         def hidden(hf, b):
             if (hf, b) not in h16:
@@ -181,18 +205,19 @@ def tile_list_locus_cell_tracks_kernel(
                 nc.vector.tensor_tensor(
                     out=dst.rearrange("p (c i t) -> p c t i", i=RUN, t=PACK),
                     in0=bank[:].rearrange("p t (c i) -> p c t i", i=RUN),
-                    in1=mod[hf][b][:, :, u * TOK : (u + 1) * TOK].rearrange("p t (c i) -> p c t i", i=RUN),
+                    in1=mod_cols(hf, b, u * TOK, TOK).rearrange("p t (c i) -> p c t i", i=RUN),
                     op=ALU.mult,
                 )
 
         def quantize_h(hf, b):
-            quantize(h_q[hf][b], h_s[hf][b], h16[hf, b][:])
+            quantize(h_q[hf][b][:], h_s[hf][b][:], h16[hf, b][:])
 
-        def predict(hf):
-            for nb in range(N // P):
+        def predict(hf, nh):
+            for nb in (2 * nh, 2 * nh + 1):
                 bank = wide_banks.tile([P, HALF], F32, name="wide")
                 for b in range(2):
-                    w_cols = slice(b * N + nb * P, b * N + (nb + 1) * P)
+                    w0 = nh * N + b * NH + nb % 2 * P
+                    w_cols = slice(w0, w0 + P)
                     nc.tensor.matmul_mx(
                         out=bank[:],
                         lhsT=wt_q[:, w_cols].bitcast(FP8X4),
@@ -223,43 +248,50 @@ def tile_list_locus_cell_tracks_kernel(
 
         reorder_wb(wbw[:].bitcast(U16), wbw_raw[:].bitcast(U16))
         gather(t2s[:], t2s_all, idx2[:])
-        gather(t2w[:], t2w_all, idx2[:])
+        t2w = [held([P, HALF], U32, "t2w0")]
+        gather(t2w[0][:], t2w_all, entries(idx2, 0, HALF))
         reorder_wb(wbs[:], wbs_raw[:])
+        t2w.append(held([P, HALF], U32, "t2w1", tag="wbs_raw"))
+        gather(t2w[1][:], t2w_all, entries(idx2, HALF, HALF))
         modulation(0, 0)
 
         gather(tw[0][:], tw_all[0], idx[:])
-        cast_wa(0, 0, nc.vector.tensor_copy)
+        cast_wa(0, 0, scalar_cast)
         modulation(1, 0)
         gather(ts[:], ts_all, idx[:])
         cast_wa(0, 1, nc.vector.tensor_copy)
-        modulation(0, 1)
-        quantize(wa_q[0], wa_s[0], wa16[0][:])
+        quantize(wa_q[0][:], wa_s[0][:], wa16[0][:])
         for hf in range(2):
             gather(tw[1][:, hf * HALF : (hf + 1) * HALF], tw_all[1], entries(idx, hf * HALF, HALF))
 
         hidden(0, 0)
         cast_wa(1, 0, scalar_cast)
         cast_wa(1, 1, scalar_cast)
+        modulation(0, 1)
         quantize_h(0, 0)
-        quantize(wa_q[1], wa_s[1], wa16[1][:])
+        quantize(wa_q[1][:], wa_s[1][:], wa16[1][:])
         hidden(1, 0)
         quantize_h(1, 0)
         cast_wt(0)
-        cast_wt(1)
 
         hidden(0, 1)
         modulation(1, 1)
         quantize_h(0, 1)
-        quantize(wt_q, wt_s, wt16[:])
-        predict(0)
+        quantize_wt(0)
+        predict(0, 0)
+        cast_wt(1)
         hidden(1, 1)
         finish(0, 0)
         quantize_h(1, 1)
-        predict(1)
+        predict(1, 0)
+        quantize_wt(1)
+        predict(0, 1)
+        predict(1, 1)
 
-        last = N // P - 1
-        for hf in range(2):
-            for nb in range(1 - hf, last):
-                finish(hf, nb)
-        finish(0, last)
-        finish(1, last, LAST_PIECES)
+        finish(0, 1)
+        finish(1, 0)
+        finish(1, 1)
+        finish(0, 2)
+        finish(1, 2)
+        finish(0, 3)
+        finish(1, 3, LAST_PIECES)

@@ -24,8 +24,6 @@ TOK = 128
 RUN = 2
 PER_COL = 16
 OUT_TILES = 2 * N // P
-FREE = 2
-EARLY = 2
 NH = N // 2
 LAST_PIECES = (256, 128, 128)
 
@@ -36,6 +34,7 @@ def tile_list_locus_cell_tracks_kernel(
     nc = tc.nc
     with ExitStack() as ctx:
         keep = ctx.enter_context(tc.tile_pool(name="keep", bufs=1))
+        tied = ctx.enter_context(tc.tile_pool(name="tied", bufs=1))
         ring = ctx.enter_context(tc.tile_pool(name="ring", bufs=2))
         a_banks = ctx.enter_context(tc.psum_pool(name="a_banks", bufs=4))
         wide_banks = ctx.enter_context(tc.psum_pool(name="wide_banks", bufs=4))
@@ -52,12 +51,23 @@ def tile_list_locus_cell_tracks_kernel(
         bias = held([P, H // KP, PACK], F32, "bias")
         tw_all = [held([P, T], U32, "tw_all%d" % a) for a in range(2)]
         t2w_all = held([P, T], U32, "t2w_all")
-        shared32 = held([P, EARLY + PACK, KP], F32, "shared32")
+        h10_at = PACK * KP - TOK * PACK // 2
+        wa11_at = h10_at + (HALF - TOK) * PACK // 2
+        mod11_at = wa11_at + (PACK - 2) * KP
+        chain = held([P, mod11_at + PACK * HALF], F32, "chain")
+
+        def rows_at(start, width):
+            return chain[:, start : start + PACK * width].rearrange("p (j c) -> p j c", j=PACK)
+
         wa_raw = [
             [held([P, PACK, KP], F32, "wa_raw0%d" % a)[:] for a in range(2)],
-            [held([P, PACK, KP], F32, "wa_raw10")[:], shared32[:, EARLY:, :]],
+            [rows_at(0, KP), rows_at(wa11_at, KP)],
         ]
-        wt_raw = held([P, 2, PACK, N], F32, "wt_raw")
+        wt0_raw = held([P, PACK, N], F32, "wt0_raw")
+        wt_raw = [
+            [wt0_raw[:, :, :NH], wt0_raw[:, :, NH:]],
+            [tied.tile([P, PACK, NH], F32, name="wt10_raw", offset=0, align_bytes=64)[:], held([P, PACK, NH], F32, "wt11_raw")[:]],
+        ]
         g_all = [held([P, T], F32, "g_all%d" % nb) for nb in range(N // P)]
 
         for scale_tile in (t2s_all, wbs_raw, ts_all):
@@ -94,13 +104,15 @@ def tile_list_locus_cell_tracks_kernel(
         load_words(tw_all[1], tab_words[1])
         load_wa(1, 0)
         load_wa(1, 1)
-        for b in range(2):
-            load_rows(wt_raw[:, b], wt[b * KP : (b + 1) * KP, :])
+        load_rows(wt0_raw[:], wt[:KP, :])
+        for nh in range(2):
+            load_rows(wt_raw[1][nh], wt[KP:, nh * NH : (nh + 1) * NH])
         for nb in range(N // P):
             nc.sync.dma_start(out=g_all[nb][:], in_=gT[nb * P : (nb + 1) * P, :])
 
         ts = held([P, S], U8, "ts")
         t2s = held([P, S], U8, "t2s")
+        t2w = held([P, S], U32, "t2w")
         tw = [held([P, S], U32, "tw%d" % a) for a in range(2)]
         wbw = held([P, 2 * H], U8, "wbw")
         wbs = held([P, H], U8, "wbs")
@@ -108,25 +120,14 @@ def tile_list_locus_cell_tracks_kernel(
         wa_s = [held([P, 2 * KP], U8, "wa_s%d" % b) for b in range(2)]
         wt_q = held([P, 2 * N], U32, "wt_q")
         wt_s = held([P, 2 * N], U8, "wt_s")
-        h_q = [[held([P, HALF], U32, "h_q%d%d" % (hf, b)) for b in range(2)] for hf in range(2)]
+        h_q = {(hf, b): held([P, HALF], U32, "h_q%d%d" % (hf, b)) for hf, b in ((0, 0), (1, 0), (1, 1))}
         h_s = [[held([P, HALF], U8, "h_s%d%d" % (hf, b)) for b in range(2)] for hf in range(2)]
 
-        shared16 = held([P, FREE * TOK * PACK + 2 * KP * PACK], BF16, "shared16")
-        wa16 = [held([P, 2 * KP * PACK], BF16, "wa16"), shared16[:, FREE * TOK * PACK :]]
+        wa16 = [held([P, 2 * KP * PACK], BF16, "wa16_%d" % b) for b in range(2)]
         wt16 = held([P, 2 * N * PACK], BF16, "wt16")
-        h16 = {(1, 0): shared16[:, : HALF * PACK]}
-        mod = [
-            [held([P, PACK, HALF], F32, "mod")[:], shared32[:, :PACK, :]],
-            [wa_raw[0][0], wt_raw[:, :, :, :NH].rearrange("p u t c -> p t u c")],
-        ]
-
-        def mod_cols(hf, b, c0, count):
-            if (hf, b) == (1, 1):
-                if count == HALF:
-                    return mod[1][1]
-                return mod[1][1][:, :, c0 // NH, c0 % NH : c0 % NH + count]
-            return mod[hf][b][:, :, c0 : c0 + count]
-
+        h16 = {(1, 0): chain[:, h10_at : h10_at + HALF * PACK // 2].bitcast(BF16)}
+        mod = {(0, 0): held([P, PACK, HALF], F32, "mod")[:], (1, 0): wa_raw[0][0], (1, 1): rows_at(mod11_at, HALF)}
+        z = {}
         y_sb = {}
 
         def entries(lst, start, count):
@@ -141,10 +142,10 @@ def tile_list_locus_cell_tracks_kernel(
         def scalar_cast(dst, src):
             nc.scalar.activation(out=dst, in_=src, func=ACT.Copy)
 
-        def cast_wa(b, a, cast):
+        def cast_wa(b, a, *casts):
             dst = wa16[b][:, a * KP * PACK : (a + 1) * KP * PACK].rearrange("p (t m j) -> p m j t", t=PACK, j=PACK)
             src = wa_raw[b][a].rearrange("p j (m t) -> p m j t", t=PACK)
-            for pair in (slice(0, 2), slice(2, 4)):
+            for pair, cast in zip((slice(0, 2), slice(2, 4)), casts):
                 cast(dst[:, :, :, pair], src[:, :, :, pair])
 
         def cast_wt(nh):
@@ -152,7 +153,7 @@ def tile_list_locus_cell_tracks_kernel(
                 c0 = (2 * nh + b) * NH * PACK
                 scalar_cast(
                     wt16[:, c0 : c0 + NH * PACK].rearrange("p (c i j) -> p c j i", i=RUN, j=PACK),
-                    wt_raw[:, b, :, nh * NH : (nh + 1) * NH].rearrange("p j (c i) -> p c j i", i=RUN),
+                    wt_raw[b][nh].rearrange("p j (c i) -> p c j i", i=RUN),
                 )
 
         def quantize_wt(nh):
@@ -165,32 +166,41 @@ def tile_list_locus_cell_tracks_kernel(
                 in_=src.rearrange("p (b m t) -> p b t m", b=2, t=PACK),
             )
 
-        def modulation(hf, b):
-            cols = slice(hf * HALF, (hf + 1) * HALF)
-            for t in range(PACK):
-                c0 = b * KP + t * P
-                bank = wide_banks.tile([P, HALF], F32, name="wide")
-                nc.tensor.matmul_mx(
-                    out=bank[:],
-                    lhsT=wbw[:, 2 * c0 : 2 * (c0 + P)].bitcast(FP4X4),
-                    lhsT_scale=wbs[:, c0 : c0 + P],
-                    rhs=t2w[hf][:].bitcast(FP8X4),
-                    rhs_scale=t2s[:, cols],
-                    start=True,
-                    stop=True,
-                )
-                dst = mod_cols(hf, b, 0, HALF)[:, t]
-                src = bank[:].rearrange("p (u c) -> p u c", u=2) if (hf, b) == (1, 1) else bank[:]
-                nc.scalar.activation(out=dst, in_=src, func=ACT.Tanh, bias=bias[:, b, t : t + 1])
+        def argument(hf, b, t):
+            c0 = b * KP + t * P
+            z[hf, b, t] = wide_banks.tile([P, HALF], F32, name="wide")
+            nc.tensor.matmul_mx(
+                out=z[hf, b, t][:],
+                lhsT=wbw[:, 2 * c0 : 2 * (c0 + P)].bitcast(FP4X4),
+                lhsT_scale=wbs[:, c0 : c0 + P],
+                rhs=t2w[:, hf * HALF : (hf + 1) * HALF].bitcast(FP8X4),
+                rhs_scale=t2s[:, hf * HALF : (hf + 1) * HALF],
+                start=True,
+                stop=True,
+            )
 
-        def hidden(hf, b):
+        def tanh(hf, b, t, cols=slice(0, HALF)):
+            nc.scalar.activation(
+                out=mod[hf, b][:, t, cols], in_=z[hf, b, t][:, cols], func=ACT.Tanh, bias=bias[:, b, t : t + 1]
+            )
+
+        def modulation(hf, b):
+            for t in range(PACK):
+                argument(hf, b, t)
+                tanh(hf, b, t)
+
+        def quantize_wa(b, a):
+            cols = slice(a * KP, (a + 1) * KP)
+            quantize(wa_q[b][:, cols], wa_s[b][:, cols], wa16[b][:, a * KP * PACK : (a + 1) * KP * PACK])
+
+        def hidden(hf, b, banks=range(HALF // TOK)):
             if (hf, b) not in h16:
-                h16[hf, b] = ring.tile([P, HALF * PACK], BF16, name="h16", align_bytes=64)
-            for u in range(HALF // TOK):
+                h16[hf, b] = ring.tile([P, HALF * PACK], BF16, name="h16", align_bytes=64)[:]
+            for u in banks:
                 cols = slice(hf * HALF + u * TOK, hf * HALF + (u + 1) * TOK)
                 bank = a_banks.tile([P, PACK, TOK], F32, name="a")
-                for t in range(PACK):
-                    for a in range(2):
+                for a in range(2):
+                    for t in range(PACK):
                         w_cols = slice(a * KP + t * P, a * KP + (t + 1) * P)
                         nc.tensor.matmul_mx(
                             out=bank[:, t, :],
@@ -198,19 +208,19 @@ def tile_list_locus_cell_tracks_kernel(
                             lhsT_scale=wa_s[b][:, w_cols],
                             rhs=tw[a][:, cols].bitcast(FP8X4),
                             rhs_scale=ts[4 * a : P, cols],
-                            start=(a == 0),
-                            stop=(a == 1),
+                            start=(a == 0 and t == 0),
+                            stop=(a == 1 and t == PACK - 1),
                         )
                 dst = h16[hf, b][:, u * TOK * PACK : (u + 1) * TOK * PACK]
                 nc.vector.tensor_tensor(
                     out=dst.rearrange("p (c i t) -> p c t i", i=RUN, t=PACK),
                     in0=bank[:].rearrange("p t (c i) -> p c t i", i=RUN),
-                    in1=mod_cols(hf, b, u * TOK, TOK).rearrange("p t (c i) -> p c t i", i=RUN),
+                    in1=mod[hf, b][:, :, u * TOK : (u + 1) * TOK].rearrange("p t (c i) -> p c t i", i=RUN),
                     op=ALU.mult,
                 )
 
         def quantize_h(hf, b):
-            quantize(h_q[hf][b][:], h_s[hf][b][:], h16[hf, b][:])
+            quantize(h_q[hf, b][:], h_s[hf][b][:], h16[hf, b])
 
         def predict(hf, nh):
             for nb in (2 * nh, 2 * nh + 1):
@@ -222,12 +232,15 @@ def tile_list_locus_cell_tracks_kernel(
                         out=bank[:],
                         lhsT=wt_q[:, w_cols].bitcast(FP8X4),
                         lhsT_scale=wt_s[:, w_cols],
-                        rhs=h_q[hf][b][:].bitcast(FP8X4),
+                        rhs=h_q[hf, b][:].bitcast(FP8X4),
                         rhs_scale=h_s[hf][b][:],
                         start=(b == 0),
                         stop=(b == 1),
                     )
-                y_sb[hf, nb] = ring.tile([P, HALF], F32, name="y", bufs=OUT_TILES)
+                if (hf, nb) == (0, 0):
+                    y_sb[hf, nb] = held([P, HALF], F32, "y_first", tag="wt11_raw")
+                else:
+                    y_sb[hf, nb] = ring.tile([P, HALF], F32, name="y", bufs=OUT_TILES - 1)
                 nc.scalar.copy(out=y_sb[hf, nb][:], in_=bank[:])
 
         def finish(hf, nb, pieces=(HALF,)):
@@ -248,50 +261,61 @@ def tile_list_locus_cell_tracks_kernel(
 
         reorder_wb(wbw[:].bitcast(U16), wbw_raw[:].bitcast(U16))
         gather(t2s[:], t2s_all, idx2[:])
-        t2w = [held([P, HALF], U32, "t2w0")]
-        gather(t2w[0][:], t2w_all, entries(idx2, 0, HALF))
+        gather(t2w[:], t2w_all, idx2[:])
         reorder_wb(wbs[:], wbs_raw[:])
-        t2w.append(held([P, HALF], U32, "t2w1", tag="wbs_raw"))
-        gather(t2w[1][:], t2w_all, entries(idx2, HALF, HALF))
         modulation(0, 0)
 
         gather(tw[0][:], tw_all[0], idx[:])
-        cast_wa(0, 0, scalar_cast)
+        cast_wa(0, 0, scalar_cast, nc.vector.tensor_copy)
         modulation(1, 0)
         gather(ts[:], ts_all, idx[:])
-        cast_wa(0, 1, nc.vector.tensor_copy)
+        cast_wa(0, 1, nc.vector.tensor_copy, nc.vector.tensor_copy)
         quantize(wa_q[0][:], wa_s[0][:], wa16[0][:])
         for hf in range(2):
             gather(tw[1][:, hf * HALF : (hf + 1) * HALF], tw_all[1], entries(idx, hf * HALF, HALF))
 
-        hidden(0, 0)
-        cast_wa(1, 0, scalar_cast)
-        cast_wa(1, 1, scalar_cast)
+        mod[0, 1] = held([P, PACK, HALF], F32, "mod01", tag="t2w_all")[:]
         modulation(0, 1)
-        quantize_h(0, 0)
-        quantize(wa_q[1][:], wa_s[1][:], wa16[1][:])
-        hidden(1, 0)
-        quantize_h(1, 0)
-        cast_wt(0)
+        for t in (2, 3, 0, 1):
+            argument(1, 1, t)
+        tanh(1, 1, 2)
+        tanh(1, 1, 3)
 
-        hidden(0, 1)
-        modulation(1, 1)
-        quantize_h(0, 1)
-        quantize_wt(0)
-        predict(0, 0)
+        hidden(0, 0)
+        cast_wa(1, 0, scalar_cast, scalar_cast)
+        cast_wa(1, 1, scalar_cast, scalar_cast)
+        tanh(1, 1, 0)
+        tanh(1, 1, 1)
+        hidden(1, 0, (1,))
+        quantize_h(0, 0)
+        hidden(1, 0, (2,))
+        quantize_wa(1, 0)
+        hidden(1, 0, (0,))
+        quantize_wa(1, 1)
+        hidden(1, 0, (3,))
+        cast_wt(0)
+        h_q[0, 1] = tied.tile([P, HALF], U32, name="h_q01", offset=0, align_bytes=64)
+        h16[1, 1] = tied.tile([P, HALF * PACK], BF16, name="h16_11", offset=4 * HALF, align_bytes=64)[:]
         cast_wt(1)
+
+        hidden(0, 1, range(1))
+        quantize_h(1, 0)
+        hidden(0, 1, range(1, 4))
+        quantize_wt(0)
+        quantize_h(0, 1)
+        predict(0, 0)
         hidden(1, 1)
-        finish(0, 0)
-        quantize_h(1, 1)
-        predict(1, 0)
         quantize_wt(1)
         predict(0, 1)
+        quantize_h(1, 1)
+        finish(0, 0)
+        predict(1, 0)
         predict(1, 1)
 
         finish(0, 1)
+        finish(0, 2)
         finish(1, 0)
         finish(1, 1)
-        finish(0, 2)
         finish(1, 2)
         finish(0, 3)
         finish(1, 3, LAST_PIECES)

@@ -126,7 +126,7 @@ def tile_list_locus_cell_tracks_kernel(
         wa16 = [held([P, 2 * KP * PACK], BF16, "wa16_%d" % b) for b in range(2)]
         wt16 = held([P, 2 * N * PACK], BF16, "wt16")
         h16 = {(1, 0): chain[:, h10_at : h10_at + HALF * PACK // 2].bitcast(BF16)}
-        mod = {(0, 0): held([P, PACK, HALF], F32, "mod")[:], (1, 0): wa_raw[0][0], (1, 1): rows_at(mod11_at, HALF)}
+        mod = {(0, 0): held([P, PACK, HALF], F32, "mod")[:], (1, 0): wa_raw[0][0], (0, 1): wa_raw[0][1], (1, 1): rows_at(mod11_at, HALF)}
         z = {}
         y_sb = {}
 
@@ -142,11 +142,17 @@ def tile_list_locus_cell_tracks_kernel(
         def scalar_cast(dst, src):
             nc.scalar.activation(out=dst, in_=src, func=ACT.Copy)
 
+        def wa_col(b, a, t):
+            if b == 0:
+                return t // 2 * KP + a * 2 * P + t % 2 * P
+            return a * KP + t * P
+
         def cast_wa(b, a, *casts):
-            dst = wa16[b][:, a * KP * PACK : (a + 1) * KP * PACK].rearrange("p (t m j) -> p m j t", t=PACK, j=PACK)
             src = wa_raw[b][a].rearrange("p j (m t) -> p m j t", t=PACK)
-            for pair, cast in zip((slice(0, 2), slice(2, 4)), casts):
-                cast(dst[:, :, :, pair], src[:, :, :, pair])
+            for pair, cast in enumerate(casts):
+                c0 = wa_col(b, a, 2 * pair) * PACK
+                dst = wa16[b][:, c0 : c0 + 2 * P * PACK].rearrange("p (t m j) -> p m j t", t=2, j=PACK)
+                cast(dst, src[:, :, :, 2 * pair : 2 * pair + 2])
 
         def cast_wt(nh):
             for b in range(2):
@@ -166,9 +172,9 @@ def tile_list_locus_cell_tracks_kernel(
                 in_=src.rearrange("p (b m t) -> p b t m", b=2, t=PACK),
             )
 
-        def argument(hf, b, t):
+        def argument(hf, b, t, banks=wide_banks, name="wide"):
             c0 = b * KP + t * P
-            z[hf, b, t] = wide_banks.tile([P, HALF], F32, name="wide")
+            z[hf, b, t] = banks.tile([P, HALF], F32, name=name)
             nc.tensor.matmul_mx(
                 out=z[hf, b, t][:],
                 lhsT=wbw[:, 2 * c0 : 2 * (c0 + P)].bitcast(FP4X4),
@@ -184,14 +190,14 @@ def tile_list_locus_cell_tracks_kernel(
                 out=mod[hf, b][:, t, cols], in_=z[hf, b, t][:, cols], func=ACT.Tanh, bias=bias[:, b, t : t + 1]
             )
 
-        def modulation(hf, b):
+        def modulation(hf, b, banks=wide_banks, name="wide"):
             for t in range(PACK):
-                argument(hf, b, t)
+                argument(hf, b, t, banks, name)
                 tanh(hf, b, t)
 
-        def quantize_wa(b, a):
-            cols = slice(a * KP, (a + 1) * KP)
-            quantize(wa_q[b][:, cols], wa_s[b][:, cols], wa16[b][:, a * KP * PACK : (a + 1) * KP * PACK])
+        def quantize_wa(b, c0, count):
+            c1 = c0 + count
+            quantize(wa_q[b][:, c0:c1], wa_s[b][:, c0:c1], wa16[b][:, c0 * PACK : c1 * PACK])
 
         def hidden(hf, b, banks=range(HALF // TOK)):
             if (hf, b) not in h16:
@@ -201,7 +207,7 @@ def tile_list_locus_cell_tracks_kernel(
                 bank = a_banks.tile([P, PACK, TOK], F32, name="a")
                 for a in range(2):
                     for t in range(PACK):
-                        w_cols = slice(a * KP + t * P, a * KP + (t + 1) * P)
+                        w_cols = slice(wa_col(b, a, t), wa_col(b, a, t) + P)
                         nc.tensor.matmul_mx(
                             out=bank[:, t, :],
                             lhsT=wa_q[b][:, w_cols].bitcast(FP8X4),
@@ -270,16 +276,17 @@ def tile_list_locus_cell_tracks_kernel(
         modulation(1, 0)
         gather(ts[:], ts_all, idx[:])
         cast_wa(0, 1, nc.vector.tensor_copy, nc.vector.tensor_copy)
-        quantize(wa_q[0][:], wa_s[0][:], wa16[0][:])
+        quantize_wa(0, 0, KP)
+        quantize_wa(0, KP, KP)
         for hf in range(2):
             gather(tw[1][:, hf * HALF : (hf + 1) * HALF], tw_all[1], entries(idx, hf * HALF, HALF))
 
-        mod[0, 1] = held([P, PACK, HALF], F32, "mod01", tag="t2w_all")[:]
-        modulation(0, 1)
-        for t in (2, 3, 0, 1):
+        modulation(0, 1, a_banks, "a")
+        for t in (0, 1):
             argument(1, 1, t)
-        tanh(1, 1, 2)
-        tanh(1, 1, 3)
+        for t in (2, 3):
+            argument(1, 1, t, a_banks, "a")
+            tanh(1, 1, t)
 
         hidden(0, 0)
         cast_wa(1, 0, scalar_cast, scalar_cast)
@@ -289,9 +296,9 @@ def tile_list_locus_cell_tracks_kernel(
         hidden(1, 0, (1,))
         quantize_h(0, 0)
         hidden(1, 0, (2,))
-        quantize_wa(1, 0)
+        quantize_wa(1, 0, KP)
         hidden(1, 0, (0,))
-        quantize_wa(1, 1)
+        quantize_wa(1, KP, KP)
         hidden(1, 0, (3,))
         cast_wt(0)
         h_q[0, 1] = tied.tile([P, HALF], U32, name="h_q01", offset=0, align_bytes=64)

@@ -53,7 +53,7 @@ def tile_list_locus_cell_tracks_kernel(
         t2w_all = held([P, T], U32, "t2w_all")
         h10_at = PACK * KP - TOK * PACK // 2
         wa11_at = h10_at + (HALF - TOK) * PACK // 2
-        mod11_at = wa11_at + (PACK - 2) * KP
+        mod11_at = wa11_at + KP
         chain = held([P, mod11_at + PACK * HALF], F32, "chain")
 
         def rows_at(start, width):
@@ -70,17 +70,18 @@ def tile_list_locus_cell_tracks_kernel(
         ]
         g_all = [held([P, T], F32, "g_all%d" % nb) for nb in range(N // P)]
 
-        for scale_tile in (t2s_all, wbs_raw, ts_all):
+        for scale_tile in (t2s_all, ts_all, wbs_raw):
             nc.vector.memset(scale_tile[:].bitcast(I32), 0)
 
         def load_words(dst, src):
             nc.sync.dma_start(out=dst[:].bitcast(I32), in_=src.rearrange("p t i -> p (t i)").bitcast(I32))
 
-        def load_scales(dst, src, a=0):
+        def load_scales(dst, src):
+            passes = src.shape[0]
             for q in range(4):
                 nc.sync.dma_start(
-                    out=dst[32 * q + 4 * a : 32 * q + 4 * a + 4, :].bitcast(I32),
-                    in_=src[a, 4 * q : 4 * q + 4, :].bitcast(I32),
+                    out=dst[32 * q : 32 * q + 4 * passes, :].bitcast(I32),
+                    in_=src[:, 4 * q : 4 * q + 4, :].bitcast(I32),
                 )
 
         def load_rows(dst, rows):
@@ -92,14 +93,14 @@ def tile_list_locus_cell_tracks_kernel(
         nc.sync.dma_start(idx2[:], offs2)
         nc.sync.dma_start(out=wbw_raw[:].bitcast(I32), in_=wb_words[0].bitcast(I32))
         load_scales(t2s_all, tab2_scales)
+        load_rows(wa_raw[0][0][:, :, : KP // 2], wa[:KP, : KP // 2])
+        nc.sync.dma_start(idx[:], offs)
+        load_scales(ts_all, tab_scales)
         load_words(t2w_all, tab2_words[0])
+        load_rows(wa_raw[0][0][:, :, KP // 2 :], wa[:KP, KP // 2 : KP])
         nc.sync.dma_start(out=bias[:], in_=bc.rearrange("(b p t) -> p b t", p=P, t=PACK))
         load_scales(wbs_raw, wb_scales)
         load_words(tw_all[0], tab_words[0])
-        nc.sync.dma_start(idx[:], offs)
-        load_scales(ts_all, tab_scales, 0)
-        load_wa(0, 0)
-        load_scales(ts_all, tab_scales, 1)
         load_wa(0, 1)
         load_words(tw_all[1], tab_words[1])
         load_wa(1, 0)
@@ -112,7 +113,6 @@ def tile_list_locus_cell_tracks_kernel(
 
         ts = held([P, S], U8, "ts")
         t2s = held([P, S], U8, "t2s")
-        t2w = held([P, S], U32, "t2w")
         tw = [held([P, S], U32, "tw%d" % a) for a in range(2)]
         wbw = held([P, 2 * H], U8, "wbw")
         wbs = held([P, H], U8, "wbs")
@@ -154,6 +154,14 @@ def tile_list_locus_cell_tracks_kernel(
                 dst = wa16[b][:, c0 : c0 + 2 * P * PACK].rearrange("p (t m j) -> p m j t", t=2, j=PACK)
                 cast(dst, src[:, :, :, 2 * pair : 2 * pair + 2])
 
+        def cast_wa00():
+            src = wa_raw[0][0].rearrange("p j (m t) -> p m j t", t=PACK)
+            for ms in (slice(0, P // 2), slice(P // 2, P)):
+                for pair in range(2):
+                    c0 = wa_col(0, 0, 2 * pair) * PACK
+                    dst = wa16[0][:, c0 : c0 + 2 * P * PACK].rearrange("p (t m j) -> p m j t", t=2, j=PACK)
+                    scalar_cast(dst[:, ms], src[:, ms, :, 2 * pair : 2 * pair + 2])
+
         def cast_wt(nh):
             for b in range(2):
                 c0 = (2 * nh + b) * NH * PACK
@@ -179,7 +187,7 @@ def tile_list_locus_cell_tracks_kernel(
                 out=z[hf, b, t][:],
                 lhsT=wbw[:, 2 * c0 : 2 * (c0 + P)].bitcast(FP4X4),
                 lhsT_scale=wbs[:, c0 : c0 + P],
-                rhs=t2w[:, hf * HALF : (hf + 1) * HALF].bitcast(FP8X4),
+                rhs=t2w[hf][:].bitcast(FP8X4),
                 rhs_scale=t2s[:, hf * HALF : (hf + 1) * HALF],
                 start=True,
                 stop=True,
@@ -267,32 +275,35 @@ def tile_list_locus_cell_tracks_kernel(
 
         reorder_wb(wbw[:].bitcast(U16), wbw_raw[:].bitcast(U16))
         gather(t2s[:], t2s_all, idx2[:])
-        gather(t2w[:], t2w_all, idx2[:])
+        cast_wa00()
+        gather(ts[:], ts_all, idx[:])
+        t2w = [held([P, HALF], U32, "t2w0")]
+        gather(t2w[0][:], t2w_all, entries(idx2, 0, HALF))
         reorder_wb(wbs[:], wbs_raw[:])
+        t2w.append(held([P, HALF], U32, "t2w1", tag="wbs_raw"))
+        gather(t2w[1][:], t2w_all, entries(idx2, HALF, HALF))
         modulation(0, 0)
 
         gather(tw[0][:], tw_all[0], idx[:])
-        cast_wa(0, 0, scalar_cast, nc.vector.tensor_copy)
         modulation(1, 0)
-        gather(ts[:], ts_all, idx[:])
         cast_wa(0, 1, nc.vector.tensor_copy, nc.vector.tensor_copy)
         quantize_wa(0, 0, KP)
         quantize_wa(0, KP, KP)
         for hf in range(2):
             gather(tw[1][:, hf * HALF : (hf + 1) * HALF], tw_all[1], entries(idx, hf * HALF, HALF))
 
+        argument(1, 1, PACK - 1)
+        tanh(1, 1, PACK - 1)
         modulation(0, 1, a_banks, "a")
-        for t in (0, 1):
+        for t in range(PACK - 1):
             argument(1, 1, t)
-        for t in (2, 3):
-            argument(1, 1, t, a_banks, "a")
-            tanh(1, 1, t)
+
 
         hidden(0, 0)
         cast_wa(1, 0, scalar_cast, scalar_cast)
         cast_wa(1, 1, scalar_cast, scalar_cast)
-        tanh(1, 1, 0)
-        tanh(1, 1, 1)
+        for t in range(PACK - 1):
+            tanh(1, 1, t)
         hidden(1, 0, (1,))
         quantize_h(0, 0)
         hidden(1, 0, (2,))

@@ -63,10 +63,9 @@ def tile_list_locus_cell_tracks_kernel(
             [held([P, PACK, KP], F32, "wa_raw0%d" % a)[:] for a in range(2)],
             [rows_at(0, KP), rows_at(wa11_at, KP)],
         ]
-        wt0_raw = held([P, PACK, N], F32, "wt0_raw")
         wt_raw = [
-            [wt0_raw[:, :, :NH], wt0_raw[:, :, NH:]],
-            [tied.tile([P, PACK, NH], F32, name="wt10_raw", offset=0, align_bytes=64)[:], held([P, PACK, NH], F32, "wt11_raw")[:]],
+            [held([P, PACK, NH], F32, "wt0%d_raw" % nh)[:] for nh in range(2)],
+            [tied.tile([P, PACK, NH], F32, name="wt10_raw", offset=1024, align_bytes=64)[:], held([P, PACK, NH], F32, "wt11_raw")[:]],
         ]
         g_all = [held([P, T], F32, "g_all%d" % nb) for nb in range(N // P)]
 
@@ -105,10 +104,10 @@ def tile_list_locus_cell_tracks_kernel(
         load_words(tw_all[1], tab_words[1])
         load_wa(1, 0)
         load_wa(1, 1)
-        load_rows(wt0_raw[:], wt[:KP, :])
-        for nh in range(2):
-            load_rows(wt_raw[1][nh], wt[KP:, nh * NH : (nh + 1) * NH])
         for nb in range(N // P):
+            if nb < 2:
+                for b in range(2):
+                    load_rows(wt_raw[b][nb], wt[b * KP : (b + 1) * KP, nb * NH : (nb + 1) * NH])
             nc.sync.dma_start(out=g_all[nb][:], in_=gT[nb * P : (nb + 1) * P, :])
 
         ts = held([P, S], U8, "ts")
@@ -120,11 +119,11 @@ def tile_list_locus_cell_tracks_kernel(
         wa_s = [held([P, 2 * KP], U8, "wa_s%d" % b) for b in range(2)]
         wt_q = held([P, 2 * N], U32, "wt_q")
         wt_s = held([P, 2 * N], U8, "wt_s")
-        h_q = {(hf, b): held([P, HALF], U32, "h_q%d%d" % (hf, b)) for hf, b in ((0, 0), (1, 0), (1, 1))}
+        h_q = {(hf, b): held([P, HALF], U32, "h_q%d%d" % (hf, b)) for hf, b in ((0, 0), (1, 0))}
         h_s = [[held([P, HALF], U8, "h_s%d%d" % (hf, b)) for b in range(2)] for hf in range(2)]
 
         wa16 = [held([P, 2 * KP * PACK], BF16, "wa16_%d" % b) for b in range(2)]
-        wt16 = held([P, 2 * N * PACK], BF16, "wt16")
+        wt16 = held([P, 3 * NH * PACK], BF16, "wt16")
         h16 = {(1, 0): chain[:, h10_at : h10_at + HALF * PACK // 2].bitcast(BF16)}
         mod = {(0, 0): held([P, PACK, HALF], F32, "mod")[:], (1, 0): wa_raw[0][0], (0, 1): wa_raw[0][1], (1, 1): rows_at(mod11_at, HALF)}
         z = {}
@@ -162,17 +161,15 @@ def tile_list_locus_cell_tracks_kernel(
                     dst = wa16[0][:, c0 : c0 + 2 * P * PACK].rearrange("p (t m j) -> p m j t", t=2, j=PACK)
                     scalar_cast(dst[:, ms], src[:, ms, :, 2 * pair : 2 * pair + 2])
 
-        def cast_wt(nh):
-            for b in range(2):
-                c0 = (2 * nh + b) * NH * PACK
-                scalar_cast(
-                    wt16[:, c0 : c0 + NH * PACK].rearrange("p (c i j) -> p c j i", i=RUN, j=PACK),
-                    wt_raw[b][nh].rearrange("p j (c i) -> p c j i", i=RUN),
-                )
+        def cast_wt(nh, b, dst):
+            scalar_cast(
+                dst.rearrange("p (c i j) -> p c j i", i=RUN, j=PACK),
+                wt_raw[b][nh].rearrange("p j (c i) -> p c j i", i=RUN),
+            )
 
-        def quantize_wt(nh):
-            cols = slice(nh * N, (nh + 1) * N)
-            quantize(wt_q[:, cols], wt_s[:, cols], wt16[:, nh * N * PACK : (nh + 1) * N * PACK])
+        def quantize_wt(part, src):
+            cols = slice(part * NH, part * NH + src.shape[1] // PACK)
+            quantize(wt_q[:, cols], wt_s[:, cols], src)
 
         def reorder_wb(dst, src):
             nc.vector.tensor_copy(
@@ -208,7 +205,7 @@ def tile_list_locus_cell_tracks_kernel(
             quantize(wa_q[b][:, c0:c1], wa_s[b][:, c0:c1], wa16[b][:, c0 * PACK : c1 * PACK])
 
         def hidden(hf, b, banks=range(HALF // TOK)):
-            if (hf, b) not in h16:
+            if (hf, b) not in h16 and (hf, b) != (1, 1):
                 h16[hf, b] = ring.tile([P, HALF * PACK], BF16, name="h16", align_bytes=64)[:]
             for u in banks:
                 cols = slice(hf * HALF + u * TOK, hf * HALF + (u + 1) * TOK)
@@ -225,7 +222,11 @@ def tile_list_locus_cell_tracks_kernel(
                             start=(a == 0 and t == 0),
                             stop=(a == 1 and t == PACK - 1),
                         )
-                dst = h16[hf, b][:, u * TOK * PACK : (u + 1) * TOK * PACK]
+                if (hf, b) == (1, 1):
+                    first, staging = [(u0, s) for u0, s in h16_last if u0 <= u][-1]
+                    dst = staging[:, (u - first) * TOK * PACK : (u - first + 1) * TOK * PACK]
+                else:
+                    dst = h16[hf, b][:, u * TOK * PACK : (u + 1) * TOK * PACK]
                 nc.vector.tensor_tensor(
                     out=dst.rearrange("p (c i t) -> p c t i", i=RUN, t=PACK),
                     in0=bank[:].rearrange("p t (c i) -> p c t i", i=RUN),
@@ -236,8 +237,9 @@ def tile_list_locus_cell_tracks_kernel(
         def quantize_h(hf, b):
             quantize(h_q[hf, b][:], h_s[hf][b][:], h16[hf, b])
 
-        def predict(hf, nh):
-            for nb in (2 * nh, 2 * nh + 1):
+        def predict(hf, *blocks):
+            for nb in blocks:
+                nh = nb // 2
                 bank = wide_banks.tile([P, HALF], F32, name="wide")
                 for b in range(2):
                     w0 = nh * N + b * NH + nb % 2 * P
@@ -251,10 +253,7 @@ def tile_list_locus_cell_tracks_kernel(
                         start=(b == 0),
                         stop=(b == 1),
                     )
-                if (hf, nb) == (0, 0):
-                    y_sb[hf, nb] = held([P, HALF], F32, "y_first", tag="wt11_raw")
-                else:
-                    y_sb[hf, nb] = ring.tile([P, HALF], F32, name="y", bufs=OUT_TILES - 1)
+                y_sb[hf, nb] = ring.tile([P, HALF], F32, name="y", bufs=OUT_TILES)
                 nc.scalar.copy(out=y_sb[hf, nb][:], in_=bank[:])
 
         def finish(hf, nb, pieces=(HALF,)):
@@ -311,29 +310,43 @@ def tile_list_locus_cell_tracks_kernel(
         hidden(1, 0, (0,))
         quantize_wa(1, KP, KP)
         hidden(1, 0, (3,))
-        cast_wt(0)
-        h_q[0, 1] = tied.tile([P, HALF], U32, name="h_q01", offset=0, align_bytes=64)
-        h16[1, 1] = tied.tile([P, HALF * PACK], BF16, name="h16_11", offset=4 * HALF, align_bytes=64)[:]
-        cast_wt(1)
+        wt_part = [wt16[:, i * NH * PACK : (i + 1) * NH * PACK] for i in range(3)]
+        cast_wt(0, 0, wt_part[0])
+        cast_wt(0, 1, wt_part[1])
+        cast_wt(1, 0, wt_part[2])
+        h_q[0, 1] = held([P, HALF], U32, "h_q01", tag="wt00_raw")
+        h_q[1, 1] = tied.tile([P, HALF], U32, name="h_q11", offset=0, align_bytes=64)
+        h16_last = [
+            (0, tied.tile([P, TOK * PACK], BF16, name="h16_last0", offset=5120, align_bytes=64)),
+            (1, tied.tile([P, TOK * PACK], BF16, name="h16_last1", offset=2048, align_bytes=64)),
+            (2, tied.tile([P, 2 * TOK * PACK], BF16, name="h16_last2", offset=3072, align_bytes=64)),
+        ]
 
         hidden(0, 1, range(1))
         quantize_h(1, 0)
         hidden(0, 1, range(1, 4))
-        quantize_wt(0)
+        hidden(1, 1, (0,))
         quantize_h(0, 1)
-        predict(0, 0)
-        hidden(1, 1)
-        quantize_wt(1)
-        predict(0, 1)
-        quantize_h(1, 1)
+        quantize_wt(0, wt16[:, : 2 * NH * PACK])
+        predict(0, 0, 1)
+        hidden(1, 1, (1, 2, 3))
+        for first, staging in h16_last:
+            cols = slice(first * TOK, first * TOK + staging.shape[1] // PACK)
+            quantize(h_q[1, 1][:, cols], h_s[1][1][:, cols], staging[:])
+        wt16_last = tied.tile([P, NH * PACK], BF16, name="wt16_last", offset=5120, align_bytes=64)
+        cast_wt(1, 1, wt16_last[:])
+        predict(1, 0, 1)
         finish(0, 0)
-        predict(1, 0)
-        predict(1, 1)
-
+        quantize_wt(2, wt_part[2])
+        quantize_wt(3, wt16_last[:])
+        predict(0, 2)
         finish(0, 1)
-        finish(0, 2)
+        predict(1, 2)
         finish(1, 0)
+        predict(0, 3)
         finish(1, 1)
+        predict(1, 3)
+        finish(0, 2)
         finish(1, 2)
         finish(0, 3)
         finish(1, 3, LAST_PIECES)

@@ -141,6 +141,9 @@ def tile_list_locus_cell_tracks_kernel(
         def scalar_cast(dst, src):
             nc.scalar.activation(out=dst, in_=src, func=ACT.Copy)
 
+        def pool_cast(dst, src):
+            nc.gpsimd.tensor_scalar(out=dst, in0=src, scalar1=1.0, scalar2=0.0, op0=ALU.mult, op1=ALU.add)
+
         def wa_col(b, a, t):
             if b == 0:
                 return t // 2 * KP + a * 2 * P + t % 2 * P
@@ -153,13 +156,13 @@ def tile_list_locus_cell_tracks_kernel(
                 dst = wa16[b][:, c0 : c0 + 2 * P * PACK].rearrange("p (t m j) -> p m j t", t=2, j=PACK)
                 cast(dst, src[:, :, :, 2 * pair : 2 * pair + 2])
 
-        def cast_wa00():
-            src = wa_raw[0][0].rearrange("p j (m t) -> p m j t", t=PACK)
-            for ms in (slice(0, P // 2), slice(P // 2, P)):
-                for pair in range(2):
-                    c0 = wa_col(0, 0, 2 * pair) * PACK
-                    dst = wa16[0][:, c0 : c0 + 2 * P * PACK].rearrange("p (t m j) -> p m j t", t=2, j=PACK)
-                    scalar_cast(dst[:, ms], src[:, ms, :, 2 * pair : 2 * pair + 2])
+        def pool_cast_wa(b, a, parts=(slice(0, P),)):
+            src = wa_raw[b][a].rearrange("p j (m t) -> p m j t", t=PACK)
+            for ms in parts:
+                for t in range(PACK):
+                    c0 = wa_col(b, a, t) * PACK
+                    dst = wa16[b][:, c0 : c0 + P * PACK].rearrange("p (m j) -> p m j", j=PACK)
+                    pool_cast(dst[:, ms], src[:, ms, :, t])
 
         def cast_wt(nh, b, dst):
             scalar_cast(
@@ -274,7 +277,7 @@ def tile_list_locus_cell_tracks_kernel(
 
         reorder_wb(wbw[:].bitcast(U16), wbw_raw[:].bitcast(U16))
         gather(t2s[:], t2s_all, idx2[:])
-        cast_wa00()
+        pool_cast_wa(0, 0, (slice(0, P // 2), slice(P // 2, P)))
         gather(ts[:], ts_all, idx[:])
         t2w = [held([P, HALF], U32, "t2w0")]
         gather(t2w[0][:], t2w_all, entries(idx2, 0, HALF))
@@ -299,7 +302,7 @@ def tile_list_locus_cell_tracks_kernel(
 
 
         hidden(0, 0)
-        cast_wa(1, 0, scalar_cast, scalar_cast)
+        pool_cast_wa(1, 0)
         cast_wa(1, 1, scalar_cast, scalar_cast)
         for t in range(PACK - 1):
             tanh(1, 1, t)

@@ -302,7 +302,7 @@ def tile_list_locus_cell_tracks_kernel(
 
 
         hidden(0, 0)
-        pool_cast_wa(1, 0)
+        cast_wa(1, 0, scalar_cast, scalar_cast)
         cast_wa(1, 1, scalar_cast, scalar_cast)
         for t in range(PACK - 1):
             tanh(1, 1, t)

@@ -23,8 +23,8 @@ HALF = S // 2
 TOK = 128
 RUN = 2
 PER_COL = 16
-OUT_TILES = 2 * N // P
 NH = N // 2
+POOL_BANKS = 2
 LAST_PIECES = (256, 128, 128)
 
 
@@ -35,12 +35,13 @@ def tile_list_locus_cell_tracks_kernel(
     with ExitStack() as ctx:
         keep = ctx.enter_context(tc.tile_pool(name="keep", bufs=1))
         tied = ctx.enter_context(tc.tile_pool(name="tied", bufs=1))
-        ring = ctx.enter_context(tc.tile_pool(name="ring", bufs=2))
-        a_banks = ctx.enter_context(tc.psum_pool(name="a_banks", bufs=4))
-        wide_banks = ctx.enter_context(tc.psum_pool(name="wide_banks", bufs=4))
+        banks = ctx.enter_context(tc.psum_pool(name="banks", bufs=8))
 
         def held(shape, dtype, name, tag=None):
             return keep.tile(shape, dtype, name=name, tag=tag or name, align_bytes=64)
+
+        def placed(shape, dtype, name, offset):
+            return tied.tile(shape, dtype, name=name, offset=offset, align_bytes=64)
 
         idx = keep.tile([P, S // PER_COL], U16, name="idx")
         idx2 = keep.tile([P, S // PER_COL], U16, name="idx2")
@@ -51,25 +52,14 @@ def tile_list_locus_cell_tracks_kernel(
         bias = held([P, H // KP, PACK], F32, "bias")
         tw_all = [held([P, T], U32, "tw_all%d" % a) for a in range(2)]
         t2w_all = held([P, T], U32, "t2w_all")
-        h10_at = PACK * KP - TOK * PACK // 2
-        wa11_at = h10_at + (HALF - TOK) * PACK // 2
-        mod11_at = wa11_at + KP
-        chain = held([P, mod11_at + PACK * HALF], F32, "chain")
-
-        def rows_at(start, width):
-            return chain[:, start : start + PACK * width].rearrange("p (j c) -> p j c", j=PACK)
-
         wa_raw = [
-            [held([P, PACK, KP], F32, "wa_raw0%d" % a)[:] for a in range(2)],
-            [rows_at(0, KP), rows_at(wa11_at, KP)],
+            [held([P, PACK, KP], F32, "wa_raw0%d" % a) for a in range(2)],
+            [placed([P, PACK, KP], F32, "wa_raw10", 0), held([P, PACK, KP], F32, "wa_raw11")],
         ]
-        wt_raw = [
-            [held([P, PACK, NH], F32, "wt0%d_raw" % nh)[:] for nh in range(2)],
-            [tied.tile([P, PACK, NH], F32, name="wt10_raw", offset=1024, align_bytes=64)[:], held([P, PACK, NH], F32, "wt11_raw")[:]],
-        ]
+        wt_raw = [[held([P, PACK, NH], F32, "wt_raw%d%d" % (nh, b)) for b in range(2)] for nh in range(2)]
         g_all = [held([P, T], F32, "g_all%d" % nb) for nb in range(N // P)]
 
-        for scale_tile in (t2s_all, ts_all, wbs_raw):
+        for scale_tile in (t2s_all, wbs_raw, ts_all):
             nc.vector.memset(scale_tile[:].bitcast(I32), 0)
 
         def load_words(dst, src):
@@ -84,7 +74,7 @@ def tile_list_locus_cell_tracks_kernel(
                 )
 
         def load_rows(dst, rows):
-            nc.sync.dma_start(out=dst, in_=rows.rearrange("(p j) c -> p j c", j=PACK))
+            nc.sync.dma_start(out=dst[:], in_=rows.rearrange("(p j) c -> p j c", j=PACK))
 
         def load_wa(b, a):
             load_rows(wa_raw[b][a], wa[a * KP : (a + 1) * KP, b * KP : (b + 1) * KP])
@@ -92,13 +82,12 @@ def tile_list_locus_cell_tracks_kernel(
         nc.sync.dma_start(idx2[:], offs2)
         nc.sync.dma_start(out=wbw_raw[:].bitcast(I32), in_=wb_words[0].bitcast(I32))
         load_scales(t2s_all, tab2_scales)
-        load_rows(wa_raw[0][0][:, :, : KP // 2], wa[:KP, : KP // 2])
-        nc.sync.dma_start(idx[:], offs)
-        load_scales(ts_all, tab_scales)
         load_words(t2w_all, tab2_words[0])
-        load_rows(wa_raw[0][0][:, :, KP // 2 :], wa[:KP, KP // 2 : KP])
         nc.sync.dma_start(out=bias[:], in_=bc.rearrange("(b p t) -> p b t", p=P, t=PACK))
         load_scales(wbs_raw, wb_scales)
+        load_wa(0, 0)
+        nc.sync.dma_start(idx[:], offs)
+        load_scales(ts_all, tab_scales)
         load_words(tw_all[0], tab_words[0])
         load_wa(0, 1)
         load_words(tw_all[1], tab_words[1])
@@ -107,7 +96,7 @@ def tile_list_locus_cell_tracks_kernel(
         for nb in range(N // P):
             if nb < 2:
                 for b in range(2):
-                    load_rows(wt_raw[b][nb], wt[b * KP : (b + 1) * KP, nb * NH : (nb + 1) * NH])
+                    load_rows(wt_raw[nb][b], wt[b * KP : (b + 1) * KP, nb * NH : (nb + 1) * NH])
             nc.sync.dma_start(out=g_all[nb][:], in_=gT[nb * P : (nb + 1) * P, :])
 
         ts = held([P, S], U8, "ts")
@@ -115,19 +104,27 @@ def tile_list_locus_cell_tracks_kernel(
         tw = [held([P, S], U32, "tw%d" % a) for a in range(2)]
         wbw = held([P, 2 * H], U8, "wbw")
         wbs = held([P, H], U8, "wbs")
-        wa_q = [held([P, 2 * KP], U32, "wa_q%d" % b) for b in range(2)]
-        wa_s = [held([P, 2 * KP], U8, "wa_s%d" % b) for b in range(2)]
+        wa_q = {(b, 1): held([P, KP], U32, "wa_q%d1" % b) for b in range(2)}
+        wa_q[0, 0] = placed([P, KP], U32, "wa_q00", 8192)
+        wa_q[1, 0] = placed([P, KP], U32, "wa_q10", 11264)
+        wa_s = {(b, i): held([P, KP], U8, "wa_s%d%d" % (b, i)) for b, i in ((0, 0), (0, 1), (1, 1))}
         wt_q = held([P, 2 * N], U32, "wt_q")
-        wt_s = held([P, 2 * N], U8, "wt_s")
-        h_q = {(hf, b): held([P, HALF], U32, "h_q%d%d" % (hf, b)) for hf, b in ((0, 0), (1, 0))}
         h_s = [[held([P, HALF], U8, "h_s%d%d" % (hf, b)) for b in range(2)] for hf in range(2)]
+        h_q = {(1, 1): held([P, HALF], U32, "h_q11")}
 
-        wa16 = [held([P, 2 * KP * PACK], BF16, "wa16_%d" % b) for b in range(2)]
-        wt16 = held([P, 3 * NH * PACK], BF16, "wt16")
-        h16 = {(1, 0): chain[:, h10_at : h10_at + HALF * PACK // 2].bitcast(BF16)}
-        mod = {(0, 0): held([P, PACK, HALF], F32, "mod")[:], (1, 0): wa_raw[0][0], (0, 1): wa_raw[0][1], (1, 1): rows_at(mod11_at, HALF)}
-        z = {}
-        y_sb = {}
+        pair_w = 2 * P * PACK
+        wa16_0 = held([P, 4 * pair_w], BF16, "wa16_0")
+        wa16 = {(0, a): [wa16_0[:, (2 * pair + a) * pair_w : (2 * pair + a + 1) * pair_w] for pair in range(2)] for a in range(2)}
+        wa16_10 = held([P, 2 * pair_w], BF16, "wa16_10")
+        wa16[1, 0] = [wa16_10[:, pair * pair_w : (pair + 1) * pair_w] for pair in range(2)]
+        wt16 = {(nh, b): held([P, NH * PACK], BF16, "wt16_%d%d" % (nh, b)) for nh, b in ((0, 0), (1, 0), (1, 1))}
+        bank_w = TOK * PACK
+        h16 = {}
+        for hf, b, count in ((0, 0, 4), (1, 0, 3), (0, 1, 4), (1, 1, 4)):
+            staging = held([P, count * bank_w], BF16, "h16_%d%d" % (hf, b))
+            h16[hf, b, 0] = staging[:]
+        mod = [[held([P, PACK, HALF], F32, "mod%d%d" % (hf, b)) for b in range(2)] for hf in range(2)]
+        a_sb = {(b, u): held([P, TOK, PACK], F32, "a_sb%d%d" % (b, u)) for b in range(2) for u in range(POOL_BANKS)}
 
         def entries(lst, start, count):
             return lst[:, start // PER_COL : (start + count) // PER_COL]
@@ -135,44 +132,49 @@ def tile_list_locus_cell_tracks_kernel(
         def gather(dst, table, lst):
             nc.vector.tensor_copy(dst, table[:].indirect(lst))
 
+        def gather_halves(dst, table, lst):
+            for hf in range(2):
+                gather(dst[:, hf * HALF : (hf + 1) * HALF], table, entries(lst, hf * HALF, HALF))
+
         def quantize(codes, scales, src):
             nc.vector.quantize_mx(out=codes.bitcast(FP8X4), scales=scales, in_=src)
 
         def scalar_cast(dst, src):
             nc.scalar.activation(out=dst, in_=src, func=ACT.Copy)
 
-        def pool_cast(dst, src):
-            nc.gpsimd.tensor_scalar(out=dst, in0=src, scalar1=1.0, scalar2=0.0, op0=ALU.mult, op1=ALU.add)
+        def cast_wa(b, a, *casts):
+            src = wa_raw[b][a][:].rearrange("p j (m t) -> p m j t", t=PACK)
+            for pair, cast in enumerate(casts):
+                dst = wa16[b, a][pair].rearrange("p (t m j) -> p m j t", t=2, j=PACK)
+                cast(dst, src[:, :, :, 2 * pair : 2 * pair + 2])
+
+        def pool_cast_wa(b, a):
+            src = wa_raw[b][a][:].rearrange("p j (m t) -> p m j t", t=PACK)
+            for t in range(PACK):
+                dst = wa16[b, a][t // 2].rearrange("p (t m j) -> p m j t", t=2, j=PACK)
+                nc.gpsimd.tensor_scalar(
+                    out=dst[:, :, :, t % 2], in0=src[:, :, :, t], scalar1=1.0, scalar2=0.0, op0=ALU.mult, op1=ALU.add
+                )
 
         def wa_col(b, a, t):
             if b == 0:
-                return t // 2 * KP + a * 2 * P + t % 2 * P
-            return a * KP + t * P
+                return t // 2, a * 2 * P + t % 2 * P
+            return a, t * P
 
-        def cast_wa(b, a, *casts):
-            src = wa_raw[b][a].rearrange("p j (m t) -> p m j t", t=PACK)
-            for pair, cast in enumerate(casts):
-                c0 = wa_col(b, a, 2 * pair) * PACK
-                dst = wa16[b][:, c0 : c0 + 2 * P * PACK].rearrange("p (t m j) -> p m j t", t=2, j=PACK)
-                cast(dst, src[:, :, :, 2 * pair : 2 * pair + 2])
+        def quantize_wa(b, i, src, c0=0):
+            cols = slice(c0, c0 + src.shape[1] // PACK)
+            quantize(wa_q[b, i][:, cols], wa_s[b, i][:, cols], src)
 
-        def pool_cast_wa(b, a, parts=(slice(0, P),)):
-            src = wa_raw[b][a].rearrange("p j (m t) -> p m j t", t=PACK)
-            for ms in parts:
-                for t in range(PACK):
-                    c0 = wa_col(b, a, t) * PACK
-                    dst = wa16[b][:, c0 : c0 + P * PACK].rearrange("p (m j) -> p m j", j=PACK)
-                    pool_cast(dst[:, ms], src[:, ms, :, t])
-
-        def cast_wt(nh, b, dst):
+        def cast_wt(nh, b):
             scalar_cast(
-                dst.rearrange("p (c i j) -> p c j i", i=RUN, j=PACK),
-                wt_raw[b][nh].rearrange("p j (c i) -> p c j i", i=RUN),
+                wt16[nh, b][:].rearrange("p (c i j) -> p c j i", i=RUN, j=PACK),
+                wt_raw[nh][b][:].rearrange("p j (c i) -> p c j i", i=RUN),
             )
 
-        def quantize_wt(part, src):
-            cols = slice(part * NH, part * NH + src.shape[1] // PACK)
-            quantize(wt_q[:, cols], wt_s[:, cols], src)
+        def quantize_wt(nh):
+            for b in range(2):
+                cols = slice(nh * N + b * NH, nh * N + (b + 1) * NH)
+                quantize(wt_q[:, cols], wt_s[:, cols], wt16[nh, b][:])
 
         def reorder_wb(dst, src):
             nc.vector.tensor_copy(
@@ -180,176 +182,156 @@ def tile_list_locus_cell_tracks_kernel(
                 in_=src.rearrange("p (b m t) -> p b t m", b=2, t=PACK),
             )
 
-        def argument(hf, b, t, banks=wide_banks, name="wide"):
-            c0 = b * KP + t * P
-            z[hf, b, t] = banks.tile([P, HALF], F32, name=name)
-            nc.tensor.matmul_mx(
-                out=z[hf, b, t][:],
-                lhsT=wbw[:, 2 * c0 : 2 * (c0 + P)].bitcast(FP4X4),
-                lhsT_scale=wbs[:, c0 : c0 + P],
-                rhs=t2w[hf][:].bitcast(FP8X4),
-                rhs_scale=t2s[:, hf * HALF : (hf + 1) * HALF],
-                start=True,
-                stop=True,
-            )
-
-        def tanh(hf, b, t, cols=slice(0, HALF)):
-            nc.scalar.activation(
-                out=mod[hf, b][:, t, cols], in_=z[hf, b, t][:, cols], func=ACT.Tanh, bias=bias[:, b, t : t + 1]
-            )
-
-        def modulation(hf, b, banks=wide_banks, name="wide"):
+        def modulation(hf, b):
+            cols = slice(hf * HALF, (hf + 1) * HALF)
             for t in range(PACK):
-                argument(hf, b, t, banks, name)
-                tanh(hf, b, t)
+                c0 = b * KP + t * P
+                z = banks.tile([P, HALF], F32, name="bank")
+                nc.tensor.matmul_mx(
+                    out=z[:],
+                    lhsT=wbw[:, 2 * c0 : 2 * (c0 + P)].bitcast(FP4X4),
+                    lhsT_scale=wbs[:, c0 : c0 + P],
+                    rhs=t2w[hf][:].bitcast(FP8X4),
+                    rhs_scale=t2s[:, cols],
+                    start=True,
+                    stop=True,
+                )
+                nc.scalar.activation(out=mod[hf][b][:, t, :], in_=z[:], func=ACT.Tanh, bias=bias[:, b, t : t + 1])
 
-        def quantize_wa(b, c0, count):
-            c1 = c0 + count
-            quantize(wa_q[b][:, c0:c1], wa_s[b][:, c0:c1], wa16[b][:, c0 * PACK : c1 * PACK])
+        def hidden(hf, b, u):
+            cols = slice(hf * HALF + u * TOK, hf * HALF + (u + 1) * TOK)
+            bank = banks.tile([P, HALF], F32, name="bank")
+            sums = bank[:].rearrange("p (t j) -> p t j", t=PACK)
+            passes = (hf, 1 - hf)
+            for a in passes:
+                for t in range(PACK):
+                    i, c0 = wa_col(b, a, t)
+                    nc.tensor.matmul_mx(
+                        out=sums[:, t, :],
+                        lhsT=wa_q[b, i][:, c0 : c0 + P].bitcast(FP8X4),
+                        lhsT_scale=wa_s[b, i][:, c0 : c0 + P],
+                        rhs=tw[a][:, cols].bitcast(FP8X4),
+                        rhs_scale=ts[4 * a : P, cols],
+                        start=(a == passes[0] and t == 0),
+                        stop=(a == passes[1] and t == PACK - 1),
+                    )
+            return sums
 
-        def hidden(hf, b, banks=range(HALF // TOK)):
-            if (hf, b) not in h16 and (hf, b) != (1, 1):
-                h16[hf, b] = ring.tile([P, HALF * PACK], BF16, name="h16", align_bytes=64)[:]
-            for u in banks:
-                cols = slice(hf * HALF + u * TOK, hf * HALF + (u + 1) * TOK)
-                bank = a_banks.tile([P, PACK, TOK], F32, name="a")
-                for a in range(2):
-                    for t in range(PACK):
-                        w_cols = slice(wa_col(b, a, t), wa_col(b, a, t) + P)
-                        nc.tensor.matmul_mx(
-                            out=bank[:, t, :],
-                            lhsT=wa_q[b][:, w_cols].bitcast(FP8X4),
-                            lhsT_scale=wa_s[b][:, w_cols],
-                            rhs=tw[a][:, cols].bitcast(FP8X4),
-                            rhs_scale=ts[4 * a : P, cols],
-                            start=(a == 0 and t == 0),
-                            stop=(a == 1 and t == PACK - 1),
-                        )
-                if (hf, b) == (1, 1):
-                    first, staging = [(u0, s) for u0, s in h16_last if u0 <= u][-1]
-                    dst = staging[:, (u - first) * TOK * PACK : (u - first + 1) * TOK * PACK]
-                else:
-                    dst = h16[hf, b][:, u * TOK * PACK : (u + 1) * TOK * PACK]
+        def product(hf, b, u, sums):
+            first = u if (hf, b, u) in h16 else 0
+            dst = h16[hf, b, first][:, (u - first) * bank_w : (u - first + 1) * bank_w]
+            factor = mod[hf][b][:, :, u * TOK : (u + 1) * TOK]
+            if (b, u) in a_sb and hf == 0:
+                nc.scalar.copy(out=a_sb[b, u][:], in_=sums.rearrange("p t j -> p j t"))
+                nc.gpsimd.tensor_tensor(
+                    out=dst.rearrange("p (j t) -> p j t", t=PACK),
+                    in0=a_sb[b, u][:],
+                    in1=factor.rearrange("p t j -> p j t"),
+                    op=ALU.mult,
+                )
+            else:
                 nc.vector.tensor_tensor(
                     out=dst.rearrange("p (c i t) -> p c t i", i=RUN, t=PACK),
-                    in0=bank[:].rearrange("p t (c i) -> p c t i", i=RUN),
-                    in1=mod[hf, b][:, :, u * TOK : (u + 1) * TOK].rearrange("p t (c i) -> p c t i", i=RUN),
+                    in0=sums.rearrange("p t (c i) -> p c t i", i=RUN),
+                    in1=factor.rearrange("p t (c i) -> p c t i", i=RUN),
                     op=ALU.mult,
                 )
 
-        def quantize_h(hf, b):
-            quantize(h_q[hf, b][:], h_s[hf][b][:], h16[hf, b])
+        def hidden_group(b, count=2 * HALF // TOK):
+            for i in range(count):
+                product(i // 4, b, i % 4, hidden(i // 4, b, i % 4))
 
-        def predict(hf, *blocks):
-            for nb in blocks:
-                nh = nb // 2
-                bank = wide_banks.tile([P, HALF], F32, name="wide")
-                for b in range(2):
-                    w0 = nh * N + b * NH + nb % 2 * P
-                    w_cols = slice(w0, w0 + P)
-                    nc.tensor.matmul_mx(
-                        out=bank[:],
-                        lhsT=wt_q[:, w_cols].bitcast(FP8X4),
-                        lhsT_scale=wt_s[:, w_cols],
-                        rhs=h_q[hf, b][:].bitcast(FP8X4),
-                        rhs_scale=h_s[hf][b][:],
-                        start=(b == 0),
-                        stop=(b == 1),
-                    )
-                y_sb[hf, nb] = ring.tile([P, HALF], F32, name="y", bufs=OUT_TILES)
-                nc.scalar.copy(out=y_sb[hf, nb][:], in_=bank[:])
+        def quantize_h(hf, b):
+            for first in range(HALF // TOK):
+                if (hf, b, first) in h16:
+                    src = h16[hf, b, first]
+                    cols = slice(first * TOK, first * TOK + src.shape[1] // PACK)
+                    quantize(h_q[hf, b][:, cols], h_s[hf][b][:, cols], src)
+
+        def predict(hf, nb):
+            bank = banks.tile([P, HALF], F32, name="bank")
+            for b in range(2):
+                w0 = nb // 2 * N + b * NH + nb % 2 * P
+                nc.tensor.matmul_mx(
+                    out=bank[:],
+                    lhsT=wt_q[:, w0 : w0 + P].bitcast(FP8X4),
+                    lhsT_scale=wt_s[:, w0 : w0 + P],
+                    rhs=h_q[hf, b][:].bitcast(FP8X4),
+                    rhs_scale=h_s[hf][b][:],
+                    start=(b == 0),
+                    stop=(b == 1),
+                )
+            nc.scalar.copy(out=y_sb[hf][:, nb, :], in_=bank[:])
 
         def finish(hf, nb, pieces=(HALF,)):
-            diff = ring.tile([P, HALF], F32, name="diff", bufs=OUT_TILES)
             c0 = 0
             for width in pieces:
-                cols = slice(c0, c0 + width)
+                piece = diff[hf][:, nb, c0 : c0 + width]
                 s0 = hf * HALF + c0
                 nc.vector.tensor_tensor(
-                    out=diff[:, cols],
+                    out=piece,
                     in0=g_all[nb][:].indirect(entries(idx, s0, width)),
-                    in1=y_sb[hf, nb][:, cols],
+                    in1=y_sb[hf][:, nb, c0 : c0 + width],
                     op=ALU.subtract,
                 )
-                nc.scalar.activation(out=diff[:, cols], in_=diff[:, cols], func=ACT.Abs)
-                nc.sync.dma_start(out=out[nb * P : (nb + 1) * P, s0 : s0 + width], in_=diff[:, cols])
+                nc.scalar.activation(out=piece, in_=piece, func=ACT.Abs)
+                nc.sync.dma_start(out=out[nb * P : (nb + 1) * P, s0 : s0 + width], in_=piece)
                 c0 = c0 + width
 
         reorder_wb(wbw[:].bitcast(U16), wbw_raw[:].bitcast(U16))
         gather(t2s[:], t2s_all, idx2[:])
-        pool_cast_wa(0, 0, (slice(0, P // 2), slice(P // 2, P)))
-        gather(ts[:], ts_all, idx[:])
         t2w = [held([P, HALF], U32, "t2w0")]
         gather(t2w[0][:], t2w_all, entries(idx2, 0, HALF))
         reorder_wb(wbs[:], wbs_raw[:])
         t2w.append(held([P, HALF], U32, "t2w1", tag="wbs_raw"))
         gather(t2w[1][:], t2w_all, entries(idx2, HALF, HALF))
-        modulation(0, 0)
+        for b in range(2):
+            for hf in range(2):
+                modulation(hf, b)
 
+        pool_cast_wa(0, 0)
+        gather(ts[:], ts_all, idx[:])
         gather(tw[0][:], tw_all[0], idx[:])
-        modulation(1, 0)
         cast_wa(0, 1, nc.vector.tensor_copy, nc.vector.tensor_copy)
-        quantize_wa(0, 0, KP)
-        quantize_wa(0, KP, KP)
-        for hf in range(2):
-            gather(tw[1][:, hf * HALF : (hf + 1) * HALF], tw_all[1], entries(idx, hf * HALF, HALF))
+        for pair in range(2):
+            quantize_wa(0, pair, wa16_0[:, 2 * pair * pair_w : 2 * (pair + 1) * pair_w])
+        gather_halves(tw[1], tw_all[1], idx)
 
-        argument(1, 1, PACK - 1)
-        tanh(1, 1, PACK - 1)
-        modulation(0, 1, a_banks, "a")
-        for t in range(PACK - 1):
-            argument(1, 1, t)
-
-
-        hidden(0, 0)
+        hidden_group(0, 7)
+        last_sums = hidden(1, 0, 3)
         cast_wa(1, 0, scalar_cast, scalar_cast)
-        cast_wa(1, 1, scalar_cast, scalar_cast)
-        for t in range(PACK - 1):
-            tanh(1, 1, t)
-        hidden(1, 0, (1,))
+        wa_s[1, 0] = held([P, KP], U8, "wa_s10", tag="wa_s00")
+        wa16[1, 1] = [held([P, pair_w], BF16, "wa16_110")[:], placed([P, pair_w], BF16, "wa16_111", 7168)[:]]
+        quantize_wa(1, 0, wa16_10[:])
+        cast_wa(1, 1, scalar_cast, nc.vector.tensor_copy)
+        for pair in range(2):
+            quantize_wa(1, 1, wa16[1, 1][pair], pair * 2 * P)
+        h_q[0, 0] = held([P, HALF], U32, "h_q00", tag="wa_raw11")
         quantize_h(0, 0)
-        hidden(1, 0, (2,))
-        quantize_wa(1, 0, KP)
-        hidden(1, 0, (0,))
-        quantize_wa(1, KP, KP)
-        hidden(1, 0, (3,))
-        wt_part = [wt16[:, i * NH * PACK : (i + 1) * NH * PACK] for i in range(3)]
-        cast_wt(0, 0, wt_part[0])
-        cast_wt(0, 1, wt_part[1])
-        cast_wt(1, 0, wt_part[2])
-        h_q[0, 1] = held([P, HALF], U32, "h_q01", tag="wt00_raw")
-        h_q[1, 1] = tied.tile([P, HALF], U32, name="h_q11", offset=0, align_bytes=64)
-        h16_last = [
-            (0, tied.tile([P, TOK * PACK], BF16, name="h16_last0", offset=5120, align_bytes=64)),
-            (1, tied.tile([P, TOK * PACK], BF16, name="h16_last1", offset=2048, align_bytes=64)),
-            (2, tied.tile([P, 2 * TOK * PACK], BF16, name="h16_last2", offset=3072, align_bytes=64)),
-        ]
+        h16[1, 0, 3] = placed([P, bank_w], BF16, "h16_103", 7168)[:]
+        product(1, 0, 3, last_sums)
+        cast_wt(0, 0)
 
-        hidden(0, 1, range(1))
-        quantize_h(1, 0)
-        hidden(0, 1, range(1, 4))
-        hidden(1, 1, (0,))
+        hidden_group(1)
+        wt16[0, 1] = held([P, NH * PACK], BF16, "wt16_01", tag="mod10")
+        cast_wt(0, 1)
+        for b in range(2):
+            cast_wt(1, b)
+        h_q[0, 1] = placed([P, HALF], U32, "h_q01", 10240)
+        wt_s = held([P, 2 * N], U8, "wt_s", tag="wa_s00")
+        h_q[1, 0] = placed([P, HALF], U32, "h_q10", 12288)
+        quantize_wt(0)
         quantize_h(0, 1)
-        quantize_wt(0, wt16[:, : 2 * NH * PACK])
-        predict(0, 0, 1)
-        hidden(1, 1, (1, 2, 3))
-        for first, staging in h16_last:
-            cols = slice(first * TOK, first * TOK + staging.shape[1] // PACK)
-            quantize(h_q[1, 1][:, cols], h_s[1][1][:, cols], staging[:])
-        wt16_last = tied.tile([P, NH * PACK], BF16, name="wt16_last", offset=5120, align_bytes=64)
-        cast_wt(1, 1, wt16_last[:])
-        predict(1, 0, 1)
-        finish(0, 0)
-        quantize_wt(2, wt_part[2])
-        quantize_wt(3, wt16_last[:])
-        predict(0, 2)
-        finish(0, 1)
-        predict(1, 2)
-        finish(1, 0)
-        predict(0, 3)
-        finish(1, 1)
-        predict(1, 3)
-        finish(0, 2)
-        finish(1, 2)
-        finish(0, 3)
-        finish(1, 3, LAST_PIECES)
+        quantize_h(1, 0)
+        quantize_h(1, 1)
+        quantize_wt(1)
+
+        y_sb = [held([P, N // P, HALF], F32, "y%d" % hf, tag="wa_raw0%d" % hf) for hf in range(2)]
+        diff = [held([P, N // P, HALF], F32, "diff%d" % hf, tag="mod%d0" % hf) for hf in range(2)]
+        tiles = [(hf, nb) for nh in range(2) for hf in range(2) for nb in (2 * nh, 2 * nh + 1)]
+        tiles[5], tiles[6] = tiles[6], tiles[5]
+        for hf, nb in tiles:
+            predict(hf, nb)
+        for hf, nb in tiles[:-1]:
+            finish(hf, nb)
+        finish(*tiles[-1], LAST_PIECES)

@@ -124,7 +124,7 @@ def tile_list_locus_cell_tracks_kernel(
             staging = held([P, count * bank_w], BF16, "h16_%d%d" % (hf, b))
             h16[hf, b, 0] = staging[:]
         mod = [[held([P, PACK, HALF], F32, "mod%d%d" % (hf, b)) for b in range(2)] for hf in range(2)]
-        a_sb = {(b, u): held([P, TOK, PACK], F32, "a_sb%d%d" % (b, u)) for b in range(2) for u in range(POOL_BANKS)}
+        a_sb = {(b, u): held([P, TOK * PACK], F32, "a_sb%d%d" % (b, u)) for b in range(2) for u in range(POOL_BANKS)}
 
         def entries(lst, start, count):
             return lst[:, start // PER_COL : (start + count) // PER_COL]
@@ -222,11 +222,12 @@ def tile_list_locus_cell_tracks_kernel(
             dst = h16[hf, b, first][:, (u - first) * bank_w : (u - first + 1) * bank_w]
             factor = mod[hf][b][:, :, u * TOK : (u + 1) * TOK]
             if (b, u) in a_sb and hf == 0:
-                nc.scalar.copy(out=a_sb[b, u][:], in_=sums.rearrange("p t j -> p j t"))
+                copied = a_sb[b, u][:].rearrange("p (c t i) -> p c t i", t=PACK, i=RUN)
+                nc.scalar.copy(out=copied, in_=sums.rearrange("p t (c i) -> p c t i", i=RUN))
                 nc.gpsimd.tensor_tensor(
-                    out=dst.rearrange("p (j t) -> p j t", t=PACK),
-                    in0=a_sb[b, u][:],
-                    in1=factor.rearrange("p t j -> p j t"),
+                    out=dst.rearrange("p (c i t) -> p c t i", i=RUN, t=PACK),
+                    in0=copied,
+                    in1=factor.rearrange("p t (c i) -> p c t i", i=RUN),
                     op=ALU.mult,
                 )
             else:

@@ -24,7 +24,8 @@ TOK = 128
 RUN = 2
 PER_COL = 16
 NH = N // 2
-POOL_BANKS = 2
+POOL_SHARE = {(0, 0, 0): TOK, (0, 0, 1): TOK // 2, (1, 0, 3): TOK, (0, 1, 1): TOK}
+A_BANKS = (2, 3, 4, 5, 6, 0, 1, 7)
 LAST_PIECES = (256, 128, 128)
 
 
@@ -35,7 +36,10 @@ def tile_list_locus_cell_tracks_kernel(
     with ExitStack() as ctx:
         keep = ctx.enter_context(tc.tile_pool(name="keep", bufs=1))
         tied = ctx.enter_context(tc.tile_pool(name="tied", bufs=1))
-        banks = ctx.enter_context(tc.psum_pool(name="banks", bufs=8))
+        banks = ctx.enter_context(tc.psum_pool(name="banks", bufs=1))
+
+        def psum_bank(number):
+            return banks.tile([P, HALF], F32, name="bank%d" % number)
 
         def held(shape, dtype, name, tag=None):
             return keep.tile(shape, dtype, name=name, tag=tag or name, align_bytes=64)
@@ -101,7 +105,7 @@ def tile_list_locus_cell_tracks_kernel(
 
         ts = held([P, S], U8, "ts")
         t2s = held([P, S], U8, "t2s")
-        tw = [held([P, S], U32, "tw%d" % a) for a in range(2)]
+        tw = {(a, hf): held([P, HALF], U32, "tw%d%d" % (a, hf)) for a in range(2) for hf in range(2)}
         wbw = held([P, 2 * H], U8, "wbw")
         wbs = held([P, H], U8, "wbs")
         wa_q = {(b, 1): held([P, KP], U32, "wa_q%d1" % b) for b in range(2)}
@@ -117,14 +121,15 @@ def tile_list_locus_cell_tracks_kernel(
         wa16 = {(0, a): [wa16_0[:, (2 * pair + a) * pair_w : (2 * pair + a + 1) * pair_w] for pair in range(2)] for a in range(2)}
         wa16_10 = held([P, 2 * pair_w], BF16, "wa16_10")
         wa16[1, 0] = [wa16_10[:, pair * pair_w : (pair + 1) * pair_w] for pair in range(2)]
-        wt16 = {(nh, b): held([P, NH * PACK], BF16, "wt16_%d%d" % (nh, b)) for nh, b in ((0, 0), (1, 0), (1, 1))}
+        wt16 = {(nh, b): held([P, NH * PACK], BF16, "wt16_%d%d" % (nh, b)) for nh, b in ((0, 0), (1, 1))}
         bank_w = TOK * PACK
         h16 = {}
         for hf, b, count in ((0, 0, 4), (1, 0, 3), (0, 1, 4), (1, 1, 4)):
             staging = held([P, count * bank_w], BF16, "h16_%d%d" % (hf, b))
             h16[hf, b, 0] = staging[:]
         mod = [[held([P, PACK, HALF], F32, "mod%d%d" % (hf, b)) for b in range(2)] for hf in range(2)]
-        a_sb = {(b, u): held([P, TOK * PACK], F32, "a_sb%d%d" % (b, u)) for b in range(2) for u in range(POOL_BANKS)}
+        a_sb = {key: held([P, n * PACK], F32, "a_sb%d%d%d" % key) for key, n in POOL_SHARE.items() if key != (1, 0, 3)}
+        a_sb[1, 0, 3] = placed([P, TOK * PACK], F32, "a_sb103", 17408)
 
         def entries(lst, start, count):
             return lst[:, start // PER_COL : (start + count) // PER_COL]
@@ -132,9 +137,8 @@ def tile_list_locus_cell_tracks_kernel(
         def gather(dst, table, lst):
             nc.vector.tensor_copy(dst, table[:].indirect(lst))
 
-        def gather_halves(dst, table, lst):
-            for hf in range(2):
-                gather(dst[:, hf * HALF : (hf + 1) * HALF], table, entries(lst, hf * HALF, HALF))
+        def gather_tw(a, hf):
+            gather(tw[a, hf][:], tw_all[a], entries(idx, hf * HALF, HALF))
 
         def quantize(codes, scales, src):
             nc.vector.quantize_mx(out=codes.bitcast(FP8X4), scales=scales, in_=src)
@@ -182,11 +186,11 @@ def tile_list_locus_cell_tracks_kernel(
                 in_=src.rearrange("p (b m t) -> p b t m", b=2, t=PACK),
             )
 
-        def modulation(hf, b):
+        def modulation(hf, b, slices=range(PACK), late=False):
             cols = slice(hf * HALF, (hf + 1) * HALF)
-            for t in range(PACK):
+            for t in slices:
                 c0 = b * KP + t * P
-                z = banks.tile([P, HALF], F32, name="bank")
+                z = psum_bank(t % 2 if late else 5 + (8 * b + 4 * hf + t) % 3)
                 nc.tensor.matmul_mx(
                     out=z[:],
                     lhsT=wbw[:, 2 * c0 : 2 * (c0 + P)].bitcast(FP4X4),
@@ -200,7 +204,7 @@ def tile_list_locus_cell_tracks_kernel(
 
         def hidden(hf, b, u):
             cols = slice(hf * HALF + u * TOK, hf * HALF + (u + 1) * TOK)
-            bank = banks.tile([P, HALF], F32, name="bank")
+            bank = psum_bank((4 * hf + u, A_BANKS[4 * hf + u])[b])
             sums = bank[:].rearrange("p (t j) -> p t j", t=PACK)
             passes = (hf, 1 - hf)
             for a in passes:
@@ -210,7 +214,7 @@ def tile_list_locus_cell_tracks_kernel(
                         out=sums[:, t, :],
                         lhsT=wa_q[b, i][:, c0 : c0 + P].bitcast(FP8X4),
                         lhsT_scale=wa_s[b, i][:, c0 : c0 + P],
-                        rhs=tw[a][:, cols].bitcast(FP8X4),
+                        rhs=tw[a, hf][:, u * TOK : (u + 1) * TOK].bitcast(FP8X4),
                         rhs_scale=ts[4 * a : P, cols],
                         start=(a == passes[0] and t == 0),
                         stop=(a == passes[1] and t == PACK - 1),
@@ -221,22 +225,16 @@ def tile_list_locus_cell_tracks_kernel(
             first = u if (hf, b, u) in h16 else 0
             dst = h16[hf, b, first][:, (u - first) * bank_w : (u - first + 1) * bank_w]
             factor = mod[hf][b][:, :, u * TOK : (u + 1) * TOK]
-            if (b, u) in a_sb and hf == 0:
-                copied = a_sb[b, u][:].rearrange("p (c t i) -> p c t i", t=PACK, i=RUN)
-                nc.scalar.copy(out=copied, in_=sums.rearrange("p t (c i) -> p c t i", i=RUN))
-                nc.gpsimd.tensor_tensor(
-                    out=dst.rearrange("p (c i t) -> p c t i", i=RUN, t=PACK),
-                    in0=copied,
-                    in1=factor.rearrange("p t (c i) -> p c t i", i=RUN),
-                    op=ALU.mult,
-                )
-            else:
-                nc.vector.tensor_tensor(
-                    out=dst.rearrange("p (c i t) -> p c t i", i=RUN, t=PACK),
-                    in0=sums.rearrange("p t (c i) -> p c t i", i=RUN),
-                    in1=factor.rearrange("p t (c i) -> p c t i", i=RUN),
-                    op=ALU.mult,
-                )
+            dst = dst.rearrange("p (c i t) -> p c t i", i=RUN, t=PACK)
+            sums = sums.rearrange("p t (c i) -> p c t i", i=RUN)
+            factor = factor.rearrange("p t (c i) -> p c t i", i=RUN)
+            split = POOL_SHARE.get((hf, b, u), 0) // RUN
+            if split > 0:
+                copied = a_sb[hf, b, u][:].rearrange("p (c t i) -> p c t i", t=PACK, i=RUN)
+                nc.scalar.copy(out=copied, in_=sums[:, :split])
+                nc.gpsimd.tensor_tensor(out=dst[:, :split], in0=copied, in1=factor[:, :split], op=ALU.mult)
+            if split < TOK // RUN:
+                nc.vector.tensor_tensor(out=dst[:, split:], in0=sums[:, split:], in1=factor[:, split:], op=ALU.mult)
 
         def hidden_group(b, count=2 * HALF // TOK):
             for i in range(count):
@@ -250,7 +248,7 @@ def tile_list_locus_cell_tracks_kernel(
                     quantize(h_q[hf, b][:, cols], h_s[hf][b][:, cols], src)
 
         def predict(hf, nb):
-            bank = banks.tile([P, HALF], F32, name="bank")
+            bank = psum_bank(A_BANKS[tiles.index((hf, nb))])
             for b in range(2):
                 w0 = nb // 2 * N + b * NH + nb % 2 * P
                 nc.tensor.matmul_mx(
@@ -286,17 +284,20 @@ def tile_list_locus_cell_tracks_kernel(
         reorder_wb(wbs[:], wbs_raw[:])
         t2w.append(held([P, HALF], U32, "t2w1", tag="wbs_raw"))
         gather(t2w[1][:], t2w_all, entries(idx2, HALF, HALF))
-        for b in range(2):
-            for hf in range(2):
-                modulation(hf, b)
+        modulation(0, 0)
+        modulation(1, 0)
+        modulation(0, 1)
+        modulation(1, 1, range(2))
 
         pool_cast_wa(0, 0)
         gather(ts[:], ts_all, idx[:])
-        gather(tw[0][:], tw_all[0], idx[:])
+        gather_tw(0, 0)
+        gather_tw(0, 1)
         cast_wa(0, 1, nc.vector.tensor_copy, nc.vector.tensor_copy)
         for pair in range(2):
             quantize_wa(0, pair, wa16_0[:, 2 * pair * pair_w : 2 * (pair + 1) * pair_w])
-        gather_halves(tw[1], tw_all[1], idx)
+        gather_tw(1, 0)
+        gather_tw(1, 1)
 
         hidden_group(0, 7)
         last_sums = hidden(1, 0, 3)
@@ -309,12 +310,14 @@ def tile_list_locus_cell_tracks_kernel(
             quantize_wa(1, 1, wa16[1, 1][pair], pair * 2 * P)
         h_q[0, 0] = held([P, HALF], U32, "h_q00", tag="wa_raw11")
         quantize_h(0, 0)
-        h16[1, 0, 3] = placed([P, bank_w], BF16, "h16_103", 7168)[:]
+        h16[1, 0, 3] = held([P, bank_w], BF16, "h16_103", tag="h16_00")[:]
         product(1, 0, 3, last_sums)
+        modulation(1, 1, range(2, PACK), late=True)
         cast_wt(0, 0)
 
         hidden_group(1)
-        wt16[0, 1] = held([P, NH * PACK], BF16, "wt16_01", tag="mod10")
+        wt16[0, 1] = placed([P, NH * PACK], BF16, "wt16_01", 16384)
+        wt16[1, 0] = placed([P, NH * PACK], BF16, "wt16_10", 18432)
         cast_wt(0, 1)
         for b in range(2):
             cast_wt(1, b)

@@ -137,8 +137,10 @@ def tile_list_locus_cell_tracks_kernel(
         def gather(dst, table, lst):
             nc.vector.tensor_copy(dst, table[:].indirect(lst))
 
-        def gather_tw(a, hf):
-            gather(tw[a, hf][:], tw_all[a], entries(idx, hf * HALF, HALF))
+        def gather_tw(a, hf, pieces=1):
+            width = HALF // pieces
+            for c0 in range(0, HALF, width):
+                gather(tw[a, hf][:, c0 : c0 + width], tw_all[a], entries(idx, hf * HALF + c0, width))
 
         def quantize(codes, scales, src):
             nc.vector.quantize_mx(out=codes.bitcast(FP8X4), scales=scales, in_=src)
@@ -148,13 +150,13 @@ def tile_list_locus_cell_tracks_kernel(
 
         def cast_wa(b, a, *casts):
             src = wa_raw[b][a][:].rearrange("p j (m t) -> p m j t", t=PACK)
-            for pair, cast in enumerate(casts):
+            for pair, cast in casts:
                 dst = wa16[b, a][pair].rearrange("p (t m j) -> p m j t", t=2, j=PACK)
                 cast(dst, src[:, :, :, 2 * pair : 2 * pair + 2])
 
-        def pool_cast_wa(b, a):
+        def pool_cast_wa(b, a, slices):
             src = wa_raw[b][a][:].rearrange("p j (m t) -> p m j t", t=PACK)
-            for t in range(PACK):
+            for t in slices:
                 dst = wa16[b, a][t // 2].rearrange("p (t m j) -> p m j t", t=2, j=PACK)
                 nc.gpsimd.tensor_scalar(
                     out=dst[:, :, :, t % 2], in0=src[:, :, :, t], scalar1=1.0, scalar2=0.0, op0=ALU.mult, op1=ALU.add
@@ -284,28 +286,29 @@ def tile_list_locus_cell_tracks_kernel(
         reorder_wb(wbs[:], wbs_raw[:])
         t2w.append(held([P, HALF], U32, "t2w1", tag="wbs_raw"))
         gather(t2w[1][:], t2w_all, entries(idx2, HALF, HALF))
+        cast_wa(0, 0, (0, scalar_cast))
         modulation(0, 0)
         modulation(1, 0)
         modulation(0, 1)
         modulation(1, 1, range(2))
 
-        pool_cast_wa(0, 0)
+        pool_cast_wa(0, 0, (2, 3))
         gather(ts[:], ts_all, idx[:])
         gather_tw(0, 0)
         gather_tw(0, 1)
-        cast_wa(0, 1, nc.vector.tensor_copy, nc.vector.tensor_copy)
+        cast_wa(0, 1, (0, nc.vector.tensor_copy), (1, nc.vector.tensor_copy))
         for pair in range(2):
             quantize_wa(0, pair, wa16_0[:, 2 * pair * pair_w : 2 * (pair + 1) * pair_w])
-        gather_tw(1, 0)
+        gather_tw(1, 0, pieces=2)
         gather_tw(1, 1)
 
         hidden_group(0, 7)
         last_sums = hidden(1, 0, 3)
-        cast_wa(1, 0, scalar_cast, scalar_cast)
+        cast_wa(1, 0, (0, scalar_cast), (1, scalar_cast))
         wa_s[1, 0] = held([P, KP], U8, "wa_s10", tag="wa_s00")
         wa16[1, 1] = [held([P, pair_w], BF16, "wa16_110")[:], placed([P, pair_w], BF16, "wa16_111", 7168)[:]]
         quantize_wa(1, 0, wa16_10[:])
-        cast_wa(1, 1, scalar_cast, nc.vector.tensor_copy)
+        cast_wa(1, 1, (0, scalar_cast), (1, nc.vector.tensor_copy))
         for pair in range(2):
             quantize_wa(1, 1, wa16[1, 1][pair], pair * 2 * P)
         h_q[0, 0] = held([P, HALF], U32, "h_q00", tag="wa_raw11")

@@ -24,8 +24,9 @@ TOK = 128
 RUN = 2
 PER_COL = 16
 NH = N // 2
-POOL_SHARE = {(0, 0, 0): TOK, (0, 0, 1): TOK // 2, (1, 0, 3): TOK, (0, 1, 1): TOK}
-A_BANKS = (2, 3, 4, 5, 6, 0, 1, 7)
+POOL_SHARE = {(0, 0, 0): 3 * TOK // 4, (0, 0, 1): TOK, (1, 0, 3): TOK, (0, 1, 1): TOK}
+A_BANKS = (0, 1, 2, 3, 4, 7, 5, 6)
+POOL_COLS = 3 * P // 4
 LAST_PIECES = (256, 128, 128)
 
 
@@ -58,21 +59,22 @@ def tile_list_locus_cell_tracks_kernel(
         t2w_all = held([P, T], U32, "t2w_all")
         wa_raw = [
             [held([P, PACK, KP], F32, "wa_raw0%d" % a) for a in range(2)],
-            [placed([P, PACK, KP], F32, "wa_raw10", 0), held([P, PACK, KP], F32, "wa_raw11")],
+            [placed([P, PACK, KP], F32, "wa_raw10", 4096), held([P, PACK, KP], F32, "wa_raw11")],
         ]
         wt_raw = [[held([P, PACK, NH], F32, "wt_raw%d%d" % (nh, b)) for b in range(2)] for nh in range(2)]
         g_all = [held([P, T], F32, "g_all%d" % nb) for nb in range(N // P)]
 
-        for scale_tile in (t2s_all, wbs_raw, ts_all):
+        for scale_tile in (t2s_all, wbs_raw):
             nc.vector.memset(scale_tile[:].bitcast(I32), 0)
+        nc.gpsimd.memset(ts_all[:].bitcast(I32), 0)
 
         def load_words(dst, src):
             nc.sync.dma_start(out=dst[:].bitcast(I32), in_=src.rearrange("p t i -> p (t i)").bitcast(I32))
 
-        def load_scales(dst, src):
+        def load_scales(dst, src, queue=nc.sync):
             passes = src.shape[0]
             for q in range(4):
-                nc.sync.dma_start(
+                queue.dma_start(
                     out=dst[32 * q : 32 * q + 4 * passes, :].bitcast(I32),
                     in_=src[:, 4 * q : 4 * q + 4, :].bitcast(I32),
                 )
@@ -91,7 +93,7 @@ def tile_list_locus_cell_tracks_kernel(
         load_scales(wbs_raw, wb_scales)
         load_wa(0, 0)
         nc.sync.dma_start(idx[:], offs)
-        load_scales(ts_all, tab_scales)
+        load_scales(ts_all, tab_scales, nc.gpsimd)
         load_words(tw_all[0], tab_words[0])
         load_wa(0, 1)
         load_words(tw_all[1], tab_words[1])
@@ -109,8 +111,8 @@ def tile_list_locus_cell_tracks_kernel(
         wbw = held([P, 2 * H], U8, "wbw")
         wbs = held([P, H], U8, "wbs")
         wa_q = {(b, 1): held([P, KP], U32, "wa_q%d1" % b) for b in range(2)}
-        wa_q[0, 0] = placed([P, KP], U32, "wa_q00", 8192)
-        wa_q[1, 0] = placed([P, KP], U32, "wa_q10", 11264)
+        wa_q[0, 0] = held([P, KP], U32, "wa_q00")
+        wa_q[1, 0] = placed([P, KP], U32, "wa_q10", 1024)
         wa_s = {(b, i): held([P, KP], U8, "wa_s%d%d" % (b, i)) for b, i in ((0, 0), (0, 1), (1, 1))}
         wt_q = held([P, 2 * N], U32, "wt_q")
         h_s = [[held([P, HALF], U8, "h_s%d%d" % (hf, b)) for b in range(2)] for hf in range(2)]
@@ -121,15 +123,14 @@ def tile_list_locus_cell_tracks_kernel(
         wa16 = {(0, a): [wa16_0[:, (2 * pair + a) * pair_w : (2 * pair + a + 1) * pair_w] for pair in range(2)] for a in range(2)}
         wa16_10 = held([P, 2 * pair_w], BF16, "wa16_10")
         wa16[1, 0] = [wa16_10[:, pair * pair_w : (pair + 1) * pair_w] for pair in range(2)]
-        wt16 = {(nh, b): held([P, NH * PACK], BF16, "wt16_%d%d" % (nh, b)) for nh, b in ((0, 0), (1, 1))}
+        wt16 = {(nh, b): held([P, NH * PACK], BF16, "wt16_%d%d" % (nh, b)) for nh, b in ((0, 0), (1, 0))}
         bank_w = TOK * PACK
         h16 = {}
         for hf, b, count in ((0, 0, 4), (1, 0, 3), (0, 1, 4), (1, 1, 4)):
             staging = held([P, count * bank_w], BF16, "h16_%d%d" % (hf, b))
             h16[hf, b, 0] = staging[:]
         mod = [[held([P, PACK, HALF], F32, "mod%d%d" % (hf, b)) for b in range(2)] for hf in range(2)]
-        a_sb = {key: held([P, n * PACK], F32, "a_sb%d%d%d" % key) for key, n in POOL_SHARE.items() if key != (1, 0, 3)}
-        a_sb[1, 0, 3] = placed([P, TOK * PACK], F32, "a_sb103", 17408)
+        a_sb = {key: held([P, n * PACK], F32, "a_sb%d%d%d" % key) for key, n in POOL_SHARE.items()}
 
         def entries(lst, start, count):
             return lst[:, start // PER_COL : (start + count) // PER_COL]
@@ -154,12 +155,18 @@ def tile_list_locus_cell_tracks_kernel(
                 dst = wa16[b, a][pair].rearrange("p (t m j) -> p m j t", t=2, j=PACK)
                 cast(dst, src[:, :, :, 2 * pair : 2 * pair + 2])
 
-        def pool_cast_wa(b, a, slices):
+        def cast_wa00():
+            src = wa_raw[0][0][:].rearrange("p j (m t) -> p m j t", t=PACK)
+            for pair in range(2):
+                dst = wa16[0, 0][pair].rearrange("p (t m j) -> p m j t", t=2, j=PACK)
+                scalar_cast(dst[:, POOL_COLS:], src[:, POOL_COLS:, :, 2 * pair : 2 * pair + 2])
+
+        def pool_cast_wa(b, a):
             src = wa_raw[b][a][:].rearrange("p j (m t) -> p m j t", t=PACK)
-            for t in slices:
+            for t in range(PACK):
                 dst = wa16[b, a][t // 2].rearrange("p (t m j) -> p m j t", t=2, j=PACK)
                 nc.gpsimd.tensor_scalar(
-                    out=dst[:, :, :, t % 2], in0=src[:, :, :, t], scalar1=1.0, scalar2=0.0, op0=ALU.mult, op1=ALU.add
+                    out=dst[:, :POOL_COLS, :, t % 2], in0=src[:, :POOL_COLS, :, t], scalar1=1.0, scalar2=0.0, op0=ALU.mult, op1=ALU.add
                 )
 
         def wa_col(b, a, t):
@@ -177,10 +184,9 @@ def tile_list_locus_cell_tracks_kernel(
                 wt_raw[nh][b][:].rearrange("p j (c i) -> p c j i", i=RUN),
             )
 
-        def quantize_wt(nh):
-            for b in range(2):
-                cols = slice(nh * N + b * NH, nh * N + (b + 1) * NH)
-                quantize(wt_q[:, cols], wt_s[:, cols], wt16[nh, b][:])
+        def quantize_wt(nh, b):
+            cols = slice(nh * N + b * NH, nh * N + (b + 1) * NH)
+            quantize(wt_q[:, cols], wt_s[:, cols], wt16[nh, b][:])
 
         def reorder_wb(dst, src):
             nc.vector.tensor_copy(
@@ -192,7 +198,7 @@ def tile_list_locus_cell_tracks_kernel(
             cols = slice(hf * HALF, (hf + 1) * HALF)
             for t in slices:
                 c0 = b * KP + t * P
-                z = psum_bank(t % 2 if late else 5 + (8 * b + 4 * hf + t) % 3)
+                z = psum_bank(3 + t if late else 5 + (8 * b + 4 * hf + t) % 3)
                 nc.tensor.matmul_mx(
                     out=z[:],
                     lhsT=wbw[:, 2 * c0 : 2 * (c0 + P)].bitcast(FP4X4),
@@ -238,8 +244,8 @@ def tile_list_locus_cell_tracks_kernel(
             if split < TOK // RUN:
                 nc.vector.tensor_tensor(out=dst[:, split:], in0=sums[:, split:], in1=factor[:, split:], op=ALU.mult)
 
-        def hidden_group(b, count=2 * HALF // TOK):
-            for i in range(count):
+        def hidden_group(b, numbers):
+            for i in numbers:
                 product(i // 4, b, i % 4, hidden(i // 4, b, i % 4))
 
         def quantize_h(hf, b):
@@ -286,13 +292,13 @@ def tile_list_locus_cell_tracks_kernel(
         reorder_wb(wbs[:], wbs_raw[:])
         t2w.append(held([P, HALF], U32, "t2w1", tag="wbs_raw"))
         gather(t2w[1][:], t2w_all, entries(idx2, HALF, HALF))
-        cast_wa(0, 0, (0, scalar_cast))
+        cast_wa00()
         modulation(0, 0)
         modulation(1, 0)
         modulation(0, 1)
         modulation(1, 1, range(2))
 
-        pool_cast_wa(0, 0, (2, 3))
+        pool_cast_wa(0, 0)
         gather(ts[:], ts_all, idx[:])
         gather_tw(0, 0)
         gather_tw(0, 1)
@@ -300,45 +306,53 @@ def tile_list_locus_cell_tracks_kernel(
         for pair in range(2):
             quantize_wa(0, pair, wa16_0[:, 2 * pair * pair_w : 2 * (pair + 1) * pair_w])
         gather_tw(1, 0, pieces=2)
-        gather_tw(1, 1)
+        gather_tw(1, 1, pieces=2)
 
-        hidden_group(0, 7)
+        hidden_group(0, range(7))
         last_sums = hidden(1, 0, 3)
         cast_wa(1, 0, (0, scalar_cast), (1, scalar_cast))
-        wa_s[1, 0] = held([P, KP], U8, "wa_s10", tag="wa_s00")
-        wa16[1, 1] = [held([P, pair_w], BF16, "wa16_110")[:], placed([P, pair_w], BF16, "wa16_111", 7168)[:]]
-        quantize_wa(1, 0, wa16_10[:])
+        wa_s[1, 0] = placed([P, KP], U8, "wa_s10", 4096)
+        wa16[1, 1] = [held([P, pair_w], BF16, "wa16_110")[:], placed([P, pair_w], BF16, "wa16_111", 5120)[:]]
+        quantize_wa(1, 0, wa16[1, 0][0])
         cast_wa(1, 1, (0, scalar_cast), (1, nc.vector.tensor_copy))
+        quantize_wa(1, 0, wa16[1, 0][1], 2 * P)
         for pair in range(2):
             quantize_wa(1, 1, wa16[1, 1][pair], pair * 2 * P)
         h_q[0, 0] = held([P, HALF], U32, "h_q00", tag="wa_raw11")
         quantize_h(0, 0)
         h16[1, 0, 3] = held([P, bank_w], BF16, "h16_103", tag="h16_00")[:]
         product(1, 0, 3, last_sums)
+
+        hidden_group(1, range(4))
         modulation(1, 1, range(2, PACK), late=True)
         cast_wt(0, 0)
-
-        hidden_group(1)
-        wt16[0, 1] = placed([P, NH * PACK], BF16, "wt16_01", 16384)
-        wt16[1, 0] = placed([P, NH * PACK], BF16, "wt16_10", 18432)
+        hidden_group(1, range(4, 8))
+        wt16[0, 1] = held([P, NH * PACK], BF16, "wt16_01", tag="a_sb103")
         cast_wt(0, 1)
-        for b in range(2):
-            cast_wt(1, b)
-        h_q[0, 1] = placed([P, HALF], U32, "h_q01", 10240)
-        wt_s = held([P, 2 * N], U8, "wt_s", tag="wa_s00")
-        h_q[1, 0] = placed([P, HALF], U32, "h_q10", 12288)
-        quantize_wt(0)
+        cast_wt(1, 0)
+        h_q[0, 1] = placed([P, HALF], U32, "h_q01", 0)
+        wt_s = placed([P, 2 * N], U8, "wt_s", 4096)
+        h_q[1, 0] = placed([P, HALF], U32, "h_q10", 2048)
+        quantize_wt(0, 0)
+        quantize_wt(0, 1)
         quantize_h(0, 1)
         quantize_h(1, 0)
         quantize_h(1, 1)
-        quantize_wt(1)
+        quantize_wt(1, 0)
 
         y_sb = [held([P, N // P, HALF], F32, "y%d" % hf, tag="wa_raw0%d" % hf) for hf in range(2)]
         diff = [held([P, N // P, HALF], F32, "diff%d" % hf, tag="mod%d0" % hf) for hf in range(2)]
         tiles = [(hf, nb) for nh in range(2) for hf in range(2) for nb in (2 * nh, 2 * nh + 1)]
         tiles[5], tiles[6] = tiles[6], tiles[5]
-        for hf, nb in tiles:
+        for hf, nb in tiles[:4]:
             predict(hf, nb)
-        for hf, nb in tiles[:-1]:
+        wt16[1, 1] = held([P, NH * PACK], BF16, "wt16_11", tag="h16_11")
+        cast_wt(1, 1)
+        for hf, nb in tiles[:2]:
+            finish(hf, nb)
+        quantize_wt(1, 1)
+        for hf, nb in tiles[4:]:
+            predict(hf, nb)
+        for hf, nb in tiles[2:-1]:
             finish(hf, nb)
         finish(*tiles[-1], LAST_PIECES)

@@ -233,14 +233,20 @@ def tile_list_locus_cell_tracks_kernel(
             first = u if (hf, b, u) in h16 else 0
             dst = h16[hf, b, first][:, (u - first) * bank_w : (u - first + 1) * bank_w]
             factor = mod[hf][b][:, :, u * TOK : (u + 1) * TOK]
+            share = POOL_SHARE.get((hf, b, u), 0)
+            if share > 0:
+                copied = a_sb[hf, b, u][:].rearrange("p (j t) -> p j t", t=PACK)
+                nc.scalar.copy(out=copied, in_=sums.rearrange("p t j -> p j t")[:, :share])
+                nc.gpsimd.tensor_tensor(
+                    out=dst.rearrange("p (j t) -> p j t", t=PACK)[:, :share],
+                    in0=copied,
+                    in1=factor.rearrange("p t j -> p j t")[:, :share],
+                    op=ALU.mult,
+                )
             dst = dst.rearrange("p (c i t) -> p c t i", i=RUN, t=PACK)
             sums = sums.rearrange("p t (c i) -> p c t i", i=RUN)
             factor = factor.rearrange("p t (c i) -> p c t i", i=RUN)
-            split = POOL_SHARE.get((hf, b, u), 0) // RUN
-            if split > 0:
-                copied = a_sb[hf, b, u][:].rearrange("p (c t i) -> p c t i", t=PACK, i=RUN)
-                nc.scalar.copy(out=copied, in_=sums[:, :split])
-                nc.gpsimd.tensor_tensor(out=dst[:, :split], in0=copied, in1=factor[:, :split], op=ALU.mult)
+            split = share // RUN
             if split < TOK // RUN:
                 nc.vector.tensor_tensor(out=dst[:, split:], in0=sums[:, split:], in1=factor[:, split:], op=ALU.mult)
 

@@ -1,6 +1,7 @@
 from contextlib import ExitStack
 
 import concourse.mybir as mybir
+from concourse.masks import make_identity
 
 K, C, H, N, T, S = 1024, 512, 1024, 512, 2048, 1024
 FLOPS = 2 * S * (K * H + C * H + H * N)
@@ -54,19 +55,22 @@ def tile_list_locus_cell_tracks_kernel(
         t2s_all = held([P, T], U8, "t2s_all")
         wbs_raw = held([P, H], U8, "wbs_raw")
         wbw_raw = held([P, 2 * H], U8, "wbw_raw")
-        bias = held([P, H // KP, PACK], F32, "bias")
+        bias_rows = held([P, KP], F32, "bias_rows")
         tw_all = [held([P, T], U32, "tw_all%d" % a) for a in range(2)]
         t2w_all = held([P, T], U32, "t2w_all")
         wa_raw = [
             [held([P, PACK, KP], F32, "wa_raw0%d" % a) for a in range(2)],
             [placed([P, PACK, KP], F32, "wa_raw10", 4096), held([P, PACK, KP], F32, "wa_raw11")],
         ]
-        wt_raw = [[held([P, PACK, NH], F32, "wt_raw%d%d" % (nh, b)) for b in range(2)] for nh in range(2)]
+        wt_raw = [held([P, PACK, N], F32, "wt_raw%d" % b) for b in range(2)]
         g_all = [held([P, T], F32, "g_all%d" % nb) for nb in range(N // P)]
 
         for scale_tile in (t2s_all, wbs_raw):
             nc.vector.memset(scale_tile[:].bitcast(I32), 0)
         nc.gpsimd.memset(ts_all[:].bitcast(I32), 0)
+        zero = held([P, 1], F32, "zero")
+        nc.vector.memset(zero[:], 0.0)
+        nc.scalar.activation(out=bias_rows[:], in_=zero[:].to_broadcast([P, KP]), func=ACT.Copy)
 
         def load_words(dst, src):
             nc.sync.dma_start(out=dst[:].bitcast(I32), in_=src.rearrange("p t i -> p (t i)").bitcast(I32))
@@ -89,7 +93,7 @@ def tile_list_locus_cell_tracks_kernel(
         nc.sync.dma_start(out=wbw_raw[:].bitcast(I32), in_=wb_words[0].bitcast(I32))
         load_scales(t2s_all, tab2_scales)
         load_words(t2w_all, tab2_words[0])
-        nc.sync.dma_start(out=bias[:], in_=bc.rearrange("(b p t) -> p b t", p=P, t=PACK))
+        nc.sync.dma_start(out=bias_rows[0 : H // KP, :], in_=bc.rearrange("(b r) -> b r", r=KP))
         load_scales(wbs_raw, wb_scales)
         load_wa(0, 0)
         nc.sync.dma_start(idx[:], offs)
@@ -99,15 +103,28 @@ def tile_list_locus_cell_tracks_kernel(
         load_words(tw_all[1], tab_words[1])
         load_wa(1, 0)
         load_wa(1, 1)
+        for b in range(2):
+            rows = wt[b * KP : (b + 1) * KP, :].rearrange("(m t e) n -> t m e n", t=PACK, e=2)
+            for t in range(PACK):
+                nc.sync.dma_start(out=wt_raw[b][:, t, :], in_=rows[t])
         for nb in range(N // P):
-            if nb < 2:
-                for b in range(2):
-                    load_rows(wt_raw[nb][b], wt[b * KP : (b + 1) * KP, nb * NH : (nb + 1) * NH])
             nc.sync.dma_start(out=g_all[nb][:], in_=gT[nb * P : (nb + 1) * P, :])
+
+        identity = held([P, P], F32, "identity")
+        make_identity(nc, identity[:])
+        turned = psum_bank(0)[:].rearrange("p (t x) -> p t x", t=PACK)
+        bias_cols = held([P, KP], F32, "bias_cols")
+        nc.scalar.activation(
+            out=bias_cols[:].rearrange("p (t m e) -> p t m e", t=PACK, e=2),
+            in_=bias_rows[:].rearrange("p (m t e) -> p t m e", t=PACK, e=2),
+            func=ACT.Copy,
+        )
+        for t in range(PACK):
+            nc.tensor.transpose(turned[:, t, :], bias_cols[:, t * P : (t + 1) * P], identity[:])
 
         ts = held([P, S], U8, "ts")
         t2s = held([P, S], U8, "t2s")
-        tw = {(a, hf): held([P, HALF], U32, "tw%d%d" % (a, hf)) for a in range(2) for hf in range(2)}
+        tw = [held([P, S], U32, "tw%d" % a) for a in range(2)]
         wbw = held([P, 2 * H], U8, "wbw")
         wbs = held([P, H], U8, "wbs")
         wa_q = {(b, 1): held([P, KP], U32, "wa_q%d1" % b) for b in range(2)}
@@ -123,7 +140,7 @@ def tile_list_locus_cell_tracks_kernel(
         wa16 = {(0, a): [wa16_0[:, (2 * pair + a) * pair_w : (2 * pair + a + 1) * pair_w] for pair in range(2)] for a in range(2)}
         wa16_10 = held([P, 2 * pair_w], BF16, "wa16_10")
         wa16[1, 0] = [wa16_10[:, pair * pair_w : (pair + 1) * pair_w] for pair in range(2)]
-        wt16 = {(nh, b): held([P, NH * PACK], BF16, "wt16_%d%d" % (nh, b)) for nh, b in ((0, 0), (1, 0))}
+        wt16 = {(nh, b): held([P, NH * PACK], BF16, "wt16_%d%d" % (nh, b)) for nh, b in ((0, 0), (0, 1))}
         bank_w = TOK * PACK
         h16 = {}
         for hf, b, count in ((0, 0, 4), (1, 0, 3), (0, 1, 4), (1, 1, 4)):
@@ -138,35 +155,40 @@ def tile_list_locus_cell_tracks_kernel(
         def gather(dst, table, lst):
             nc.vector.tensor_copy(dst, table[:].indirect(lst))
 
-        def gather_tw(a, hf, pieces=1):
-            width = HALF // pieces
-            for c0 in range(0, HALF, width):
-                gather(tw[a, hf][:, c0 : c0 + width], tw_all[a], entries(idx, hf * HALF + c0, width))
+        def gather_tw(a, pieces=1):
+            width = S // pieces
+            for c0 in range(0, S, width):
+                gather(tw[a][:, c0 : c0 + width], tw_all[a], entries(idx, c0, width))
 
         def quantize(codes, scales, src):
             nc.vector.quantize_mx(out=codes.bitcast(FP8X4), scales=scales, in_=src)
 
         def scalar_cast(dst, src):
-            nc.scalar.activation(out=dst, in_=src, func=ACT.Copy)
+            nc.scalar.copy(out=dst, in_=src)
 
         def cast_wa(b, a, *casts):
-            src = wa_raw[b][a][:].rearrange("p j (m t) -> p m j t", t=PACK)
+            src = wa_raw[b][a][:].rearrange("p j (m t e) -> p m j t e", t=PACK, e=2)
             for pair, cast in casts:
-                dst = wa16[b, a][pair].rearrange("p (t m j) -> p m j t", t=2, j=PACK)
+                dst = wa16[b, a][pair].rearrange("p (t m e j) -> p m j t e", t=2, e=2, j=PACK)
                 cast(dst, src[:, :, :, 2 * pair : 2 * pair + 2])
 
         def cast_wa00():
-            src = wa_raw[0][0][:].rearrange("p j (m t) -> p m j t", t=PACK)
+            src = wa_raw[0][0][:].rearrange("p j (m t e) -> p m j t e", t=PACK, e=2)
             for pair in range(2):
-                dst = wa16[0, 0][pair].rearrange("p (t m j) -> p m j t", t=2, j=PACK)
-                scalar_cast(dst[:, POOL_COLS:], src[:, POOL_COLS:, :, 2 * pair : 2 * pair + 2])
+                dst = wa16[0, 0][pair].rearrange("p (t m e j) -> p m j t e", t=2, e=2, j=PACK)
+                scalar_cast(dst[:, POOL_COLS // 2 :], src[:, POOL_COLS // 2 :, :, 2 * pair : 2 * pair + 2])
 
         def pool_cast_wa(b, a):
-            src = wa_raw[b][a][:].rearrange("p j (m t) -> p m j t", t=PACK)
+            src = wa_raw[b][a][:].rearrange("p j (m t e) -> p t m e j", t=PACK, e=2)
             for t in range(PACK):
-                dst = wa16[b, a][t // 2].rearrange("p (t m j) -> p m j t", t=2, j=PACK)
+                dst = wa16[b, a][t // 2].rearrange("p (t m e j) -> p t m e j", t=2, e=2, j=PACK)
                 nc.gpsimd.tensor_scalar(
-                    out=dst[:, :POOL_COLS, :, t % 2], in0=src[:, :POOL_COLS, :, t], scalar1=1.0, scalar2=0.0, op0=ALU.mult, op1=ALU.add
+                    out=dst[:, t % 2, : POOL_COLS // 2],
+                    in0=src[:, t, : POOL_COLS // 2],
+                    scalar1=1.0,
+                    scalar2=0.0,
+                    op0=ALU.mult,
+                    op1=ALU.add,
                 )
 
         def wa_col(b, a, t):
@@ -181,15 +203,15 @@ def tile_list_locus_cell_tracks_kernel(
         def cast_wt(nh, b):
             scalar_cast(
                 wt16[nh, b][:].rearrange("p (c i j) -> p c j i", i=RUN, j=PACK),
-                wt_raw[nh][b][:].rearrange("p j (c i) -> p c j i", i=RUN),
+                wt_raw[b][:, :, nh * NH : (nh + 1) * NH].rearrange("p j (c i) -> p c j i", i=RUN),
             )
 
         def quantize_wt(nh, b):
             cols = slice(nh * N + b * NH, nh * N + (b + 1) * NH)
             quantize(wt_q[:, cols], wt_s[:, cols], wt16[nh, b][:])
 
-        def reorder_wb(dst, src):
-            nc.vector.tensor_copy(
+        def reorder_wb(move, dst, src):
+            move(
                 out=dst.rearrange("p (b t m) -> p b t m", b=2, t=PACK),
                 in_=src.rearrange("p (b m t) -> p b t m", b=2, t=PACK),
             )
@@ -208,7 +230,7 @@ def tile_list_locus_cell_tracks_kernel(
                     start=True,
                     stop=True,
                 )
-                nc.scalar.activation(out=mod[hf][b][:, t, :], in_=z[:], func=ACT.Tanh, bias=bias[:, b, t : t + 1])
+                nc.scalar.activation(out=mod[hf][b][:, t, :], in_=z[:], func=ACT.Tanh, bias=bias[:, t, b : b + 1])
 
         def hidden(hf, b, u):
             cols = slice(hf * HALF + u * TOK, hf * HALF + (u + 1) * TOK)
@@ -222,7 +244,7 @@ def tile_list_locus_cell_tracks_kernel(
                         out=sums[:, t, :],
                         lhsT=wa_q[b, i][:, c0 : c0 + P].bitcast(FP8X4),
                         lhsT_scale=wa_s[b, i][:, c0 : c0 + P],
-                        rhs=tw[a, hf][:, u * TOK : (u + 1) * TOK].bitcast(FP8X4),
+                        rhs=tw[a][:, cols].bitcast(FP8X4),
                         rhs_scale=ts[4 * a : P, cols],
                         start=(a == passes[0] and t == 0),
                         stop=(a == passes[1] and t == PACK - 1),
@@ -291,12 +313,14 @@ def tile_list_locus_cell_tracks_kernel(
                 nc.sync.dma_start(out=out[nb * P : (nb + 1) * P, s0 : s0 + width], in_=piece)
                 c0 = c0 + width
 
-        reorder_wb(wbw[:].bitcast(U16), wbw_raw[:].bitcast(U16))
+        reorder_wb(nc.vector.tensor_copy, wbw[:].bitcast(U32), wbw_raw[:].bitcast(U32))
         gather(t2s[:], t2s_all, idx2[:])
         t2w = [held([P, HALF], U32, "t2w0")]
         gather(t2w[0][:], t2w_all, entries(idx2, 0, HALF))
-        reorder_wb(wbs[:], wbs_raw[:])
-        t2w.append(held([P, HALF], U32, "t2w1", tag="wbs_raw"))
+        reorder_wb(nc.scalar.copy, wbs[:].bitcast(U16), wbs_raw[:].bitcast(U16))
+        bias = held([P, PACK, H // KP], F32, "bias", tag="wbs_raw")
+        nc.scalar.activation(out=bias[:], in_=turned[:, :, 0 : H // KP], func=ACT.Copy)
+        t2w.append(held([P, HALF], U32, "t2w1"))
         gather(t2w[1][:], t2w_all, entries(idx2, HALF, HALF))
         cast_wa00()
         modulation(0, 0)
@@ -306,13 +330,11 @@ def tile_list_locus_cell_tracks_kernel(
 
         pool_cast_wa(0, 0)
         gather(ts[:], ts_all, idx[:])
-        gather_tw(0, 0)
-        gather_tw(0, 1)
+        gather_tw(0)
         cast_wa(0, 1, (0, nc.vector.tensor_copy), (1, nc.vector.tensor_copy))
         for pair in range(2):
             quantize_wa(0, pair, wa16_0[:, 2 * pair * pair_w : 2 * (pair + 1) * pair_w])
-        gather_tw(1, 0, pieces=2)
-        gather_tw(1, 1, pieces=2)
+        gather_tw(1, pieces=4)
 
         hidden_group(0, range(7))
         last_sums = hidden(1, 0, 3)
@@ -333,7 +355,7 @@ def tile_list_locus_cell_tracks_kernel(
         modulation(1, 1, range(2, PACK), late=True)
         cast_wt(0, 0)
         hidden_group(1, range(4, 8))
-        wt16[0, 1] = held([P, NH * PACK], BF16, "wt16_01", tag="a_sb103")
+        wt16[1, 0] = held([P, NH * PACK], BF16, "wt16_10", tag="a_sb103")
         cast_wt(0, 1)
         cast_wt(1, 0)
         h_q[0, 1] = placed([P, HALF], U32, "h_q01", 0)
@@ -350,10 +372,12 @@ def tile_list_locus_cell_tracks_kernel(
         diff = [held([P, N // P, HALF], F32, "diff%d" % hf, tag="mod%d0" % hf) for hf in range(2)]
         tiles = [(hf, nb) for nh in range(2) for hf in range(2) for nb in (2 * nh, 2 * nh + 1)]
         tiles[5], tiles[6] = tiles[6], tiles[5]
-        for hf, nb in tiles[:4]:
+        for hf, nb in tiles[:2]:
             predict(hf, nb)
         wt16[1, 1] = held([P, NH * PACK], BF16, "wt16_11", tag="h16_11")
         cast_wt(1, 1)
+        for hf, nb in tiles[2:4]:
+            predict(hf, nb)
         for hf, nb in tiles[:2]:
             finish(hf, nb)
         quantize_wt(1, 1)

from contextlib import ExitStack

import concourse.mybir as mybir
from concourse.masks import make_identity

K, C, H, N, T, S = 1024, 512, 1024, 512, 2048, 1024
FLOPS = 2 * S * (K * H + C * H + H * N)

F32 = mybir.dt.float32
BF16 = mybir.dt.bfloat16
I32 = mybir.dt.int32
U32 = mybir.dt.uint32
U16 = mybir.dt.uint16
U8 = mybir.dt.uint8
FP8X4 = mybir.dt.float8_e4m3fn_x4
FP4X4 = mybir.dt.float4_e2m1fn_x4
ACT = mybir.ActivationFunctionType
ALU = mybir.AluOpType

P = 128
PACK = 4
KP = P * PACK
HALF = S // 2
TOK = 128
RUN = 2
PER_COL = 16
NH = N // 2
POOL_SHARE = {(0, 0, 0): 3 * TOK // 4, (0, 0, 1): TOK, (1, 0, 3): TOK, (0, 1, 1): TOK}
A_BANKS = (0, 1, 2, 3, 4, 7, 5, 6)
POOL_COLS = 3 * P // 4
LAST_PIECES = (256, 128, 128)


def tile_list_locus_cell_tracks_kernel(
    tc, tab_words, tab_scales, offs, tab2_words, tab2_scales, offs2, wa, wb_words, wb_scales, bc, wt, gT, out
):
    nc = tc.nc
    with ExitStack() as ctx:
        keep = ctx.enter_context(tc.tile_pool(name="keep", bufs=1))
        tied = ctx.enter_context(tc.tile_pool(name="tied", bufs=1))
        banks = ctx.enter_context(tc.psum_pool(name="banks", bufs=1))

        def psum_bank(number):
            return banks.tile([P, HALF], F32, name="bank%d" % number)

        def held(shape, dtype, name, tag=None):
            return keep.tile(shape, dtype, name=name, tag=tag or name, align_bytes=64)

        def placed(shape, dtype, name, offset):
            return tied.tile(shape, dtype, name=name, offset=offset, align_bytes=64)

        idx = keep.tile([P, S // PER_COL], U16, name="idx")
        idx2 = keep.tile([P, S // PER_COL], U16, name="idx2")
        ts_all = held([P, T], U8, "ts_all")
        t2s_all = held([P, T], U8, "t2s_all")
        wbs_raw = held([P, H], U8, "wbs_raw")
        wbw_raw = held([P, 2 * H], U8, "wbw_raw")
        bias_rows = held([P, KP], F32, "bias_rows")
        tw_all = [held([P, T], U32, "tw_all%d" % a) for a in range(2)]
        t2w_all = held([P, T], U32, "t2w_all")
        wa_raw = [
            [held([P, PACK, KP], F32, "wa_raw0%d" % a) for a in range(2)],
            [placed([P, PACK, KP], F32, "wa_raw10", 4096), held([P, PACK, KP], F32, "wa_raw11")],
        ]
        wt_raw = [held([P, PACK, N], F32, "wt_raw%d" % b) for b in range(2)]
        g_all = [held([P, T], F32, "g_all%d" % nb) for nb in range(N // P)]

        for scale_tile in (t2s_all, wbs_raw):
            nc.vector.memset(scale_tile[:].bitcast(I32), 0)
        nc.gpsimd.memset(ts_all[:].bitcast(I32), 0)
        zero = held([P, 1], F32, "zero")
        nc.vector.memset(zero[:], 0.0)
        nc.scalar.activation(out=bias_rows[:], in_=zero[:].to_broadcast([P, KP]), func=ACT.Copy)

        def load_words(dst, src):
            nc.sync.dma_start(out=dst[:].bitcast(I32), in_=src.rearrange("p t i -> p (t i)").bitcast(I32))

        def load_scales(dst, src, queue=nc.sync):
            passes = src.shape[0]
            for q in range(4):
                queue.dma_start(
                    out=dst[32 * q : 32 * q + 4 * passes, :].bitcast(I32),
                    in_=src[:, 4 * q : 4 * q + 4, :].bitcast(I32),
                )

        def load_rows(dst, rows):
            nc.sync.dma_start(out=dst[:], in_=rows.rearrange("(p j) c -> p j c", j=PACK))

        def load_wa(b, a):
            load_rows(wa_raw[b][a], wa[a * KP : (a + 1) * KP, b * KP : (b + 1) * KP])

        nc.sync.dma_start(idx2[:], offs2)
        nc.sync.dma_start(out=wbw_raw[:].bitcast(I32), in_=wb_words[0].bitcast(I32))
        load_scales(t2s_all, tab2_scales)
        load_words(t2w_all, tab2_words[0])
        nc.sync.dma_start(out=bias_rows[0 : H // KP, :], in_=bc.rearrange("(b r) -> b r", r=KP))
        load_scales(wbs_raw, wb_scales)
        load_wa(0, 0)
        nc.sync.dma_start(idx[:], offs)
        load_scales(ts_all, tab_scales, nc.gpsimd)
        load_words(tw_all[0], tab_words[0])
        load_wa(0, 1)
        load_words(tw_all[1], tab_words[1])
        load_wa(1, 0)
        load_wa(1, 1)
        for b in range(2):
            rows = wt[b * KP : (b + 1) * KP, :].rearrange("(m t e) n -> t m e n", t=PACK, e=2)
            for t in range(PACK):
                nc.sync.dma_start(out=wt_raw[b][:, t, :], in_=rows[t])
        for nb in range(N // P):
            nc.sync.dma_start(out=g_all[nb][:], in_=gT[nb * P : (nb + 1) * P, :])

        identity = held([P, P], F32, "identity")
        make_identity(nc, identity[:])
        turned = psum_bank(0)[:].rearrange("p (t x) -> p t x", t=PACK)
        bias_cols = held([P, KP], F32, "bias_cols")
        nc.scalar.activation(
            out=bias_cols[:].rearrange("p (t m e) -> p t m e", t=PACK, e=2),
            in_=bias_rows[:].rearrange("p (m t e) -> p t m e", t=PACK, e=2),
            func=ACT.Copy,
        )
        for t in range(PACK):
            nc.tensor.transpose(turned[:, t, :], bias_cols[:, t * P : (t + 1) * P], identity[:])

        ts = held([P, S], U8, "ts")
        t2s = held([P, S], U8, "t2s")
        tw = [held([P, S], U32, "tw%d" % a) for a in range(2)]
        wbw = held([P, 2 * H], U8, "wbw")
        wbs = held([P, H], U8, "wbs")
        wa_q = {(b, 1): held([P, KP], U32, "wa_q%d1" % b) for b in range(2)}
        wa_q[0, 0] = held([P, KP], U32, "wa_q00")
        wa_q[1, 0] = placed([P, KP], U32, "wa_q10", 1024)
        wa_s = {(b, i): held([P, KP], U8, "wa_s%d%d" % (b, i)) for b, i in ((0, 0), (0, 1), (1, 1))}
        wt_q = held([P, 2 * N], U32, "wt_q")
        h_s = [[held([P, HALF], U8, "h_s%d%d" % (hf, b)) for b in range(2)] for hf in range(2)]
        h_q = {(1, 1): held([P, HALF], U32, "h_q11")}

        pair_w = 2 * P * PACK
        wa16_0 = held([P, 4 * pair_w], BF16, "wa16_0")
        wa16 = {(0, a): [wa16_0[:, (2 * pair + a) * pair_w : (2 * pair + a + 1) * pair_w] for pair in range(2)] for a in range(2)}
        wa16_10 = held([P, 2 * pair_w], BF16, "wa16_10")
        wa16[1, 0] = [wa16_10[:, pair * pair_w : (pair + 1) * pair_w] for pair in range(2)]
        wt16 = {(nh, b): held([P, NH * PACK], BF16, "wt16_%d%d" % (nh, b)) for nh, b in ((0, 0), (0, 1))}
        bank_w = TOK * PACK
        h16 = {}
        for hf, b, count in ((0, 0, 4), (1, 0, 3), (0, 1, 4), (1, 1, 4)):
            staging = held([P, count * bank_w], BF16, "h16_%d%d" % (hf, b))
            h16[hf, b, 0] = staging[:]
        mod = [[held([P, PACK, HALF], F32, "mod%d%d" % (hf, b)) for b in range(2)] for hf in range(2)]
        a_sb = {key: held([P, n * PACK], F32, "a_sb%d%d%d" % key) for key, n in POOL_SHARE.items()}

        def entries(lst, start, count):
            return lst[:, start // PER_COL : (start + count) // PER_COL]

        def gather(dst, table, lst):
            nc.vector.tensor_copy(dst, table[:].indirect(lst))

        def gather_tw(a, pieces=1):
            width = S // pieces
            for c0 in range(0, S, width):
                gather(tw[a][:, c0 : c0 + width], tw_all[a], entries(idx, c0, width))

        def quantize(codes, scales, src):
            nc.vector.quantize_mx(out=codes.bitcast(FP8X4), scales=scales, in_=src)

        def scalar_cast(dst, src):
            nc.scalar.copy(out=dst, in_=src)

        def cast_wa(b, a, *casts):
            src = wa_raw[b][a][:].rearrange("p j (m t e) -> p m j t e", t=PACK, e=2)
            for pair, cast in casts:
                dst = wa16[b, a][pair].rearrange("p (t m e j) -> p m j t e", t=2, e=2, j=PACK)
                cast(dst, src[:, :, :, 2 * pair : 2 * pair + 2])

        def cast_wa00():
            src = wa_raw[0][0][:].rearrange("p j (m t e) -> p m j t e", t=PACK, e=2)
            for pair in range(2):
                dst = wa16[0, 0][pair].rearrange("p (t m e j) -> p m j t e", t=2, e=2, j=PACK)
                scalar_cast(dst[:, POOL_COLS // 2 :], src[:, POOL_COLS // 2 :, :, 2 * pair : 2 * pair + 2])

        def pool_cast_wa(b, a):
            src = wa_raw[b][a][:].rearrange("p j (m t e) -> p t m e j", t=PACK, e=2)
            for t in range(PACK):
                dst = wa16[b, a][t // 2].rearrange("p (t m e j) -> p t m e j", t=2, e=2, j=PACK)
                nc.gpsimd.tensor_scalar(
                    out=dst[:, t % 2, : POOL_COLS // 2],
                    in0=src[:, t, : POOL_COLS // 2],
                    scalar1=1.0,
                    scalar2=0.0,
                    op0=ALU.mult,
                    op1=ALU.add,
                )

        def wa_col(b, a, t):
            if b == 0:
                return t // 2, a * 2 * P + t % 2 * P
            return a, t * P

        def quantize_wa(b, i, src, c0=0):
            cols = slice(c0, c0 + src.shape[1] // PACK)
            quantize(wa_q[b, i][:, cols], wa_s[b, i][:, cols], src)

        def cast_wt(nh, b):
            scalar_cast(
                wt16[nh, b][:].rearrange("p (c i j) -> p c j i", i=RUN, j=PACK),
                wt_raw[b][:, :, nh * NH : (nh + 1) * NH].rearrange("p j (c i) -> p c j i", i=RUN),
            )

        def quantize_wt(nh, b):
            cols = slice(nh * N + b * NH, nh * N + (b + 1) * NH)
            quantize(wt_q[:, cols], wt_s[:, cols], wt16[nh, b][:])

        def reorder_wb(move, dst, src):
            move(
                out=dst.rearrange("p (b t m) -> p b t m", b=2, t=PACK),
                in_=src.rearrange("p (b m t) -> p b t m", b=2, t=PACK),
            )

        def modulation(hf, b, slices=range(PACK), late=False):
            cols = slice(hf * HALF, (hf + 1) * HALF)
            for t in slices:
                c0 = b * KP + t * P
                z = psum_bank(3 + t if late else 5 + (8 * b + 4 * hf + t) % 3)
                nc.tensor.matmul_mx(
                    out=z[:],
                    lhsT=wbw[:, 2 * c0 : 2 * (c0 + P)].bitcast(FP4X4),
                    lhsT_scale=wbs[:, c0 : c0 + P],
                    rhs=t2w[hf][:].bitcast(FP8X4),
                    rhs_scale=t2s[:, cols],
                    start=True,
                    stop=True,
                )
                nc.scalar.activation(out=mod[hf][b][:, t, :], in_=z[:], func=ACT.Tanh, bias=bias[:, t, b : b + 1])

        def hidden(hf, b, u):
            cols = slice(hf * HALF + u * TOK, hf * HALF + (u + 1) * TOK)
            bank = psum_bank((4 * hf + u, A_BANKS[4 * hf + u])[b])
            sums = bank[:].rearrange("p (t j) -> p t j", t=PACK)
            passes = (hf, 1 - hf)
            for a in passes:
                for t in range(PACK):
                    i, c0 = wa_col(b, a, t)
                    nc.tensor.matmul_mx(
                        out=sums[:, t, :],
                        lhsT=wa_q[b, i][:, c0 : c0 + P].bitcast(FP8X4),
                        lhsT_scale=wa_s[b, i][:, c0 : c0 + P],
                        rhs=tw[a][:, cols].bitcast(FP8X4),
                        rhs_scale=ts[4 * a : P, cols],
                        start=(a == passes[0] and t == 0),
                        stop=(a == passes[1] and t == PACK - 1),
                    )
            return sums

        def product(hf, b, u, sums):
            first = u if (hf, b, u) in h16 else 0
            dst = h16[hf, b, first][:, (u - first) * bank_w : (u - first + 1) * bank_w]
            factor = mod[hf][b][:, :, u * TOK : (u + 1) * TOK]
            share = POOL_SHARE.get((hf, b, u), 0)
            if share > 0:
                copied = a_sb[hf, b, u][:].rearrange("p (j t) -> p j t", t=PACK)
                nc.scalar.copy(out=copied, in_=sums.rearrange("p t j -> p j t")[:, :share])
                nc.gpsimd.tensor_tensor(
                    out=dst.rearrange("p (j t) -> p j t", t=PACK)[:, :share],
                    in0=copied,
                    in1=factor.rearrange("p t j -> p j t")[:, :share],
                    op=ALU.mult,
                )
            dst = dst.rearrange("p (c i t) -> p c t i", i=RUN, t=PACK)
            sums = sums.rearrange("p t (c i) -> p c t i", i=RUN)
            factor = factor.rearrange("p t (c i) -> p c t i", i=RUN)
            split = share // RUN
            if split < TOK // RUN:
                nc.vector.tensor_tensor(out=dst[:, split:], in0=sums[:, split:], in1=factor[:, split:], op=ALU.mult)

        def hidden_group(b, numbers):
            for i in numbers:
                product(i // 4, b, i % 4, hidden(i // 4, b, i % 4))

        def quantize_h(hf, b):
            for first in range(HALF // TOK):
                if (hf, b, first) in h16:
                    src = h16[hf, b, first]
                    cols = slice(first * TOK, first * TOK + src.shape[1] // PACK)
                    quantize(h_q[hf, b][:, cols], h_s[hf][b][:, cols], src)

        def predict(hf, nb):
            bank = psum_bank(A_BANKS[tiles.index((hf, nb))])
            for b in range(2):
                w0 = nb // 2 * N + b * NH + nb % 2 * P
                nc.tensor.matmul_mx(
                    out=bank[:],
                    lhsT=wt_q[:, w0 : w0 + P].bitcast(FP8X4),
                    lhsT_scale=wt_s[:, w0 : w0 + P],
                    rhs=h_q[hf, b][:].bitcast(FP8X4),
                    rhs_scale=h_s[hf][b][:],
                    start=(b == 0),
                    stop=(b == 1),
                )
            nc.scalar.copy(out=y_sb[hf][:, nb, :], in_=bank[:])

        def finish(hf, nb, pieces=(HALF,)):
            c0 = 0
            for width in pieces:
                piece = diff[hf][:, nb, c0 : c0 + width]
                s0 = hf * HALF + c0
                nc.vector.tensor_tensor(
                    out=piece,
                    in0=g_all[nb][:].indirect(entries(idx, s0, width)),
                    in1=y_sb[hf][:, nb, c0 : c0 + width],
                    op=ALU.subtract,
                )
                nc.scalar.activation(out=piece, in_=piece, func=ACT.Abs)
                nc.sync.dma_start(out=out[nb * P : (nb + 1) * P, s0 : s0 + width], in_=piece)
                c0 = c0 + width

        reorder_wb(nc.vector.tensor_copy, wbw[:].bitcast(U32), wbw_raw[:].bitcast(U32))
        gather(t2s[:], t2s_all, idx2[:])
        t2w = [held([P, HALF], U32, "t2w0")]
        gather(t2w[0][:], t2w_all, entries(idx2, 0, HALF))
        reorder_wb(nc.scalar.copy, wbs[:].bitcast(U16), wbs_raw[:].bitcast(U16))
        bias = held([P, PACK, H // KP], F32, "bias", tag="wbs_raw")
        nc.scalar.activation(out=bias[:], in_=turned[:, :, 0 : H // KP], func=ACT.Copy)
        t2w.append(held([P, HALF], U32, "t2w1"))
        gather(t2w[1][:], t2w_all, entries(idx2, HALF, HALF))
        cast_wa00()
        modulation(0, 0)
        modulation(1, 0)
        modulation(0, 1)
        modulation(1, 1, range(2))

        pool_cast_wa(0, 0)
        gather(ts[:], ts_all, idx[:])
        gather_tw(0)
        cast_wa(0, 1, (0, nc.vector.tensor_copy), (1, nc.vector.tensor_copy))
        for pair in range(2):
            quantize_wa(0, pair, wa16_0[:, 2 * pair * pair_w : 2 * (pair + 1) * pair_w])
        gather_tw(1, pieces=4)

        hidden_group(0, range(7))
        last_sums = hidden(1, 0, 3)
        cast_wa(1, 0, (0, scalar_cast), (1, scalar_cast))
        wa_s[1, 0] = placed([P, KP], U8, "wa_s10", 4096)
        wa16[1, 1] = [held([P, pair_w], BF16, "wa16_110")[:], placed([P, pair_w], BF16, "wa16_111", 5120)[:]]
        quantize_wa(1, 0, wa16[1, 0][0])
        cast_wa(1, 1, (0, scalar_cast), (1, nc.vector.tensor_copy))
        quantize_wa(1, 0, wa16[1, 0][1], 2 * P)
        for pair in range(2):
            quantize_wa(1, 1, wa16[1, 1][pair], pair * 2 * P)
        h_q[0, 0] = held([P, HALF], U32, "h_q00", tag="wa_raw11")
        quantize_h(0, 0)
        h16[1, 0, 3] = held([P, bank_w], BF16, "h16_103", tag="h16_00")[:]
        product(1, 0, 3, last_sums)

        hidden_group(1, range(4))
        modulation(1, 1, range(2, PACK), late=True)
        cast_wt(0, 0)
        hidden_group(1, range(4, 8))
        wt16[1, 0] = held([P, NH * PACK], BF16, "wt16_10", tag="a_sb103")
        cast_wt(0, 1)
        cast_wt(1, 0)
        h_q[0, 1] = placed([P, HALF], U32, "h_q01", 0)
        wt_s = placed([P, 2 * N], U8, "wt_s", 4096)
        h_q[1, 0] = placed([P, HALF], U32, "h_q10", 2048)
        quantize_wt(0, 0)
        quantize_wt(0, 1)
        quantize_h(0, 1)
        quantize_h(1, 0)
        quantize_h(1, 1)
        quantize_wt(1, 0)

        y_sb = [held([P, N // P, HALF], F32, "y%d" % hf, tag="wa_raw0%d" % hf) for hf in range(2)]
        diff = [held([P, N // P, HALF], F32, "diff%d" % hf, tag="mod%d0" % hf) for hf in range(2)]
        tiles = [(hf, nb) for nh in range(2) for hf in range(2) for nb in (2 * nh, 2 * nh + 1)]
        tiles[5], tiles[6] = tiles[6], tiles[5]
        for hf, nb in tiles[:2]:
            predict(hf, nb)
        wt16[1, 1] = held([P, NH * PACK], BF16, "wt16_11", tag="h16_11")
        cast_wt(1, 1)
        for hf, nb in tiles[2:4]:
            predict(hf, nb)
        for hf, nb in tiles[:2]:
            finish(hf, nb)
        quantize_wt(1, 1)
        for hf, nb in tiles[4:]:
            predict(hf, nb)
        for hf, nb in tiles[2:-1]:
            finish(hf, nb)
        finish(*tiles[-1], LAST_PIECES)
